import numpy as np
import ml_dtypes


def mxq(x, axis, fmt="e4m3"):
    dtype, down = {"e4m3": (ml_dtypes.float8_e4m3fn, 7), "e5m2": (ml_dtypes.float8_e5m2, 14)}[fmt]
    v = np.moveaxis(np.asarray(x, np.float32).astype(ml_dtypes.bfloat16).astype(np.float64), axis, -1)
    blocks = v.reshape(v.shape[:-1] + (-1, 32))
    amax = np.abs(blocks).max(-1, keepdims=True)
    byte = np.maximum(np.where(amax > 0, np.frexp(amax)[1] - 1 + 127, 0) - down, 1)
    scale = np.exp2(byte - 127.0)
    codes = (blocks / scale).astype(np.float32).astype(dtype).astype(np.float64)
    return np.moveaxis((codes * scale).reshape(v.shape), -1, axis)


WIDE = False


def mx_kscale(k):
    if not WIDE:
        return np.ones(k)
    levels = np.array([10, -10, 5, -5, 0])
    if k % 512:
        return np.exp2(np.random.permutation(np.resize(levels, k // 32))).repeat(32)
    a = np.empty((k // 512, 16))
    for p in range(k // 512):
        a[p, :8] = np.random.permutation(np.resize(levels, 8))
        for g in range(8):
            far = levels[np.abs(levels - a[p, g]) >= 10]
            a[p, g + 8] = far[np.random.randint(len(far))]
    return np.exp2(a.ravel()).repeat(32)


def f64(x):
    return np.asarray(x).astype(np.float64)


def striped(idx):
    return np.tile(idx.reshape(-1, 16).T, (8, 1)).astype(np.uint16)


def unstriped(offs):
    return offs[:16].T.reshape(-1).astype(np.int64)


def pack_weight(w):
    k, n = w.shape
    w = f64(np.asarray(w, np.float32).astype(ml_dtypes.bfloat16)).reshape(k // 32, 32, n)
    amax = np.abs(w).max(1)
    byte = np.clip(np.where(amax > 0, np.frexp(amax)[1] - 1 + 127 - 7, 1), 1, 254)
    scaled = (w * np.exp2(127.0 - byte)[:, None, :]).reshape(k, n).astype(np.float32)
    words = np.ascontiguousarray(scaled.reshape(k // 512, 128, 4, n).transpose(0, 1, 3, 2)).astype(ml_dtypes.float8_e4m3fn).view(np.uint8)
    return words, np.ascontiguousarray(byte.astype(np.uint8).reshape(k // 512, 16, n))


def unpack_weight(words, scales):
    g, p, n, _ = words.shape
    vals = np.ascontiguousarray(words).view(ml_dtypes.float8_e4m3fn).astype(np.float64) * np.repeat(np.exp2(scales.astype(np.float64) - 127.0), 8, axis=1)[..., None]
    return vals.transpose(0, 1, 3, 2).reshape(g * 512, n)


def planes(y):
    n, m = y.shape
    v = y.astype(np.float32).astype(ml_dtypes.bfloat16).astype(np.float64).reshape(n // 32, 32, m)
    top = np.abs(v).max(1)
    byte = np.clip(np.where(top > 0, np.frexp(top)[1] - 1 + 127 - 7, 1), 1, 254)
    codes = (v * np.exp2(127.0 - byte)[:, None, :]).reshape(n, m).astype(np.float32).astype(ml_dtypes.float8_e4m3fn).view(np.uint8)
    words = codes.reshape(n // 512, 128, 4, m).transpose(0, 1, 3, 2)
    return np.ascontiguousarray(words), np.ascontiguousarray(byte.astype(np.uint8).reshape(n // 512, 16, m))


def relu(v):
    return np.maximum(v, 0.0)


K, T, S, H, N, V = 1024, 1024, 512, 512, 512, 256


def setup_inputs():
    n = np.random.standard_normal
    s = mx_kscale(K)[:, None]
    u = mx_kscale(H)
    packed_xT = pack_weight(n((K, T)) * s)
    return {
        "x_words": packed_xT[0],
        "x_scales": packed_xT[1],
        "w1": (n((K, H)) / np.sqrt(K) / s * u).astype(np.float32),
        "w2": (n((H, N)) / np.sqrt(5 * H) / u[:, None]).astype(np.float32),
        "w3": (n((H, N)) / np.sqrt(5 * H) / u[:, None]).astype(np.float32),
        "w4": (n((H, N)) / np.sqrt(5 * H) / u[:, None]).astype(np.float32),
        "w5": (n((H, N)) / np.sqrt(5 * H) / u[:, None]).astype(np.float32),
        "w6": (n((H, N)) / np.sqrt(5 * H) / u[:, None]).astype(np.float32),
        "offs": striped(np.random.permutation(T)[:S]),
        "own": striped(np.random.permutation(S)[:V]),
        "ea": striped(np.random.permutation(S)[:V]),
        "eb": striped(np.random.permutation(S)[:V]),
        "ec": striped(np.random.permutation(S)[:V]),
        "ed": striped(np.random.permutation(S)[:V]),
    }


def reference(x_words, x_scales, w1, w2, w3, w4, w5, w6, offs, own, ea, eb, ec, ed):
    xq = unpack_weight(x_words, x_scales)[:, unstriped(offs)]
    h = relu(mxq(f64(w1), 0, "e4m3").T @ xq)
    hown = h[:, unstriped(own)]
    hea = h[:, unstriped(ea)]
    hec = h[:, unstriped(ec)]
    s1 = hea + hec
    d1 = np.abs(hea - hec)
    heb = h[:, unstriped(eb)]
    hed = h[:, unstriped(ed)]
    s2 = heb + hed
    d2 = np.abs(heb - hed)
    out_0 = mxq(f64(w2), 0, "e4m3").T @ mxq(hown, 0, "e4m3") + mxq(f64(w3), 0, "e4m3").T @ mxq(s1, 0, "e4m3") + mxq(f64(w4), 0, "e4m3").T @ mxq(d1, 0, "e4m3") + mxq(f64(w5), 0, "e4m3").T @ mxq(s2, 0, "e4m3") + mxq(f64(w6), 0, "e4m3").T @ mxq(d2, 0, "e4m3")
    return (out_0,) + planes(out_0)

@@ -1,0 +1,203 @@
+from contextlib import ExitStack
+
+import concourse.mybir as mybir
+
+K, T, S, H, N, V = 1024, 1024, 512, 512, 512, 256
+FLOPS = 2 * K * H * S + 5 * 2 * H * N * V
+
+F32 = mybir.dt.float32
+BF16 = mybir.dt.bfloat16
+I32 = mybir.dt.int32
+U32 = mybir.dt.uint32
+U16 = mybir.dt.uint16
+U8 = mybir.dt.uint8
+FP8X4 = mybir.dt.float8_e4m3fn_x4
+ACT = mybir.ActivationFunctionType
+ALU = mybir.AluOpType
+
+P = 128
+PACK = 4
+HALF = V // 2
+W1_SCALAR_M = (44, 44)
+
+
+def tile_picked_ymeshcnn_relu_po_kernel(tc, x_words, x_scales, w1, w2, w3, w4, w5, w6, offs, own, ea, eb, ec, ed, out_0, out_1, out_2):
+    nc = tc.nc
+    with ExitStack() as ctx:
+        keep = ctx.enter_context(tc.tile_pool(name="keep", bufs=1))
+        psum = ctx.enter_context(tc.psum_pool(name="psum", bufs=1))
+
+        def load_list(ap, name):
+            tile = keep.tile(list(ap.shape), U16, name=name)
+            nc.sync.dma_start(tile[:], ap)
+            return tile
+
+        def load_weight(rows, name):
+            raw = keep.tile([P, PACK, 512], F32, name=name + "_raw")
+            nc.sync.dma_start(out=raw[:], in_=rows.rearrange("(p j) c -> p j c", j=PACK))
+            return raw
+
+        def deal(copy, grouped, raw, m0, m1):
+            copy(out=grouped[:].rearrange("p t m j -> p m j t")[:, m0:m1], in_=raw[:].rearrange("p j (m t) -> p m j t", t=PACK)[:, m0:m1])
+
+        def mx_tiles(width, name):
+            return (keep.tile([P, width], U32, name=name + "_codes", tag=name + "_codes", align_bytes=64), keep.tile([P, width], U8, name=name + "_scales", tag=name + "_scales", align_bytes=64))
+
+        def quantize(mx, cols, flat):
+            nc.vector.quantize_mx(out=mx[0][:, cols].bitcast(FP8X4), scales=mx[1][:, cols], in_=flat)
+
+        def woven(tile):
+            return tile[:].rearrange("p (c i) t -> p c t i", i=4)
+
+        def planar(tile):
+            return tile[:].rearrange("p t (c i) -> p c t i", i=4)
+
+        xs = keep.tile([P, T], U8, name="xs", align_bytes=64)
+        nc.vector.memset(xs[:].bitcast(I32), 0)
+
+        def load_words(o):
+            tile = keep.tile([P, T], I32, name="xw%d" % o, align_bytes=64)
+            nc.sync.dma_start(out=tile[:], in_=x_words[o].rearrange("p n t -> p (n t)").bitcast(I32))
+            return tile
+
+        xw = [load_words(0)]
+        lists = {name: load_list(ap, name + "_t") for name, ap in (("offs", offs), ("ea", ea), ("ec", ec), ("eb", eb), ("ed", ed))}
+        w1_raw = [load_weight(w1[0:512, :], "w1_0")]
+        lists["own"] = load_list(own, "own_t")
+        for q in range(4):
+            nc.sync.dma_start(out=xs[32 * q : 32 * q + 8, :].bitcast(I32), in_=x_scales[:, 4 * q : 4 * q + 4, :].bitcast(I32))
+        xw.append(load_words(1))
+        w1_raw.append(load_weight(w1[512:1024, :], "w1_1"))
+        offs_t = lists["offs"]
+        names = ("s1", "d1", "s2", "d2", "own")
+        w_raw = {name: load_weight(ap, "w_" + name) for name, ap in zip(names, (w3, w4, w5, w6, w2))}
+
+        banks = [psum.tile([P, S], F32, name="hbank%d" % t, tag="bank%d" % t) for t in range(PACK)]
+        h = []
+        xsg = keep.tile([P, S], U8, name="xsg", align_bytes=64)
+        for o in range(2):
+            xg = keep.tile([P, S], U32, name="xg%d" % o, align_bytes=64)
+            nc.vector.tensor_copy(xg[:], xw[o][:].bitcast(U32).indirect(offs_t[:]))
+            grouped = keep.tile([P, PACK, P, PACK], BF16, name="w1g", tag="w1g", align_bytes=64)
+            deal(nc.scalar.copy, grouped, w1_raw[o], 0, W1_SCALAR_M[o])
+            deal(nc.vector.tensor_copy, grouped, w1_raw[o], W1_SCALAR_M[o], P)
+            if o == 0:
+                nc.vector.tensor_copy(xsg[:], xs[:].indirect(offs_t[:]))
+            mx = mx_tiles(H, "w1_%d" % o)
+            for t in range(PACK):
+                cols = slice(P * t, P * (t + 1))
+                quantize(mx, cols, grouped[:, t].rearrange("p m j -> p (m j)"))
+                nc.tensor.matmul_mx(out=banks[t][:], lhsT=mx[0][:, cols].bitcast(FP8X4), lhsT_scale=mx[1][:, cols],
+                                    rhs=xg[:].bitcast(FP8X4), rhs_scale=xsg[4 * o : P, :], start=(o == 0), stop=(o == 1))
+        for t in range(PACK):
+            tile = keep.tile([P, S], F32, name="h%d" % t)
+            nc.scalar.activation(tile[:], banks[t][:], ACT.Relu)
+            h.append(tile)
+
+        w_bf = {}
+        w_mx = {}
+        a_mx = {}
+
+        def cast_weight(name, tag):
+            w_bf[name] = keep.tile([P, PACK, P, PACK], BF16, name="wg_" + name, tag=tag, align_bytes=64)
+            deal(nc.scalar.copy, w_bf[name], w_raw[name], 0, P)
+
+        def quantize_weight(name):
+            w_mx[name] = mx_tiles(N, "w_" + name)
+            quantize(w_mx[name], slice(0, N), w_bf[name][:].rearrange("p t m j -> p (t m j)"))
+
+        def gather(list_names, cols, tags):
+            width = 16 * (cols.stop - cols.start)
+            tiles = [keep.tile([P, PACK, width], F32, name=tag, tag=tag, align_bytes=64) for tag in tags]
+            for t in range(PACK):
+                for name, tile in zip(list_names, tiles):
+                    nc.vector.tensor_copy(tile[:, t, :], h[t][:].indirect(lists[name][:, cols]))
+            return tiles
+
+        def bf_tile(width, name):
+            return keep.tile([P, width, PACK], BF16, name="bf_" + name, tag="bf_" + name, align_bytes=64)
+
+        def quantize_act(name, cols, tile):
+            if name not in a_mx:
+                a_mx[name] = mx_tiles(V, "a_" + name)
+            quantize(a_mx[name], cols, tile[:].rearrange("p v t -> p (v t)"))
+
+        def difference(eng, a, c, name):
+            diff = keep.tile([P, PACK, V], F32, name="diff_" + name, tag="diff_" + name, align_bytes=64)
+            eng.tensor_tensor(diff[:], a[:], c[:], ALU.subtract)
+            return diff
+
+        def total(eng, a, c, name):
+            s_bf = bf_tile(V, name)
+            eng.tensor_tensor(woven(s_bf), planar(a), planar(c), ALU.add)
+            return s_bf
+
+        def magnitude(diff, name):
+            d_bf = bf_tile(V, name)
+            nc.scalar.activation(woven(d_bf), planar(diff), ACT.Abs)
+            return d_bf
+
+        y_mx = mx_tiles(V, "y")
+        ybanks = {}
+        halves = [slice(HALF * half, HALF * (half + 1)) for half in range(2)]
+        whole = slice(0, V)
+
+        def product(name, half):
+            for t in range(PACK):
+                if name == names[0]:
+                    ybanks[half, t] = psum.tile([P, HALF], F32, name="ybank%d%d" % (half, t), tag="bank%d" % (t + 4 * (1 - half)))
+                cols = slice(P * t, P * (t + 1))
+                nc.tensor.matmul_mx(out=ybanks[half, t][:], lhsT=w_mx[name][0][:, cols].bitcast(FP8X4), lhsT_scale=w_mx[name][1][:, cols],
+                                    rhs=a_mx[name][0][:, halves[half]].bitcast(FP8X4), rhs_scale=a_mx[name][1][:, halves[half]],
+                                    start=(name == names[0]), stop=(name == names[-1]))
+
+        def both(name, tile):
+            quantize_weight(name)
+            quantize_act(name, whole, tile)
+            product(name, 0)
+            product(name, 1)
+
+        def finish(half, copies, cast):
+            y = keep.tile([P, PACK, HALF], F32, name="y%d" % half)
+            for t in range(PACK):
+                copies[t](out=y[:, t, :], in_=ybanks[half, t][:])
+            nc.sync.dma_start(out=out_0.rearrange("(p t) v -> p t v", t=PACK)[:, :, halves[half]], in_=y[:])
+            y_bf = bf_tile(HALF, "y%d" % half)
+            cast(out=woven(y_bf), in_=planar(y))
+            quantize(y_mx, halves[half], y_bf[:].rearrange("p v t -> p (v t)"))
+
+        a1, c1 = gather(("ea", "ec"), slice(0, 16), ("g_ea", "g_ec"))
+        diff1 = difference(nc.vector, a1, c1, "d1")
+        s1 = total(nc.vector, a1, c1, "s1")
+        cast_weight("s1", "w1_1_codes")
+        cast_weight("d1", "w1_1_scales")
+        d1 = magnitude(diff1, "d1")
+        both("s1", s1)
+        both("d1", d1)
+        a2, c2 = gather(("eb", "ed"), slice(0, 16), ("w1_1_codes", "w1_1_scales"))
+        diff2 = difference(nc.vector, a2, c2, "d2")
+        s2 = total(nc.vector, a2, c2, "s2")
+        cast_weight("s2", "g_ea")
+        cast_weight("d2", "g_ec")
+        d2 = magnitude(diff2, "d2")
+        cast_weight("own", "diff_d1")
+        both("s2", s2)
+        both("d2", d2)
+        (own0,) = gather(("own",), slice(0, 8), ("bf_d2",))
+        own0_bf = bf_tile(HALF, "own0")
+        nc.scalar.copy(out=woven(own0_bf), in_=planar(own0))
+        quantize_weight("own")
+        quantize_act("own", halves[0], own0_bf)
+        product("own", 0)
+        (own1,) = gather(("own",), slice(8, 16), ("bf_own0",))
+        own1_bf = bf_tile(HALF, "own1")
+        nc.vector.tensor_copy(out=woven(own1_bf), in_=planar(own1))
+        quantize_act("own", halves[1], own1_bf)
+        product("own", 1)
+        finish(0, [nc.scalar.copy] * 4, nc.scalar.copy)
+        finish(1, [nc.scalar.copy, nc.vector.tensor_copy] * 2, nc.vector.tensor_copy)
+
+        nc.sync.dma_start(out=out_1[0].rearrange("p v t -> p (v t)").bitcast(I32), in_=y_mx[0][:].bitcast(I32))
+        for q in range(4):
+            eng = nc.scalar if q % 2 else nc.sync
+            eng.dma_start(out=out_2[0, 4 * q : 4 * q + 4, :].bitcast(I32), in_=y_mx[1][32 * q : 32 * q + 4, :].bitcast(I32))

@@ -17,8 +17,13 @@ ALU = mybir.AluOpType
 
 P = 128
 PACK = 4
-HALF = V // 2
-W1_SCALAR_M = (44, 44)
+K_PASS = P * PACK
+QUADRANT = 32
+BANKS = 8
+RUN = 4
+
+W1_SCALAR_COLUMNS = (88, 56)
+WEAVE_SCALAR_RUNS = 22
 
 
 def tile_picked_ymeshcnn_relu_po_kernel(tc, x_words, x_scales, w1, w2, w3, w4, w5, w6, offs, own, ea, eb, ec, ed, out_0, out_1, out_2):
@@ -27,177 +32,199 @@ def tile_picked_ymeshcnn_relu_po_kernel(tc, x_words, x_scales, w1, w2, w3, w4, w
         keep = ctx.enter_context(tc.tile_pool(name="keep", bufs=1))
         psum = ctx.enter_context(tc.psum_pool(name="psum", bufs=1))
 
+        def sbuf(shape, dtype, name, tag=None):
+            return keep.tile(shape, dtype, name=name, tag=tag or name, align_bytes=64)
+
         def load_list(ap, name):
             tile = keep.tile(list(ap.shape), U16, name=name)
             nc.sync.dma_start(tile[:], ap)
             return tile
 
-        def load_weight(rows, name):
-            raw = keep.tile([P, PACK, 512], F32, name=name + "_raw")
-            nc.sync.dma_start(out=raw[:], in_=rows.rearrange("(p j) c -> p j c", j=PACK))
-            return raw
-
-        def deal(copy, grouped, raw, m0, m1):
-            copy(out=grouped[:].rearrange("p t m j -> p m j t")[:, m0:m1], in_=raw[:].rearrange("p j (m t) -> p m j t", t=PACK)[:, m0:m1])
-
-        def mx_tiles(width, name):
-            return (keep.tile([P, width], U32, name=name + "_codes", tag=name + "_codes", align_bytes=64), keep.tile([P, width], U8, name=name + "_scales", tag=name + "_scales", align_bytes=64))
-
-        def quantize(mx, cols, flat):
-            nc.vector.quantize_mx(out=mx[0][:, cols].bitcast(FP8X4), scales=mx[1][:, cols], in_=flat)
-
-        def woven(tile):
-            return tile[:].rearrange("p (c i) t -> p c t i", i=4)
-
-        def planar(tile):
-            return tile[:].rearrange("p t (c i) -> p c t i", i=4)
-
-        xs = keep.tile([P, T], U8, name="xs", align_bytes=64)
-        nc.vector.memset(xs[:].bitcast(I32), 0)
-
         def load_words(o):
-            tile = keep.tile([P, T], I32, name="xw%d" % o, align_bytes=64)
+            tile = sbuf([P, T], I32, "x_words%d" % o)
             nc.sync.dma_start(out=tile[:], in_=x_words[o].rearrange("p n t -> p (n t)").bitcast(I32))
             return tile
 
-        xw = [load_words(0)]
-        lists = {name: load_list(ap, name + "_t") for name, ap in (("offs", offs), ("ea", ea), ("ec", ec), ("eb", eb), ("ed", ed))}
-        w1_raw = [load_weight(w1[0:512, :], "w1_0")]
-        lists["own"] = load_list(own, "own_t")
-        for q in range(4):
-            nc.sync.dma_start(out=xs[32 * q : 32 * q + 8, :].bitcast(I32), in_=x_scales[:, 4 * q : 4 * q + 4, :].bitcast(I32))
-        xw.append(load_words(1))
-        w1_raw.append(load_weight(w1[512:1024, :], "w1_1"))
-        offs_t = lists["offs"]
-        names = ("s1", "d1", "s2", "d2", "own")
-        w_raw = {name: load_weight(ap, "w_" + name) for name, ap in zip(names, (w3, w4, w5, w6, w2))}
+        def load_weight(rows, name):
+            raw = sbuf([P, PACK, rows.shape[1]], F32, name + "_raw")
+            nc.sync.dma_start(out=raw[:], in_=rows.rearrange("(p j) c -> p j c", j=PACK))
+            return raw
 
-        banks = [psum.tile([P, S], F32, name="hbank%d" % t, tag="bank%d" % t) for t in range(PACK)]
-        h = []
-        xsg = keep.tile([P, S], U8, name="xsg", align_bytes=64)
-        for o in range(2):
-            xg = keep.tile([P, S], U32, name="xg%d" % o, align_bytes=64)
-            nc.vector.tensor_copy(xg[:], xw[o][:].bitcast(U32).indirect(offs_t[:]))
-            grouped = keep.tile([P, PACK, P, PACK], BF16, name="w1g", tag="w1g", align_bytes=64)
-            deal(nc.scalar.copy, grouped, w1_raw[o], 0, W1_SCALAR_M[o])
-            deal(nc.vector.tensor_copy, grouped, w1_raw[o], W1_SCALAR_M[o], P)
+        def deal(copy, dealt, raw, m0, m1):
+            copy(
+                out=dealt[:].rearrange("p t (m e) j -> p m j e t", e=2)[:, m0 // 2 : m1 // 2],
+                in_=raw[:].rearrange("p j (m e t) -> p m j e t", e=2, t=PACK)[:, m0 // 2 : m1 // 2],
+            )
+
+        def mx_tiles(width, name):
+            return sbuf([P, width], U32, name + "_codes"), sbuf([P, width], U8, name + "_scales")
+
+        def quantize(mx, cols, values):
+            nc.vector.quantize_mx(out=mx[0][:, cols].bitcast(FP8X4), scales=mx[1][:, cols], in_=values)
+
+        def plane_cols(t):
+            return slice(P * t, P * (t + 1))
+
+        def quantize_plane(mx, dealt, t):
+            quantize(mx, plane_cols(t), dealt[:, t].rearrange("p m j -> p (m j)"))
+
+        def as_woven(tile):
+            return tile[:].rearrange("p (c i) t -> p c t i", i=RUN)
+
+        def as_planes(tile):
+            return tile[:].rearrange("p t (c i) -> p c t i", i=RUN)
+
+        def flat(tile):
+            return tile[:].rearrange("p a b -> p (a b)")
+
+        scales_in = sbuf([P, T], U8, "scales_in", "picked_words1")
+        nc.vector.memset(scales_in[:].bitcast(I32), 0)
+        words_in = [load_words(0)]
+        lists = {name: load_list(ap, name) for name, ap in (("offs", offs), ("ea", ea), ("ec", ec), ("eb", eb), ("ed", ed))}
+        w1_raw = [load_weight(w1[0:K_PASS, :], "w1_0")]
+        lists["own"] = load_list(own, "own")
+        for q in range(P // QUADRANT):
+            nc.sync.dma_start(
+                out=scales_in[QUADRANT * q : QUADRANT * q + 2 * PACK, :].bitcast(I32),
+                in_=x_scales[:, PACK * q : PACK * (q + 1), :].bitcast(I32),
+            )
+        words_in.append(load_words(1))
+        w1_raw.append(load_weight(w1[K_PASS:K, :], "w1_1"))
+        operands = ("d1", "s1", "s2", "d2", "hown")
+        w_raw = {name: load_weight(ap, "w_" + name) for name, ap in zip(operands, (w4, w3, w5, w6, w2))}
+
+        pieces = [(0, slice(0, S // 2)), (0, slice(S // 2, S))] + [(t, slice(0, S)) for t in range(1, PACK)]
+        h_banks = [psum.tile([P, edges.stop - edges.start], F32, name="h_bank%d" % i, tag="bank%d" % i) for i, (t, edges) in enumerate(pieces)]
+        picked_scales = sbuf([P, S], U8, "picked_scales")
+        for o in range(K // K_PASS):
+            picked_words = sbuf([P, S], U32, "picked_words%d" % o)
+            nc.vector.tensor_copy(picked_words[:], words_in[o][:].bitcast(U32).indirect(lists["offs"][:]))
+            dealt = sbuf([P, PACK, P, PACK], BF16, "w1_dealt")
+            deal(nc.scalar.copy, dealt, w1_raw[o], 0, W1_SCALAR_COLUMNS[o])
+            deal(nc.vector.tensor_copy, dealt, w1_raw[o], W1_SCALAR_COLUMNS[o], P)
             if o == 0:
-                nc.vector.tensor_copy(xsg[:], xs[:].indirect(offs_t[:]))
-            mx = mx_tiles(H, "w1_%d" % o)
+                nc.vector.tensor_copy(picked_scales[:], scales_in[:].indirect(lists["offs"][:]))
+            w1_mx = mx_tiles(H, "w1_%d" % o)
             for t in range(PACK):
-                cols = slice(P * t, P * (t + 1))
-                quantize(mx, cols, grouped[:, t].rearrange("p m j -> p (m j)"))
-                nc.tensor.matmul_mx(out=banks[t][:], lhsT=mx[0][:, cols].bitcast(FP8X4), lhsT_scale=mx[1][:, cols],
-                                    rhs=xg[:].bitcast(FP8X4), rhs_scale=xsg[4 * o : P, :], start=(o == 0), stop=(o == 1))
-        for t in range(PACK):
-            tile = keep.tile([P, S], F32, name="h%d" % t)
-            nc.scalar.activation(tile[:], banks[t][:], ACT.Relu)
-            h.append(tile)
+                quantize_plane(w1_mx, dealt, t)
+                for bank, (plane, edges) in zip(h_banks, pieces):
+                    if plane == t:
+                        nc.tensor.matmul_mx(
+                            out=bank[:],
+                            lhsT=w1_mx[0][:, plane_cols(t)].bitcast(FP8X4),
+                            lhsT_scale=w1_mx[1][:, plane_cols(t)],
+                            rhs=picked_words[:, edges].bitcast(FP8X4),
+                            rhs_scale=picked_scales[PACK * o : P, edges],
+                            start=(o == 0),
+                            stop=(o == K // K_PASS - 1),
+                        )
+        h = [keep.tile([P, S], F32, name="h%d" % t) for t in range(PACK)]
+        for bank, (t, edges) in zip(h_banks, pieces):
+            if edges.start > 0:
+                nc.vector.tensor_scalar_max(h[t][:, edges], bank[:], 0.0)
+            else:
+                nc.scalar.activation(h[t][:, edges], bank[:], ACT.Relu)
 
-        w_bf = {}
+        w_dealt = {}
         w_mx = {}
-        a_mx = {}
+        y_banks = {}
 
-        def cast_weight(name, tag):
-            w_bf[name] = keep.tile([P, PACK, P, PACK], BF16, name="wg_" + name, tag=tag, align_bytes=64)
-            deal(nc.scalar.copy, w_bf[name], w_raw[name], 0, P)
+        def round_weight(name, tag):
+            w_dealt[name] = sbuf([P, PACK, P, PACK], BF16, "w_dealt_" + name, tag)
+            deal(nc.scalar.copy, w_dealt[name], w_raw[name], 0, P)
 
-        def quantize_weight(name):
+        def pick(planes, list_name, t):
+            nc.vector.tensor_copy(planes[:, t, :], h[t][:].indirect(lists[list_name][:]))
+
+        def pick_minus(planes, list_name, first, t):
+            nc.vector.tensor_tensor(planes[:, t, :], h[t][:].indirect(lists[list_name][:]), first[:, t, :], ALU.subtract)
+
+        def pair_sum(first, difference, name):
+            planes = sbuf([P, PACK, V], F32, name)
+            nc.vector.scalar_tensor_tensor(flat(planes), flat(first), 2.0, flat(difference), ALU.mult, ALU.add)
+            return planes
+
+        def weave(planes, name, func):
+            woven = sbuf([P, V, PACK], BF16, "woven_" + name)
+            nc.scalar.activation(as_woven(woven), as_planes(planes), func)
+            return woven
+
+        def weave_on_both(planes, name):
+            woven = sbuf([P, V, PACK], BF16, "woven_" + name)
+            nc.scalar.copy(out=as_woven(woven)[:, 0:WEAVE_SCALAR_RUNS], in_=as_planes(planes)[:, 0:WEAVE_SCALAR_RUNS])
+            nc.vector.tensor_copy(out=as_woven(woven)[:, WEAVE_SCALAR_RUNS:], in_=as_planes(planes)[:, WEAVE_SCALAR_RUNS:])
+            return woven
+
+        def quantize_woven(woven, name):
+            mx = mx_tiles(V, name)
+            quantize(mx, slice(0, V), flat(woven))
+            return mx
+
+        def product(name, mx):
+            for t in range(PACK):
+                if name == operands[0]:
+                    y_banks[t] = psum.tile([P, V], F32, name="y_bank%d" % t, tag="bank%d" % ((len(pieces) + t) % BANKS))
+                nc.tensor.matmul_mx(
+                    out=y_banks[t][:],
+                    lhsT=w_mx[name][0][:, plane_cols(t)].bitcast(FP8X4),
+                    lhsT_scale=w_mx[name][1][:, plane_cols(t)],
+                    rhs=mx[0][:].bitcast(FP8X4),
+                    rhs_scale=mx[1][:],
+                    start=(name == operands[0]),
+                    stop=(name == operands[-1]),
+                )
+
+        def quantize_and_multiply(name, woven):
             w_mx[name] = mx_tiles(N, "w_" + name)
-            quantize(w_mx[name], slice(0, N), w_bf[name][:].rearrange("p t m j -> p (t m j)"))
+            quantize(w_mx[name], slice(0, N), w_dealt[name][:].rearrange("p t m j -> p (t m j)"))
+            product(name, quantize_woven(woven, name))
 
-        def gather(list_names, cols, tags):
-            width = 16 * (cols.stop - cols.start)
-            tiles = [keep.tile([P, PACK, width], F32, name=tag, tag=tag, align_bytes=64) for tag in tags]
-            for t in range(PACK):
-                for name, tile in zip(list_names, tiles):
-                    nc.vector.tensor_copy(tile[:, t, :], h[t][:].indirect(lists[name][:, cols]))
-            return tiles
+        hea = sbuf([P, PACK, V], F32, "hea")
+        heb = sbuf([P, PACK, V], F32, "heb")
+        diff1 = sbuf([P, PACK, V], F32, "diff1")
+        for t in range(PACK):
+            pick(hea, "ea", t)
+            pick(heb, "eb", t)
+            pick_minus(diff1, "ec", hea, t)
 
-        def bf_tile(width, name):
-            return keep.tile([P, width, PACK], BF16, name="bf_" + name, tag="bf_" + name, align_bytes=64)
+        round_weight("d1", "w1_1_codes")
+        round_weight("s1", "w1_1_scales")
+        round_weight("s2", "w_d1_raw")
+        sum1 = pair_sum(hea, diff1, "sum1")
+        quantize_and_multiply("d1", weave(diff1, "d1", ACT.Abs))
+        quantize_and_multiply("s1", weave(sum1, "s1", ACT.Copy))
 
-        def quantize_act(name, cols, tile):
-            if name not in a_mx:
-                a_mx[name] = mx_tiles(V, "a_" + name)
-            quantize(a_mx[name], cols, tile[:].rearrange("p v t -> p (v t)"))
+        diff2 = sbuf([P, PACK, V], F32, "diff2", "w1_1_scales")
+        for t in range(PACK):
+            pick_minus(diff2, "ed", heb, t)
+        sum2 = pair_sum(heb, diff2, "sum2")
+        round_weight("d2", "w_s1_raw")
+        quantize_and_multiply("s2", weave(sum2, "s2", ACT.Copy))
+        quantize_and_multiply("d2", weave(diff2, "d2", ACT.Abs))
+        round_weight("hown", "w_s2_raw")
 
-        def difference(eng, a, c, name):
-            diff = keep.tile([P, PACK, V], F32, name="diff_" + name, tag="diff_" + name, align_bytes=64)
-            eng.tensor_tensor(diff[:], a[:], c[:], ALU.subtract)
-            return diff
+        hown = sbuf([P, PACK, V], F32, "hown", "woven_s2")
+        for t in range(PACK):
+            pick(hown, "own", t)
+        hown_woven = weave_on_both(hown, "hown")
+        w_mx["hown"] = mx_tiles(N, "w_hown")
+        quantize_plane(w_mx["hown"], w_dealt["hown"], 0)
+        hown_mx = quantize_woven(hown_woven, "hown")
+        for t in range(1, PACK):
+            quantize_plane(w_mx["hown"], w_dealt["hown"], t)
+        product("hown", hown_mx)
 
-        def total(eng, a, c, name):
-            s_bf = bf_tile(V, name)
-            eng.tensor_tensor(woven(s_bf), planar(a), planar(c), ALU.add)
-            return s_bf
-
-        def magnitude(diff, name):
-            d_bf = bf_tile(V, name)
-            nc.scalar.activation(woven(d_bf), planar(diff), ACT.Abs)
-            return d_bf
-
-        y_mx = mx_tiles(V, "y")
-        ybanks = {}
-        halves = [slice(HALF * half, HALF * (half + 1)) for half in range(2)]
-        whole = slice(0, V)
-
-        def product(name, half):
-            for t in range(PACK):
-                if name == names[0]:
-                    ybanks[half, t] = psum.tile([P, HALF], F32, name="ybank%d%d" % (half, t), tag="bank%d" % (t + 4 * (1 - half)))
-                cols = slice(P * t, P * (t + 1))
-                nc.tensor.matmul_mx(out=ybanks[half, t][:], lhsT=w_mx[name][0][:, cols].bitcast(FP8X4), lhsT_scale=w_mx[name][1][:, cols],
-                                    rhs=a_mx[name][0][:, halves[half]].bitcast(FP8X4), rhs_scale=a_mx[name][1][:, halves[half]],
-                                    start=(name == names[0]), stop=(name == names[-1]))
-
-        def both(name, tile):
-            quantize_weight(name)
-            quantize_act(name, whole, tile)
-            product(name, 0)
-            product(name, 1)
-
-        def finish(half, copies, cast):
-            y = keep.tile([P, PACK, HALF], F32, name="y%d" % half)
-            for t in range(PACK):
-                copies[t](out=y[:, t, :], in_=ybanks[half, t][:])
-            nc.sync.dma_start(out=out_0.rearrange("(p t) v -> p t v", t=PACK)[:, :, halves[half]], in_=y[:])
-            y_bf = bf_tile(HALF, "y%d" % half)
-            cast(out=woven(y_bf), in_=planar(y))
-            quantize(y_mx, halves[half], y_bf[:].rearrange("p v t -> p (v t)"))
-
-        a1, c1 = gather(("ea", "ec"), slice(0, 16), ("g_ea", "g_ec"))
-        diff1 = difference(nc.vector, a1, c1, "d1")
-        s1 = total(nc.vector, a1, c1, "s1")
-        cast_weight("s1", "w1_1_codes")
-        cast_weight("d1", "w1_1_scales")
-        d1 = magnitude(diff1, "d1")
-        both("s1", s1)
-        both("d1", d1)
-        a2, c2 = gather(("eb", "ed"), slice(0, 16), ("w1_1_codes", "w1_1_scales"))
-        diff2 = difference(nc.vector, a2, c2, "d2")
-        s2 = total(nc.vector, a2, c2, "s2")
-        cast_weight("s2", "g_ea")
-        cast_weight("d2", "g_ec")
-        d2 = magnitude(diff2, "d2")
-        cast_weight("own", "diff_d1")
-        both("s2", s2)
-        both("d2", d2)
-        (own0,) = gather(("own",), slice(0, 8), ("bf_d2",))
-        own0_bf = bf_tile(HALF, "own0")
-        nc.scalar.copy(out=woven(own0_bf), in_=planar(own0))
-        quantize_weight("own")
-        quantize_act("own", halves[0], own0_bf)
-        product("own", 0)
-        (own1,) = gather(("own",), slice(8, 16), ("bf_own0",))
-        own1_bf = bf_tile(HALF, "own1")
-        nc.vector.tensor_copy(out=woven(own1_bf), in_=planar(own1))
-        quantize_act("own", halves[1], own1_bf)
-        product("own", 1)
-        finish(0, [nc.scalar.copy] * 4, nc.scalar.copy)
-        finish(1, [nc.scalar.copy, nc.vector.tensor_copy] * 2, nc.vector.tensor_copy)
-
-        nc.sync.dma_start(out=out_1[0].rearrange("p v t -> p (v t)").bitcast(I32), in_=y_mx[0][:].bitcast(I32))
-        for q in range(4):
-            eng = nc.scalar if q % 2 else nc.sync
-            eng.dma_start(out=out_2[0, 4 * q : 4 * q + 4, :].bitcast(I32), in_=y_mx[1][32 * q : 32 * q + 4, :].bitcast(I32))
+        y = sbuf([P, PACK, V], F32, "y")
+        out_planes = out_0.rearrange("(p t) v -> p t v", t=PACK)
+        for t in range(0, PACK, 2):
+            nc.scalar.copy(out=y[:, t, :], in_=y_banks[t][:])
+            nc.vector.tensor_copy(out=y[:, t + 1, :], in_=y_banks[t + 1][:])
+            nc.sync.dma_start(out=out_planes[:, t : t + 2, :], in_=y[:, t : t + 2, :])
+        y_codes, y_scales = quantize_woven(weave_on_both(y, "y"), "y")
+        nc.sync.dma_start(out=out_1[0].rearrange("p v t -> p (v t)").bitcast(I32), in_=y_codes[:].bitcast(I32))
+        for q in range(P // QUADRANT):
+            queue = nc.scalar if q % 2 else nc.sync
+            queue.dma_start(
+                out=out_2[0, PACK * q : PACK * (q + 1), :].bitcast(I32),
+                in_=y_scales[QUADRANT * q : QUADRANT * q + PACK, :].bitcast(I32),
+            )

@@ -22,7 +22,7 @@ QUADRANT = 32
 BANKS = 8
 RUN = 4
 
-W1_SCALAR_COLUMNS = (88, 56)
+W1_PIECES = ((0, 0, 64, 64), (0, 64, 128, 88), (1, 0, 96, 36), (1, 96, 128, 108))
 WEAVE_SCALAR_RUNS = 22
 
 
@@ -50,14 +50,24 @@ def tile_picked_ymeshcnn_relu_po_kernel(tc, x_words, x_scales, w1, w2, w3, w4, w
             nc.sync.dma_start(out=raw[:], in_=rows.rearrange("(p j) c -> p j c", j=PACK))
             return raw
 
+        def load_w1_piece(i):
+            o, m0, m1, split = W1_PIECES[i]
+            return load_weight(w1[K_PASS * o : K_PASS * (o + 1), PACK * m0 : PACK * m1], "w1_piece%d" % i)
+
+        def deal_piece(copy, dealt, raw, first, m0, m1):
+            copy(
+                out=dealt[:].rearrange("p t (m e) j -> p m j e t", e=2)[:, m0 // 2 : m1 // 2],
+                in_=raw[:].rearrange("p j (m e t) -> p m j e t", e=2, t=PACK)[:, (m0 - first) // 2 : (m1 - first) // 2],
+            )
+
         def deal(copy, dealt, raw, m0, m1):
             copy(
                 out=dealt[:].rearrange("p t (m e) j -> p m j e t", e=2)[:, m0 // 2 : m1 // 2],
                 in_=raw[:].rearrange("p j (m e t) -> p m j e t", e=2, t=PACK)[:, m0 // 2 : m1 // 2],
             )
 
-        def mx_tiles(width, name):
-            return sbuf([P, width], U32, name + "_codes"), sbuf([P, width], U8, name + "_scales")
+        def mx_tiles(width, name, tag=None):
+            return sbuf([P, width], U32, name + "_codes", tag), sbuf([P, width], U8, name + "_scales")
 
         def quantize(mx, cols, values):
             nc.vector.quantize_mx(out=mx[0][:, cols].bitcast(FP8X4), scales=mx[1][:, cols], in_=values)
@@ -68,8 +78,8 @@ def tile_picked_ymeshcnn_relu_po_kernel(tc, x_words, x_scales, w1, w2, w3, w4, w
         def quantize_plane(mx, dealt, t):
             quantize(mx, plane_cols(t), dealt[:, t].rearrange("p m j -> p (m j)"))
 
-        def as_woven(tile):
-            return tile[:].rearrange("p (c i) t -> p c t i", i=RUN)
+        def as_woven(ap):
+            return ap.rearrange("p (c i) t -> p c t i", i=RUN)
 
         def as_planes(tile):
             return tile[:].rearrange("p t (c i) -> p c t i", i=RUN)
@@ -77,33 +87,39 @@ def tile_picked_ymeshcnn_relu_po_kernel(tc, x_words, x_scales, w1, w2, w3, w4, w
         def flat(tile):
             return tile[:].rearrange("p a b -> p (a b)")
 
-        scales_in = sbuf([P, T], U8, "scales_in", "picked_words1")
+        scales_in = sbuf([P, T], U8, "scales_in")
         nc.vector.memset(scales_in[:].bitcast(I32), 0)
+        lists = {"offs": load_list(offs, "offs")}
         words_in = [load_words(0)]
-        lists = {name: load_list(ap, name) for name, ap in (("offs", offs), ("ea", ea), ("ec", ec), ("eb", eb), ("ed", ed))}
-        w1_raw = [load_weight(w1[0:K_PASS, :], "w1_0")]
-        lists["own"] = load_list(own, "own")
+        for name, ap in (("ea", ea), ("ec", ec), ("eb", eb)):
+            lists[name] = load_list(ap, name)
+        words_in.append(load_words(1))
+        lists["ed"] = load_list(ed, "ed")
+        w1_raw = [load_w1_piece(0)]
         for q in range(P // QUADRANT):
             nc.sync.dma_start(
                 out=scales_in[QUADRANT * q : QUADRANT * q + 2 * PACK, :].bitcast(I32),
                 in_=x_scales[:, PACK * q : PACK * (q + 1), :].bitcast(I32),
             )
-        words_in.append(load_words(1))
-        w1_raw.append(load_weight(w1[K_PASS:K, :], "w1_1"))
-        operands = ("d1", "s1", "s2", "d2", "hown")
-        w_raw = {name: load_weight(ap, "w_" + name) for name, ap in zip(operands, (w4, w3, w5, w6, w2))}
+        w1_raw.extend([load_w1_piece(i) for i in range(1, len(W1_PIECES))])
+        lists["own"] = load_list(own, "own")
+        operands = ("d1", "d2", "hown", "s1", "s2")
+        w_raw = {name: load_weight(ap, "w_" + name) for name, ap in zip(operands, (w4, w6, w2, w3, w5))}
 
         pieces = [(0, slice(0, S // 2)), (0, slice(S // 2, S))] + [(t, slice(0, S)) for t in range(1, PACK)]
         h_banks = [psum.tile([P, edges.stop - edges.start], F32, name="h_bank%d" % i, tag="bank%d" % i) for i, (t, edges) in enumerate(pieces)]
-        picked_scales = sbuf([P, S], U8, "picked_scales")
+        picked_words = [sbuf([P, S], U32, "picked_words%d" % o) for o in range(K // K_PASS)]
         for o in range(K // K_PASS):
-            picked_words = sbuf([P, S], U32, "picked_words%d" % o)
-            nc.vector.tensor_copy(picked_words[:], words_in[o][:].bitcast(U32).indirect(lists["offs"][:]))
+            nc.vector.tensor_copy(picked_words[o][:], words_in[o][:].bitcast(U32).indirect(lists["offs"][:]))
+        picked_scales = sbuf([P, S], U8, "picked_scales")
+        nc.vector.tensor_copy(picked_scales[:], scales_in[:].indirect(lists["offs"][:]))
+        for o in range(K // K_PASS):
             dealt = sbuf([P, PACK, P, PACK], BF16, "w1_dealt")
-            deal(nc.scalar.copy, dealt, w1_raw[o], 0, W1_SCALAR_COLUMNS[o])
-            deal(nc.vector.tensor_copy, dealt, w1_raw[o], W1_SCALAR_COLUMNS[o], P)
-            if o == 0:
-                nc.vector.tensor_copy(picked_scales[:], scales_in[:].indirect(lists["offs"][:]))
+            for raw, (piece_pass, m0, m1, split) in zip(w1_raw, W1_PIECES):
+                if piece_pass == o:
+                    deal_piece(nc.scalar.copy, dealt, raw, m0, m0, split)
+                    if split < m1:
+                        deal_piece(nc.vector.tensor_copy, dealt, raw, m0, split, m1)
             w1_mx = mx_tiles(H, "w1_%d" % o)
             for t in range(PACK):
                 quantize_plane(w1_mx, dealt, t)
@@ -113,7 +129,7 @@ def tile_picked_ymeshcnn_relu_po_kernel(tc, x_words, x_scales, w1, w2, w3, w4, w
                             out=bank[:],
                             lhsT=w1_mx[0][:, plane_cols(t)].bitcast(FP8X4),
                             lhsT_scale=w1_mx[1][:, plane_cols(t)],
-                            rhs=picked_words[:, edges].bitcast(FP8X4),
+                            rhs=picked_words[o][:, edges].bitcast(FP8X4),
                             rhs_scale=picked_scales[PACK * o : P, edges],
                             start=(o == 0),
                             stop=(o == K // K_PASS - 1),
@@ -144,15 +160,10 @@ def tile_picked_ymeshcnn_relu_po_kernel(tc, x_words, x_scales, w1, w2, w3, w4, w
             nc.vector.scalar_tensor_tensor(flat(planes), flat(first), 2.0, flat(difference), ALU.mult, ALU.add)
             return planes
 
-        def weave(planes, name, func):
-            woven = sbuf([P, V, PACK], BF16, "woven_" + name)
-            nc.scalar.activation(as_woven(woven), as_planes(planes), func)
-            return woven
-
         def weave_on_both(planes, name):
             woven = sbuf([P, V, PACK], BF16, "woven_" + name)
-            nc.scalar.copy(out=as_woven(woven)[:, 0:WEAVE_SCALAR_RUNS], in_=as_planes(planes)[:, 0:WEAVE_SCALAR_RUNS])
-            nc.vector.tensor_copy(out=as_woven(woven)[:, WEAVE_SCALAR_RUNS:], in_=as_planes(planes)[:, WEAVE_SCALAR_RUNS:])
+            nc.scalar.copy(out=as_woven(woven[:])[:, 0:WEAVE_SCALAR_RUNS], in_=as_planes(planes)[:, 0:WEAVE_SCALAR_RUNS])
+            nc.vector.tensor_copy(out=as_woven(woven[:])[:, WEAVE_SCALAR_RUNS:], in_=as_planes(planes)[:, WEAVE_SCALAR_RUNS:])
             return woven
 
         def quantize_woven(woven, name):
@@ -174,45 +185,37 @@ def tile_picked_ymeshcnn_relu_po_kernel(tc, x_words, x_scales, w1, w2, w3, w4, w
                     stop=(name == operands[-1]),
                 )
 
-        def quantize_and_multiply(name, woven):
-            w_mx[name] = mx_tiles(N, "w_" + name)
+        def quantize_weight(name, tag):
+            w_mx[name] = mx_tiles(N, "w_" + name, tag)
             quantize(w_mx[name], slice(0, N), w_dealt[name][:].rearrange("p t m j -> p (t m j)"))
-            product(name, quantize_woven(woven, name))
 
-        hea = sbuf([P, PACK, V], F32, "hea")
-        heb = sbuf([P, PACK, V], F32, "heb")
-        diff1 = sbuf([P, PACK, V], F32, "diff1")
+        planes = {name: sbuf([P, PACK, V], F32, name) for name in ("hea", "heb", "d1", "d2", "hown")}
         for t in range(PACK):
-            pick(hea, "ea", t)
-            pick(heb, "eb", t)
-            pick_minus(diff1, "ec", hea, t)
+            pick(planes["hea"], "ea", t)
+            pick(planes["heb"], "eb", t)
+            pick_minus(planes["d1"], "ec", planes["hea"], t)
+            pick_minus(planes["d2"], "ed", planes["heb"], t)
+            pick(planes["hown"], "own", t)
+        planes["s1"] = pair_sum(planes["hea"], planes["d1"], "s1")
+        planes["s2"] = pair_sum(planes["heb"], planes["d2"], "s2")
 
-        round_weight("d1", "w1_1_codes")
-        round_weight("s1", "w1_1_scales")
-        round_weight("s2", "w_d1_raw")
-        sum1 = pair_sum(hea, diff1, "sum1")
-        quantize_and_multiply("d1", weave(diff1, "d1", ACT.Abs))
-        quantize_and_multiply("s1", weave(sum1, "s1", ACT.Copy))
+        for i, name in enumerate(operands):
+            round_weight(name, ("w1_1_codes", "w1_1_scales")[i] if i < 2 else "w_%s_raw" % operands[i - 2])
+        woven = sbuf([P, len(operands), V, PACK], BF16, "woven", "w_%s_raw" % operands[-1])
+        for i, name in enumerate(operands):
+            nc.scalar.activation(as_woven(woven[:, i]), as_planes(planes[name]), ACT.Abs if name in ("d1", "d2") else ACT.Copy)
 
-        diff2 = sbuf([P, PACK, V], F32, "diff2", "w1_1_scales")
-        for t in range(PACK):
-            pick_minus(diff2, "ed", heb, t)
-        sum2 = pair_sum(heb, diff2, "sum2")
-        round_weight("d2", "w_s1_raw")
-        quantize_and_multiply("s2", weave(sum2, "s2", ACT.Copy))
-        quantize_and_multiply("d2", weave(diff2, "d2", ACT.Abs))
-        round_weight("hown", "w_s2_raw")
-
-        hown = sbuf([P, PACK, V], F32, "hown", "woven_s2")
-        for t in range(PACK):
-            pick(hown, "own", t)
-        hown_woven = weave_on_both(hown, "hown")
-        w_mx["hown"] = mx_tiles(N, "w_hown")
-        quantize_plane(w_mx["hown"], w_dealt["hown"], 0)
-        hown_mx = quantize_woven(hown_woven, "hown")
-        for t in range(1, PACK):
-            quantize_plane(w_mx["hown"], w_dealt["hown"], t)
-        product("hown", hown_mx)
+        quantize_weight(operands[0], None)
+        for i, name in enumerate(operands):
+            mx = mx_tiles(V, name)
+            quantize(mx, slice(0, V), woven[:, i].rearrange("p v t -> p (v t)"))
+            if name == operands[-1]:
+                w_mx[name] = mx_tiles(N, "w_" + name, operands[i - 1])
+                for t in range(PACK):
+                    quantize_plane(w_mx[name], w_dealt[name], t)
+            product(name, mx)
+            if i + 2 < len(operands):
+                quantize_weight(operands[i + 1], name)
 
         y = sbuf([P, PACK, V], F32, "y")
         out_planes = out_0.rearrange("(p t) v -> p t v", t=PACK)

@@ -1,6 +1,7 @@
 from contextlib import ExitStack
 
 import concourse.mybir as mybir
+from concourse.masks import make_identity
 
 K, T, S, H, N, V = 1024, 1024, 512, 512, 512, 256
 FLOPS = 2 * K * H * S + 5 * 2 * H * N * V
@@ -30,10 +31,17 @@ def tile_picked_ymeshcnn_relu_po_kernel(tc, x_words, x_scales, w1, w2, w3, w4, w
     nc = tc.nc
     with ExitStack() as ctx:
         keep = ctx.enter_context(tc.tile_pool(name="keep", bufs=1))
+        late = ctx.enter_context(tc.tile_pool(name="late", bufs=1))
         psum = ctx.enter_context(tc.psum_pool(name="psum", bufs=1))
 
         def sbuf(shape, dtype, name, tag=None):
             return keep.tile(shape, dtype, name=name, tag=tag or name, align_bytes=64)
+
+        raw_bytes = 4 * PACK * N
+        regions = {"w_" + name: raw_bytes * i for i, name in enumerate(("d1", "hown", "d2"))}
+
+        def late_tile(shape, dtype, name, region, offset):
+            return late.tile(shape, dtype, name=name, align_bytes=64, offset=regions["w_" + region] + offset)
 
         def load_list(ap, name):
             tile = keep.tile(list(ap.shape), U16, name=name)
@@ -46,7 +54,10 @@ def tile_picked_ymeshcnn_relu_po_kernel(tc, x_words, x_scales, w1, w2, w3, w4, w
             return tile
 
         def load_weight(rows, name):
-            raw = sbuf([P, PACK, rows.shape[1]], F32, name + "_raw")
+            if name in regions:
+                raw = late.tile([P, PACK, rows.shape[1]], F32, name=name + "_raw", align_bytes=64, offset=regions[name])
+            else:
+                raw = sbuf([P, PACK, rows.shape[1]], F32, name + "_raw")
             nc.sync.dma_start(out=raw[:], in_=rows.rearrange("(p j) c -> p j c", j=PACK))
             return raw
 
@@ -103,8 +114,9 @@ def tile_picked_ymeshcnn_relu_po_kernel(tc, x_words, x_scales, w1, w2, w3, w4, w
             )
         w1_raw.extend([load_w1_piece(i) for i in range(1, len(W1_PIECES))])
         lists["own"] = load_list(own, "own")
-        operands = ("d1", "d2", "hown", "s1", "s2")
-        w_raw = {name: load_weight(ap, "w_" + name) for name, ap in zip(operands, (w4, w6, w2, w3, w5))}
+        operands = ("d1", "s1", "d2", "hown", "s2")
+        loaded = ("d1", "s1", "d2", "hown", "s2")
+        w_raw = {name: load_weight(ap, "w_" + name) for name, ap in zip(loaded, (w4, w3, w6, w2, w5))}
 
         pieces = [(0, slice(0, S // 2)), (0, slice(S // 2, S))] + [(t, slice(0, S)) for t in range(1, PACK)]
         h_banks = [psum.tile([P, edges.stop - edges.start], F32, name="h_bank%d" % i, tag="bank%d" % i) for i, (t, edges) in enumerate(pieces)]
@@ -144,21 +156,14 @@ def tile_picked_ymeshcnn_relu_po_kernel(tc, x_words, x_scales, w1, w2, w3, w4, w
         w_dealt = {}
         w_mx = {}
         y_banks = {}
-
-        def round_weight(name, tag):
-            w_dealt[name] = sbuf([P, PACK, P, PACK], BF16, "w_dealt_" + name, tag)
-            deal(nc.scalar.copy, w_dealt[name], w_raw[name], 0, P)
+        identity = sbuf([P, P], F32, "identity")
+        make_identity(nc, identity[:])
 
         def pick(planes, list_name, t):
             nc.vector.tensor_copy(planes[:, t, :], h[t][:].indirect(lists[list_name][:]))
 
         def pick_minus(planes, list_name, first, t):
             nc.vector.tensor_tensor(planes[:, t, :], h[t][:].indirect(lists[list_name][:]), first[:, t, :], ALU.subtract)
-
-        def pair_sum(first, difference, name):
-            planes = sbuf([P, PACK, V], F32, name)
-            nc.vector.scalar_tensor_tensor(flat(planes), flat(first), 2.0, flat(difference), ALU.mult, ALU.add)
-            return planes
 
         def weave_on_both(planes, name):
             woven = sbuf([P, V, PACK], BF16, "woven_" + name)
@@ -174,48 +179,129 @@ def tile_picked_ymeshcnn_relu_po_kernel(tc, x_words, x_scales, w1, w2, w3, w4, w
         def product(name, mx):
             for t in range(PACK):
                 if name == operands[0]:
-                    y_banks[t] = psum.tile([P, V], F32, name="y_bank%d" % t, tag="bank%d" % ((len(pieces) + t) % BANKS))
+                    y_banks[t] = psum.tile([P, V], F32, name="y_bank%d" % t, tag="bank%d" % (1 + t))
+                codes, scales, cols = w_mx[name][t]
                 nc.tensor.matmul_mx(
                     out=y_banks[t][:],
-                    lhsT=w_mx[name][0][:, plane_cols(t)].bitcast(FP8X4),
-                    lhsT_scale=w_mx[name][1][:, plane_cols(t)],
+                    lhsT=codes[:, cols].bitcast(FP8X4),
+                    lhsT_scale=scales[:, cols],
                     rhs=mx[0][:].bitcast(FP8X4),
                     rhs_scale=mx[1][:],
                     start=(name == operands[0]),
                     stop=(name == operands[-1]),
                 )
 
-        def quantize_weight(name, tag):
-            w_mx[name] = mx_tiles(N, "w_" + name, tag)
-            quantize(w_mx[name], slice(0, N), w_dealt[name][:].rearrange("p t m j -> p (t m j)"))
+        def quantize_weight(name, mx):
+            quantize(mx, slice(0, N), w_dealt[name][:].rearrange("p t m j -> p (t m j)"))
+            w_mx[name] = [mx + (plane_cols(t),) for t in range(PACK)]
 
-        planes = {name: sbuf([P, PACK, V], F32, name) for name in ("hea", "heb", "d1", "d2", "hown")}
+        def quantize_two_planes(name, dealt):
+            mx = mx_tiles(2 * P, "w_" + name)
+            for t in range(2):
+                quantize_plane(mx, dealt, t)
+            return [mx + (plane_cols(t),) for t in range(2)]
+
+        def late_codes(width, name, region, offset):
+            return late_tile([P, width], U32, name + "_codes", region, offset), sbuf([P, width], U8, name + "_scales")
+
+        def deal_planes(copy, dealt, raw, first):
+            copy(
+                out=dealt[:].rearrange("p t (m e) j -> p m j e t", e=2),
+                in_=raw[:].rearrange("p j (m e t) -> p m j e t", e=2, t=PACK)[:, :, :, :, first : first + 2],
+            )
+
+        def turn_sum(name, first, difference, t):
+            for half in range(V // P):
+                for i, term in enumerate((first, first, difference)):
+                    nc.tensor.matmul(
+                        turned_banks[name, half][:, t, :],
+                        planes[term][:, t, P * half : P * (half + 1)],
+                        identity[:],
+                        start=(i == 0),
+                        stop=(i == 2),
+                        is_transpose=True,
+                    )
+
+        def round_turned(name, slot):
+            for half in range(V // P):
+                turned[name, half] = late_tile([P, 2, P, 2], BF16, "turned_sb_%s%d" % (name, half), "d2", 2 * woven_bytes + turned_bytes * (2 * slot + half))
+                nc.scalar.activation(turned[name, half][:], turned_banks[name, half][:].rearrange("v (u e) p -> v u p e", e=2), ACT.Copy)
+
+        def turn_back(name, slot):
+            words = psum.tile([P, 2, V], F32, name="words_" + name, tag="bank%d" % (len(pieces) + slot))
+            for half in range(V // P):
+                for u in range(2):
+                    nc.tensor.transpose(words[:, u, P * half : P * (half + 1)], turned[name, half][:, u].rearrange("v p e -> v (p e)").bitcast(F32), identity[:])
+            return words
+
+        def weave_words(name, words):
+            woven[name] = sbuf([P, V, PACK], BF16, "woven_" + name)
+            nc.scalar.copy(out=woven[name][:].bitcast(F32), in_=words[:].rearrange("p u v -> p v u"))
+
+        def weave_abs(name, slot):
+            woven[name] = late_tile([P, V, PACK], BF16, "woven_" + name, "d2", woven_bytes * slot)
+            nc.scalar.activation(as_woven(woven[name][:]), as_planes(planes[name]), ACT.Abs)
+
+        def round_weight(name, dealt):
+            w_dealt[name] = dealt
+            deal(nc.scalar.copy, dealt, w_raw[name], 0, P)
+
+        woven_bytes = 2 * V * PACK
+        turned_bytes = 2 * H
+        dealt_shape = [P, PACK, P, PACK]
+        woven = {}
+        turned = {}
+        turned_banks = {}
+        for i, name in enumerate(("s1", "s2")):
+            for half in range(V // P):
+                turned_banks[name, half] = psum.tile([P, PACK, P], F32, name="turned_%s%d" % (name, half), tag="bank%d" % ((len(pieces) + 2 * i + half) % BANKS))
+
+        planes = {name: sbuf([P, PACK, V], F32, name) for name in ("hea", "heb", "d1")}
         for t in range(PACK):
             pick(planes["hea"], "ea", t)
             pick(planes["heb"], "eb", t)
             pick_minus(planes["d1"], "ec", planes["hea"], t)
+            turn_sum("s1", "hea", "d1", t)
+        planes["d2"] = late_tile([P, PACK, V], F32, "d2", "d1", 0)
+        for t in range(PACK):
             pick_minus(planes["d2"], "ed", planes["heb"], t)
+            turn_sum("s2", "heb", "d2", t)
+        planes["hown"] = late_tile([P, PACK, V], F32, "hown", "d1", raw_bytes // 2)
+        for t in range(PACK):
             pick(planes["hown"], "own", t)
-        planes["s1"] = pair_sum(planes["hea"], planes["d1"], "s1")
-        planes["s2"] = pair_sum(planes["heb"], planes["d2"], "s2")
 
-        for i, name in enumerate(operands):
-            round_weight(name, ("w1_1_codes", "w1_1_scales")[i] if i < 2 else "w_%s_raw" % operands[i - 2])
-        woven = sbuf([P, len(operands), V, PACK], BF16, "woven", "w_%s_raw" % operands[-1])
-        for i, name in enumerate(operands):
-            nc.scalar.activation(as_woven(woven[:, i]), as_planes(planes[name]), ACT.Abs if name in ("d1", "d2") else ACT.Copy)
+        round_weight("d1", sbuf(dealt_shape, BF16, "w_dealt_d1", "w1_1_codes"))
+        round_weight("s1", sbuf(dealt_shape, BF16, "w_dealt_s1", "w1_1_scales"))
+        round_weight("d2", sbuf(dealt_shape, BF16, "w_dealt_d2", "picked_words1"))
+        weave_abs("d1", 0)
+        round_turned("s1", 1)
+        words = turn_back("s1", 0)
+        weave_abs("d2", 1)
+        round_turned("s2", 0)
+        weave_words("s1", words)
+        words = turn_back("s2", 1)
+        round_weight("hown", sbuf(dealt_shape, BF16, "w_dealt_hown", "w_s1_raw"))
+        weave_words("s2", words)
+        last_dealt = [late_tile([P, 2, P, PACK], BF16, "w_dealt_s2_%d" % i, "hown", woven_bytes * i) for i in range(2)]
+        deal_planes(nc.scalar.copy, last_dealt[1], w_raw["s2"], 2)
 
-        quantize_weight(operands[0], None)
-        for i, name in enumerate(operands):
-            mx = mx_tiles(V, name)
-            quantize(mx, slice(0, V), woven[:, i].rearrange("p v t -> p (v t)"))
-            if name == operands[-1]:
-                w_mx[name] = mx_tiles(N, "w_" + name, operands[i - 1])
-                for t in range(PACK):
-                    quantize_plane(w_mx[name], w_dealt[name], t)
-            product(name, mx)
-            if i + 2 < len(operands):
-                quantize_weight(operands[i + 1], name)
+        quantize_weight("d1", mx_tiles(N, "w_d1"))
+        d1_mx = late_codes(V, "d1", "d2", 2 * woven_bytes + 2 * turned_bytes)
+        quantize(d1_mx, slice(0, V), flat(woven["d1"]))
+        product("d1", d1_mx)
+        woven["hown"] = late_tile([P, V, PACK], BF16, "woven_hown", "d2", 2 * woven_bytes + 3 * turned_bytes)
+        nc.vector.tensor_copy(out=as_woven(woven["hown"][:]), in_=as_planes(planes["hown"]))
+        quantize_weight("s1", late_codes(N, "w_s1", "d2", 0))
+        product("s1", quantize_woven(woven["s1"], "s1"))
+        quantize_weight("d2", late_codes(N, "w_d2", "d1", raw_bytes // 2))
+        product("d2", quantize_woven(woven["d2"], "d2"))
+        hown_mx = quantize_woven(woven["hown"], "hown")
+        quantize_weight("hown", mx_tiles(N, "w_hown"))
+        product("hown", hown_mx)
+        deal_planes(nc.vector.tensor_copy, last_dealt[0], w_raw["s2"], 0)
+        s2_mx = quantize_woven(woven["s2"], "s2")
+        w_mx["s2"] = quantize_two_planes("s2_0", last_dealt[0]) + quantize_two_planes("s2_1", last_dealt[1])
+        product("s2", s2_mx)
 
         y = sbuf([P, PACK, V], F32, "y")
         out_planes = out_0.rearrange("(p t) v -> p t v", t=PACK)

@@ -24,7 +24,7 @@ BANKS = 8
 RUN = 4
 
 W1_PIECES = ((0, 0, 64, 64), (0, 64, 128, 88), (1, 0, 96, 36), (1, 96, 128, 108))
-WEAVE_SCALAR_RUNS = 22
+WEAVE_VECTOR_RUNS = 38
 
 
 def tile_picked_ymeshcnn_relu_po_kernel(tc, x_words, x_scales, w1, w2, w3, w4, w5, w6, offs, own, ea, eb, ec, ed, out_0, out_1, out_2):
@@ -114,7 +114,7 @@ def tile_picked_ymeshcnn_relu_po_kernel(tc, x_words, x_scales, w1, w2, w3, w4, w
             )
         w1_raw.extend([load_w1_piece(i) for i in range(1, len(W1_PIECES))])
         lists["own"] = load_list(own, "own")
-        operands = ("d1", "s1", "d2", "hown", "s2")
+        operands = ("d1", "d2", "s1", "hown", "s2")
         loaded = ("d1", "s1", "d2", "hown", "s2")
         w_raw = {name: load_weight(ap, "w_" + name) for name, ap in zip(loaded, (w4, w3, w6, w2, w5))}
 
@@ -148,7 +148,7 @@ def tile_picked_ymeshcnn_relu_po_kernel(tc, x_words, x_scales, w1, w2, w3, w4, w
                         )
         h = [keep.tile([P, S], F32, name="h%d" % t) for t in range(PACK)]
         for bank, (t, edges) in zip(h_banks, pieces):
-            if edges.start > 0:
+            if edges.stop < S:
                 nc.vector.tensor_scalar_max(h[t][:, edges], bank[:], 0.0)
             else:
                 nc.scalar.activation(h[t][:, edges], bank[:], ACT.Relu)
@@ -164,12 +164,6 @@ def tile_picked_ymeshcnn_relu_po_kernel(tc, x_words, x_scales, w1, w2, w3, w4, w
 
         def pick_minus(planes, list_name, first, t):
             nc.vector.tensor_tensor(planes[:, t, :], h[t][:].indirect(lists[list_name][:]), first[:, t, :], ALU.subtract)
-
-        def weave_on_both(planes, name):
-            woven = sbuf([P, V, PACK], BF16, "woven_" + name)
-            nc.scalar.copy(out=as_woven(woven[:])[:, 0:WEAVE_SCALAR_RUNS], in_=as_planes(planes)[:, 0:WEAVE_SCALAR_RUNS])
-            nc.vector.tensor_copy(out=as_woven(woven[:])[:, WEAVE_SCALAR_RUNS:], in_=as_planes(planes)[:, WEAVE_SCALAR_RUNS:])
-            return woven
 
         def quantize_woven(woven, name):
             mx = mx_tiles(V, name)
@@ -210,17 +204,16 @@ def tile_picked_ymeshcnn_relu_po_kernel(tc, x_words, x_scales, w1, w2, w3, w4, w
                 in_=raw[:].rearrange("p j (m e t) -> p m j e t", e=2, t=PACK)[:, :, :, :, first : first + 2],
             )
 
-        def turn_sum(name, first, difference, t):
+        def turn(name, term, t, start, stop):
             for half in range(V // P):
-                for i, term in enumerate((first, first, difference)):
-                    nc.tensor.matmul(
-                        turned_banks[name, half][:, t, :],
-                        planes[term][:, t, P * half : P * (half + 1)],
-                        identity[:],
-                        start=(i == 0),
-                        stop=(i == 2),
-                        is_transpose=True,
-                    )
+                nc.tensor.matmul(
+                    turned_banks[name, half][:, t, :],
+                    planes[term][:, t, P * half : P * (half + 1)],
+                    identity[:],
+                    start=start,
+                    stop=stop,
+                    is_transpose=True,
+                )
 
         def round_turned(name, slot):
             for half in range(V // P):
@@ -261,21 +254,25 @@ def tile_picked_ymeshcnn_relu_po_kernel(tc, x_words, x_scales, w1, w2, w3, w4, w
             pick(planes["hea"], "ea", t)
             pick(planes["heb"], "eb", t)
             pick_minus(planes["d1"], "ec", planes["hea"], t)
-            turn_sum("s1", "hea", "d1", t)
+            for name, term, start, stop in (
+                ("s1", "hea", t == 0, False),
+                ("s1", "hea", False, False),
+                ("s1", "d1", False, t == PACK - 1),
+                ("s2", "heb", t == 0, False),
+                ("s2", "heb", False, False),
+            ):
+                turn(name, term, t, start, stop)
         planes["d2"] = late_tile([P, PACK, V], F32, "d2", "d1", 0)
         for t in range(PACK):
             pick_minus(planes["d2"], "ed", planes["heb"], t)
-            turn_sum("s2", "heb", "d2", t)
-        planes["hown"] = late_tile([P, PACK, V], F32, "hown", "d1", raw_bytes // 2)
-        for t in range(PACK):
-            pick(planes["hown"], "own", t)
+            turn("s2", "d2", t, False, t == PACK - 1)
 
         round_weight("d1", sbuf(dealt_shape, BF16, "w_dealt_d1", "w1_1_codes"))
         round_weight("s1", sbuf(dealt_shape, BF16, "w_dealt_s1", "w1_1_scales"))
         round_weight("d2", sbuf(dealt_shape, BF16, "w_dealt_d2", "picked_words1"))
-        weave_abs("d1", 0)
         round_turned("s1", 1)
         words = turn_back("s1", 0)
+        weave_abs("d1", 0)
         weave_abs("d2", 1)
         round_turned("s2", 0)
         weave_words("s1", words)
@@ -285,18 +282,19 @@ def tile_picked_ymeshcnn_relu_po_kernel(tc, x_words, x_scales, w1, w2, w3, w4, w
         last_dealt = [late_tile([P, 2, P, PACK], BF16, "w_dealt_s2_%d" % i, "hown", woven_bytes * i) for i in range(2)]
         deal_planes(nc.scalar.copy, last_dealt[1], w_raw["s2"], 2)
 
-        quantize_weight("d1", mx_tiles(N, "w_d1"))
-        d1_mx = late_codes(V, "d1", "d2", 2 * woven_bytes + 2 * turned_bytes)
-        quantize(d1_mx, slice(0, V), flat(woven["d1"]))
-        product("d1", d1_mx)
-        woven["hown"] = late_tile([P, V, PACK], BF16, "woven_hown", "d2", 2 * woven_bytes + 3 * turned_bytes)
-        nc.vector.tensor_copy(out=as_woven(woven["hown"][:]), in_=as_planes(planes["hown"]))
-        quantize_weight("s1", late_codes(N, "w_s1", "d2", 0))
-        product("s1", quantize_woven(woven["s1"], "s1"))
-        quantize_weight("d2", late_codes(N, "w_d2", "d1", raw_bytes // 2))
+        for name in ("d1", "s1", "d2"):
+            quantize_weight(name, mx_tiles(N, "w_" + name))
+        product("d1", quantize_woven(woven["d1"], "d1"))
         product("d2", quantize_woven(woven["d2"], "d2"))
-        hown_mx = quantize_woven(woven["hown"], "hown")
+        planes["hown"] = late_tile([P, PACK, V], F32, "hown", "d1", 0)
+        for t in range(PACK):
+            pick(planes["hown"], "own", t)
+        product("s1", quantize_woven(woven["s1"], "s1"))
+        woven["hown"] = late_tile([P, V, PACK], BF16, "woven_hown", "d2", 2 * woven_bytes + turned_bytes)
+        nc.vector.tensor_copy(out=as_woven(woven["hown"][:]), in_=as_planes(planes["hown"]))
         quantize_weight("hown", mx_tiles(N, "w_hown"))
+        hown_mx = late_codes(V, "hown", "hown", 2 * woven_bytes)
+        quantize(hown_mx, slice(0, V), flat(woven["hown"]))
         product("hown", hown_mx)
         deal_planes(nc.vector.tensor_copy, last_dealt[0], w_raw["s2"], 0)
         s2_mx = quantize_woven(woven["s2"], "s2")
@@ -309,7 +307,14 @@ def tile_picked_ymeshcnn_relu_po_kernel(tc, x_words, x_scales, w1, w2, w3, w4, w
             nc.scalar.copy(out=y[:, t, :], in_=y_banks[t][:])
             nc.vector.tensor_copy(out=y[:, t + 1, :], in_=y_banks[t + 1][:])
             nc.sync.dma_start(out=out_planes[:, t : t + 2, :], in_=y[:, t : t + 2, :])
-        y_codes, y_scales = quantize_woven(weave_on_both(y, "y"), "y")
+        y_woven = sbuf([P, V, PACK], BF16, "woven_y")
+        half = V // RUN // 2
+        nc.scalar.copy(out=as_woven(y_woven[:])[:, WEAVE_VECTOR_RUNS:], in_=as_planes(y)[:, WEAVE_VECTOR_RUNS:])
+        nc.vector.tensor_copy(out=as_woven(y_woven[:])[:, 0:half], in_=as_planes(y)[:, 0:half])
+        nc.vector.tensor_copy(out=as_woven(y_woven[:])[:, half:WEAVE_VECTOR_RUNS], in_=as_planes(y)[:, half:WEAVE_VECTOR_RUNS])
+        y_codes, y_scales = mx_tiles(V, "y")
+        for cols in (slice(0, V // 2), slice(V // 2, V)):
+            quantize((y_codes, y_scales), cols, y_woven[:, cols].rearrange("p v t -> p (v t)"))
         nc.sync.dma_start(out=out_1[0].rearrange("p v t -> p (v t)").bitcast(I32), in_=y_codes[:].bitcast(I32))
         for q in range(P // QUADRANT):
             queue = nc.scalar if q % 2 else nc.sync

@@ -125,35 +125,37 @@ def tile_picked_ymeshcnn_relu_po_kernel(tc, x_words, x_scales, w1, w2, w3, w4, w
             nc.vector.tensor_copy(picked_words[o][:], words_in[o][:].bitcast(U32).indirect(lists["offs"][:]))
         picked_scales = sbuf([P, S], U8, "picked_scales")
         nc.vector.tensor_copy(picked_scales[:], scales_in[:].indirect(lists["offs"][:]))
-        for o in range(K // K_PASS):
-            dealt = sbuf([P, PACK, P, PACK], BF16, "w1_dealt")
-            for raw, (piece_pass, m0, m1, split) in zip(w1_raw, W1_PIECES):
-                if piece_pass == o:
-                    deal_piece(nc.scalar.copy, dealt, raw, m0, m0, split)
-                    if split < m1:
-                        deal_piece(nc.vector.tensor_copy, dealt, raw, m0, split, m1)
-            w1_mx = mx_tiles(H, "w1_%d" % o)
-            for t in range(PACK):
-                quantize_plane(w1_mx, dealt, t)
-                for bank, (plane, edges) in zip(h_banks, pieces):
-                    if plane == t:
-                        nc.tensor.matmul_mx(
-                            out=bank[:],
-                            lhsT=w1_mx[0][:, plane_cols(t)].bitcast(FP8X4),
-                            lhsT_scale=w1_mx[1][:, plane_cols(t)],
-                            rhs=picked_words[o][:, edges].bitcast(FP8X4),
-                            rhs_scale=picked_scales[PACK * o : P, edges],
-                            start=(o == 0),
-                            stop=(o == K // K_PASS - 1),
-                        )
+        w1_dealt = [sbuf([P, PACK, P, PACK], BF16, "w1_dealt%d" % o) for o in range(K // K_PASS)]
+        for raw, (o, m0, m1, split) in zip(w1_raw, W1_PIECES):
+            deal_piece(nc.scalar.copy, w1_dealt[o], raw, m0, m0, split)
+            if split < m1:
+                deal_piece(nc.vector.tensor_copy, w1_dealt[o], raw, m0, split, m1)
+        for o, t in ((0, 0), (0, 1), (0, 2), (1, 0), (1, 1), (0, 3), (1, 2), (1, 3)):
+            mx = mx_tiles(P, "w1_%d%d" % (o, t), "w1_piece%d_raw" % (len(W1_PIECES) - 1) if (o, t) == (0, PACK - 1) else None)
+            quantize(mx, slice(0, P), w1_dealt[o][:, t].rearrange("p m j -> p (m j)"))
+            for bank, (plane, edges) in zip(h_banks, pieces):
+                if plane == t:
+                    nc.tensor.matmul_mx(
+                        out=bank[:],
+                        lhsT=mx[0][:].bitcast(FP8X4),
+                        lhsT_scale=mx[1][:],
+                        rhs=picked_words[o][:, edges].bitcast(FP8X4),
+                        rhs_scale=picked_scales[PACK * o : P, edges],
+                        start=(o == 0),
+                        stop=(o == K // K_PASS - 1),
+                    )
         h = [keep.tile([P, S], F32, name="h%d" % t) for t in range(PACK)]
+        first_dealt = sbuf([P, PACK, P, PACK], BF16, "w_dealt_d1", "w1_11_codes")
         for bank, (t, edges) in zip(h_banks, pieces):
             if edges.stop < S:
                 nc.vector.tensor_scalar_max(h[t][:, edges], bank[:], 0.0)
             else:
                 nc.scalar.activation(h[t][:, edges], bank[:], ACT.Relu)
+            if t == 1:
+                deal(nc.scalar.copy, first_dealt, w_raw["d1"], 0, P // 2)
+        deal(nc.scalar.copy, first_dealt, w_raw["d1"], P // 2, P)
 
-        w_dealt = {}
+        w_dealt = {"d1": first_dealt}
         w_mx = {}
         y_banks = {}
         identity = sbuf([P, P], F32, "identity")
@@ -267,8 +269,7 @@ def tile_picked_ymeshcnn_relu_po_kernel(tc, x_words, x_scales, w1, w2, w3, w4, w
             pick_minus(planes["d2"], "ed", planes["heb"], t)
             turn("s2", "d2", t, False, t == PACK - 1)
 
-        round_weight("d1", sbuf(dealt_shape, BF16, "w_dealt_d1", "w1_1_codes"))
-        round_weight("s1", sbuf(dealt_shape, BF16, "w_dealt_s1", "w1_1_scales"))
+        round_weight("s1", sbuf(dealt_shape, BF16, "w_dealt_s1", "w1_13_codes"))
         round_weight("d2", sbuf(dealt_shape, BF16, "w_dealt_d2", "picked_words1"))
         round_turned("s1", 1)
         words = turn_back("s1", 0)

@@ -25,6 +25,7 @@ RUN = 4
 
 W1_PIECES = ((0, 0, 64, 64), (0, 64, 128, 88), (1, 0, 96, 36), (1, 96, 128, 108))
 WEAVE_VECTOR_RUNS = 38
+HOWN_SCALAR_RUNS = 16
 
 
 def tile_picked_ymeshcnn_relu_po_kernel(tc, x_words, x_scales, w1, w2, w3, w4, w5, w6, offs, own, ea, eb, ec, ed, out_0, out_1, out_2):
@@ -278,24 +279,26 @@ def tile_picked_ymeshcnn_relu_po_kernel(tc, x_words, x_scales, w1, w2, w3, w4, w
         round_turned("s2", 0)
         weave_words("s1", words)
         words = turn_back("s2", 1)
+        for name in ("d1", "s1", "d2"):
+            quantize_weight(name, mx_tiles(N, "w_" + name))
+        product("d1", quantize_woven(woven["d1"], "d1"))
+        planes["hown"] = sbuf([P, PACK, V], F32, "hown", "d1")
+        for t in range(PACK):
+            pick(planes["hown"], "own", t)
+        d2_mx = late_codes(V, "d2", "d2", 2 * woven_bytes)
+        quantize(d2_mx, slice(0, V), flat(woven["d2"]))
+        product("d2", d2_mx)
+        woven["hown"] = late_tile([P, V, PACK], BF16, "woven_hown", "d2", 2 * woven_bytes + turned_bytes)
+        nc.vector.tensor_copy(out=as_woven(woven["hown"][:])[:, HOWN_SCALAR_RUNS:], in_=as_planes(planes["hown"])[:, HOWN_SCALAR_RUNS:])
         round_weight("hown", sbuf(dealt_shape, BF16, "w_dealt_hown", "w_s1_raw"))
+        nc.scalar.copy(out=as_woven(woven["hown"][:])[:, 0:HOWN_SCALAR_RUNS], in_=as_planes(planes["hown"])[:, 0:HOWN_SCALAR_RUNS])
         weave_words("s2", words)
         last_dealt = [late_tile([P, 2, P, PACK], BF16, "w_dealt_s2_%d" % i, "hown", woven_bytes * i) for i in range(2)]
         deal_planes(nc.scalar.copy, last_dealt[1], w_raw["s2"], 2)
 
-        for name in ("d1", "s1", "d2"):
-            quantize_weight(name, mx_tiles(N, "w_" + name))
-        product("d1", quantize_woven(woven["d1"], "d1"))
-        product("d2", quantize_woven(woven["d2"], "d2"))
-        planes["hown"] = late_tile([P, PACK, V], F32, "hown", "d1", 0)
-        for t in range(PACK):
-            pick(planes["hown"], "own", t)
         product("s1", quantize_woven(woven["s1"], "s1"))
-        woven["hown"] = late_tile([P, V, PACK], BF16, "woven_hown", "d2", 2 * woven_bytes + turned_bytes)
-        nc.vector.tensor_copy(out=as_woven(woven["hown"][:]), in_=as_planes(planes["hown"]))
         quantize_weight("hown", mx_tiles(N, "w_hown"))
-        hown_mx = late_codes(V, "hown", "hown", 2 * woven_bytes)
-        quantize(hown_mx, slice(0, V), flat(woven["hown"]))
+        hown_mx = quantize_woven(woven["hown"], "hown")
         product("hown", hown_mx)
         deal_planes(nc.vector.tensor_copy, last_dealt[0], w_raw["s2"], 0)
         s2_mx = quantize_woven(woven["s2"], "s2")

@@ -23,7 +23,9 @@ QUADRANT = 32
 BANKS = 8
 RUN = 4
 
-W1_PIECES = ((0, 0, 64, 64), (0, 64, 128, 88), (1, 0, 96, 36), (1, 96, 128, 108))
+PASS0_VECTOR = 84
+PLANE0_VECTOR = 72
+LATER_VECTOR = 76
 WEAVE_VECTOR_RUNS = 38
 HOWN_SCALAR_RUNS = 16
 
@@ -62,16 +64,6 @@ def tile_picked_ymeshcnn_relu_po_kernel(tc, x_words, x_scales, w1, w2, w3, w4, w
             nc.sync.dma_start(out=raw[:], in_=rows.rearrange("(p j) c -> p j c", j=PACK))
             return raw
 
-        def load_w1_piece(i):
-            o, m0, m1, split = W1_PIECES[i]
-            return load_weight(w1[K_PASS * o : K_PASS * (o + 1), PACK * m0 : PACK * m1], "w1_piece%d" % i)
-
-        def deal_piece(copy, dealt, raw, first, m0, m1):
-            copy(
-                out=dealt[:].rearrange("p t (m e) j -> p m j e t", e=2)[:, m0 // 2 : m1 // 2],
-                in_=raw[:].rearrange("p j (m e t) -> p m j e t", e=2, t=PACK)[:, (m0 - first) // 2 : (m1 - first) // 2],
-            )
-
         def deal(copy, dealt, raw, m0, m1):
             copy(
                 out=dealt[:].rearrange("p t (m e) j -> p m j e t", e=2)[:, m0 // 2 : m1 // 2],
@@ -100,61 +92,91 @@ def tile_picked_ymeshcnn_relu_po_kernel(tc, x_words, x_scales, w1, w2, w3, w4, w
             return tile[:].rearrange("p a b -> p (a b)")
 
         scales_in = sbuf([P, T], U8, "scales_in")
-        nc.vector.memset(scales_in[:].bitcast(I32), 0)
+        nc.gpsimd.memset(scales_in[:].bitcast(I32), 0)
         lists = {"offs": load_list(offs, "offs")}
         words_in = [load_words(0)]
-        for name, ap in (("ea", ea), ("ec", ec), ("eb", eb)):
-            lists[name] = load_list(ap, name)
-        words_in.append(load_words(1))
-        lists["ed"] = load_list(ed, "ed")
-        w1_raw = [load_w1_piece(0)]
         for q in range(P // QUADRANT):
             nc.sync.dma_start(
                 out=scales_in[QUADRANT * q : QUADRANT * q + 2 * PACK, :].bitcast(I32),
                 in_=x_scales[:, PACK * q : PACK * (q + 1), :].bitcast(I32),
             )
-        w1_raw.extend([load_w1_piece(i) for i in range(1, len(W1_PIECES))])
-        lists["own"] = load_list(own, "own")
+        w1_raw = [load_weight(w1[0:K_PASS, :], "w1_pass0")]
+        words_in.append(load_words(1))
+        w1_raw.append(load_weight(w1[K_PASS:K, :], "w1_pass1"))
+        first_raw = late.tile([P, 2, PACK, N // 2], F32, name="w_d1_raw", align_bytes=64, offset=regions["w_d1"])
+        first_rows = w4.rearrange("(p j) c -> p j c", j=PACK)
+        nc.sync.dma_start(out=first_raw[:, 0], in_=first_rows[:, :, 0 : N // 2])
+        for name, ap in (("ea", ea), ("eb", eb), ("ec", ec)):
+            lists[name] = load_list(ap, name)
+        nc.sync.dma_start(out=first_raw[:, 1], in_=first_rows[:, :, N // 2 : N])
+        for name, ap in (("ed", ed), ("own", own)):
+            lists[name] = load_list(ap, name)
         operands = ("d1", "d2", "s1", "hown", "s2")
-        loaded = ("d1", "s1", "d2", "hown", "s2")
-        w_raw = {name: load_weight(ap, "w_" + name) for name, ap in zip(loaded, (w4, w3, w6, w2, w5))}
+        loaded = ("s1", "d2", "hown", "s2")
+        w_raw = {name: load_weight(ap, "w_" + name) for name, ap in zip(loaded, (w3, w6, w2, w5))}
 
         pieces = [(0, slice(0, S // 2)), (0, slice(S // 2, S))] + [(t, slice(0, S)) for t in range(1, PACK)]
         h_banks = [psum.tile([P, edges.stop - edges.start], F32, name="h_bank%d" % i, tag="bank%d" % i) for i, (t, edges) in enumerate(pieces)]
-        picked_words = [sbuf([P, S], U32, "picked_words%d" % o) for o in range(K // K_PASS)]
-        for o in range(K // K_PASS):
-            nc.vector.tensor_copy(picked_words[o][:], words_in[o][:].bitcast(U32).indirect(lists["offs"][:]))
+        picked_words = [sbuf([P, S], U32, "picked_words0")]
         picked_scales = sbuf([P, S], U8, "picked_scales")
-        nc.vector.tensor_copy(picked_scales[:], scales_in[:].indirect(lists["offs"][:]))
-        w1_dealt = [sbuf([P, PACK, P, PACK], BF16, "w1_dealt%d" % o) for o in range(K // K_PASS)]
-        for raw, (o, m0, m1, split) in zip(w1_raw, W1_PIECES):
-            deal_piece(nc.scalar.copy, w1_dealt[o], raw, m0, m0, split)
-            if split < m1:
-                deal_piece(nc.vector.tensor_copy, w1_dealt[o], raw, m0, split, m1)
-        for o, t in ((0, 0), (0, 1), (0, 2), (1, 0), (1, 1), (0, 3), (1, 2), (1, 3)):
-            mx = mx_tiles(P, "w1_%d%d" % (o, t), "w1_piece%d_raw" % (len(W1_PIECES) - 1) if (o, t) == (0, PACK - 1) else None)
-            quantize(mx, slice(0, P), w1_dealt[o][:, t].rearrange("p m j -> p (m j)"))
+
+        def first_product(o, t, mx, cols):
             for bank, (plane, edges) in zip(h_banks, pieces):
                 if plane == t:
                     nc.tensor.matmul_mx(
                         out=bank[:],
-                        lhsT=mx[0][:].bitcast(FP8X4),
-                        lhsT_scale=mx[1][:],
+                        lhsT=mx[0][:, cols].bitcast(FP8X4),
+                        lhsT_scale=mx[1][:, cols],
                         rhs=picked_words[o][:, edges].bitcast(FP8X4),
                         rhs_scale=picked_scales[PACK * o : P, edges],
                         start=(o == 0),
                         stop=(o == K // K_PASS - 1),
                     )
+
+        nc.vector.tensor_copy(picked_words[0][:], words_in[0][:].bitcast(U32).indirect(lists["offs"][:]))
+        nc.vector.tensor_copy(picked_scales[:], scales_in[:].indirect(lists["offs"][:]))
+        w1_dealt0 = sbuf([P, PACK, P, PACK], BF16, "w1_dealt0")
+        deal(nc.vector.tensor_copy, w1_dealt0, w1_raw[0], 0, PASS0_VECTOR)
+        deal(nc.scalar.copy, w1_dealt0, w1_raw[0], PASS0_VECTOR, P)
+        for u in range(2):
+            mx = mx_tiles(2 * P, "w1_0%d" % u)
+            quantize(mx, slice(0, 2 * P), w1_dealt0[:, 2 * u : 2 * u + 2].rearrange("p t m j -> p (t m j)"))
+            for e in range(2):
+                first_product(0, 2 * u + e, mx, plane_cols(e))
+        picked_words.append(sbuf([P, S], U32, "picked_words1", "w1_dealt0"))
+        nc.vector.tensor_copy(picked_words[1][:], words_in[1][:].bitcast(U32).indirect(lists["offs"][:]))
+        first_plane = sbuf([P, P, PACK], BF16, "w1_first_plane")
+        raw_columns = w1_raw[1][:].rearrange("p j (m t) -> p t m j", t=PACK)
+        nc.vector.tensor_copy(out=first_plane[:, 0:PLANE0_VECTOR], in_=raw_columns[:, 0, 0:PLANE0_VECTOR])
+        nc.scalar.copy(out=first_plane[:, PLANE0_VECTOR:P], in_=raw_columns[:, 0, PLANE0_VECTOR:P])
+        mx = mx_tiles(P, "w1_10")
+        quantize(mx, slice(0, P), flat(first_plane))
+        first_product(1, 0, mx, slice(0, P))
+        later_planes = sbuf([P, PACK - 1, P, PACK], BF16, "w1_later_planes", "w1_first_plane")
+        for copy, m0, m1 in ((nc.vector.tensor_copy, 0, LATER_VECTOR), (nc.scalar.copy, LATER_VECTOR, P)):
+            copy(
+                out=later_planes[:].rearrange("p t (m e) j -> p m j e t", e=2)[:, m0 // 2 : m1 // 2],
+                in_=w1_raw[1][:].rearrange("p j (m e t) -> p m j e t", e=2, t=PACK)[:, m0 // 2 : m1 // 2, :, :, 1:PACK],
+            )
         h = [keep.tile([P, S], F32, name="h%d" % t) for t in range(PACK)]
-        first_dealt = sbuf([P, PACK, P, PACK], BF16, "w_dealt_d1", "w1_11_codes")
-        for bank, (t, edges) in zip(h_banks, pieces):
-            if edges.stop < S:
-                nc.vector.tensor_scalar_max(h[t][:, edges], bank[:], 0.0)
-            else:
-                nc.scalar.activation(h[t][:, edges], bank[:], ACT.Relu)
-            if t == 1:
-                deal(nc.scalar.copy, first_dealt, w_raw["d1"], 0, P // 2)
-        deal(nc.scalar.copy, first_dealt, w_raw["d1"], P // 2, P)
+        nc.vector.tensor_scalar_max(h[0][:, 0 : S // 2], h_banks[0][:], 0.0)
+        nc.scalar.activation(h[0][:, S // 2 : S], h_banks[1][:], ACT.Relu)
+        for t in range(1, PACK):
+            mx = mx_tiles(P, "w1_1%d" % t)
+            quantize(mx, slice(0, P), later_planes[:, t - 1].rearrange("p m j -> p (m j)"))
+            first_product(1, t, mx, slice(0, P))
+        first_dealt = sbuf([P, PACK, P, PACK], BF16, "w_dealt_d1", "w1_10_codes")
+
+        def deal_first(half):
+            nc.scalar.copy(
+                out=first_dealt[:].rearrange("p t (m e) j -> p m j e t", e=2)[:, P // 4 * half : P // 4 * (half + 1)],
+                in_=first_raw[:, half].rearrange("p j (m e t) -> p m j e t", e=2, t=PACK),
+            )
+
+        deal_first(0)
+        for bank, (t, edges) in zip(h_banks[2:], pieces[2:]):
+            nc.scalar.activation(h[t][:, edges], bank[:], ACT.Relu)
+        deal_first(1)
 
         w_dealt = {"d1": first_dealt}
         w_mx = {}
@@ -271,7 +293,7 @@ def tile_picked_ymeshcnn_relu_po_kernel(tc, x_words, x_scales, w1, w2, w3, w4, w
             turn("s2", "d2", t, False, t == PACK - 1)
 
         round_weight("s1", sbuf(dealt_shape, BF16, "w_dealt_s1", "w1_13_codes"))
-        round_weight("d2", sbuf(dealt_shape, BF16, "w_dealt_d2", "picked_words1"))
+        round_weight("d2", sbuf(dealt_shape, BF16, "w_dealt_d2", "w1_dealt0"))
         round_turned("s1", 1)
         words = turn_back("s1", 0)
         weave_abs("d1", 0)

@@ -25,9 +25,11 @@ RUN = 4
 
 PASS0_VECTOR = 84
 PLANE0_VECTOR = 72
+LATER_FILL = 36
 LATER_VECTOR = 76
+FIRST_VECTOR = 36
 WEAVE_VECTOR_RUNS = 38
-HOWN_SCALAR_RUNS = 16
+HOWN_SCALAR_RUNS = 48
 
 
 def tile_picked_ymeshcnn_relu_po_kernel(tc, x_words, x_scales, w1, w2, w3, w4, w5, w6, offs, own, ea, eb, ec, ed, out_0, out_1, out_2):
@@ -41,7 +43,7 @@ def tile_picked_ymeshcnn_relu_po_kernel(tc, x_words, x_scales, w1, w2, w3, w4, w
             return keep.tile(shape, dtype, name=name, tag=tag or name, align_bytes=64)
 
         raw_bytes = 4 * PACK * N
-        regions = {"w_" + name: raw_bytes * i for i, name in enumerate(("d1", "hown", "d2"))}
+        regions = {"w_d1": 0, "w_s1": raw_bytes, "w_d2": 3 * raw_bytes, "w_first": 5 * raw_bytes, "w_second": 2 * raw_bytes - 64}
 
         def late_tile(shape, dtype, name, region, offset):
             return late.tile(shape, dtype, name=name, align_bytes=64, offset=regions["w_" + region] + offset)
@@ -58,7 +60,7 @@ def tile_picked_ymeshcnn_relu_po_kernel(tc, x_words, x_scales, w1, w2, w3, w4, w
 
         def load_weight(rows, name):
             if name in regions:
-                raw = late.tile([P, PACK, rows.shape[1]], F32, name=name + "_raw", align_bytes=64, offset=regions[name])
+                raw = late.tile([P, PACK, N], F32, name=name + "_raw", align_bytes=64, offset=regions[name])[:, :, 0 : rows.shape[1]]
             else:
                 raw = sbuf([P, PACK, rows.shape[1]], F32, name + "_raw")
             nc.sync.dma_start(out=raw[:], in_=rows.rearrange("(p j) c -> p j c", j=PACK))
@@ -112,8 +114,9 @@ def tile_picked_ymeshcnn_relu_po_kernel(tc, x_words, x_scales, w1, w2, w3, w4, w
         for name, ap in (("ed", ed), ("own", own)):
             lists[name] = load_list(ap, name)
         operands = ("d1", "d2", "s1", "hown", "s2")
-        loaded = ("s1", "d2", "hown", "s2")
-        w_raw = {name: load_weight(ap, "w_" + name) for name, ap in zip(loaded, (w3, w6, w2, w5))}
+        w_raw = {"s1": load_weight(w3, "w_s1"), "d2": load_weight(w6, "w_six")}
+        hown_raw = [load_weight(w2[:, 0 : N // 2], "w_d2")]
+        w_raw["s2"] = load_weight(w5, "w_s2")
 
         pieces = [(0, slice(0, S // 2)), (0, slice(S // 2, S))] + [(t, slice(0, S)) for t in range(1, PACK)]
         h_banks = [psum.tile([P, edges.stop - edges.start], F32, name="h_bank%d" % i, tag="bank%d" % i) for i, (t, edges) in enumerate(pieces)]
@@ -149,34 +152,40 @@ def tile_picked_ymeshcnn_relu_po_kernel(tc, x_words, x_scales, w1, w2, w3, w4, w
         raw_columns = w1_raw[1][:].rearrange("p j (m t) -> p t m j", t=PACK)
         nc.vector.tensor_copy(out=first_plane[:, 0:PLANE0_VECTOR], in_=raw_columns[:, 0, 0:PLANE0_VECTOR])
         nc.scalar.copy(out=first_plane[:, PLANE0_VECTOR:P], in_=raw_columns[:, 0, PLANE0_VECTOR:P])
-        mx = mx_tiles(P, "w1_10")
-        quantize(mx, slice(0, P), flat(first_plane))
-        first_product(1, 0, mx, slice(0, P))
-        later_planes = sbuf([P, PACK - 1, P, PACK], BF16, "w1_later_planes", "w1_first_plane")
-        for copy, m0, m1 in ((nc.vector.tensor_copy, 0, LATER_VECTOR), (nc.scalar.copy, LATER_VECTOR, P)):
+        later_planes = sbuf([P, PACK - 1, P, PACK], BF16, "w1_later_planes")
+
+        def deal_later(copy, m0, m1):
             copy(
                 out=later_planes[:].rearrange("p t (m e) j -> p m j e t", e=2)[:, m0 // 2 : m1 // 2],
                 in_=w1_raw[1][:].rearrange("p j (m e t) -> p m j e t", e=2, t=PACK)[:, m0 // 2 : m1 // 2, :, :, 1:PACK],
             )
-        h = [keep.tile([P, S], F32, name="h%d" % t) for t in range(PACK)]
-        nc.vector.tensor_scalar_max(h[0][:, 0 : S // 2], h_banks[0][:], 0.0)
-        nc.scalar.activation(h[0][:, S // 2 : S], h_banks[1][:], ACT.Relu)
+
+        mx = mx_tiles(P, "w1_10")
+        quantize(mx, slice(0, P), flat(first_plane))
+        first_product(1, 0, mx, slice(0, P))
+        deal_later(nc.vector.tensor_copy, 0, LATER_FILL)
+        deal_later(nc.vector.tensor_copy, LATER_FILL, LATER_VECTOR)
+        deal_later(nc.scalar.copy, LATER_VECTOR, P)
         for t in range(1, PACK):
             mx = mx_tiles(P, "w1_1%d" % t)
             quantize(mx, slice(0, P), later_planes[:, t - 1].rearrange("p m j -> p (m j)"))
             first_product(1, t, mx, slice(0, P))
-        first_dealt = sbuf([P, PACK, P, PACK], BF16, "w_dealt_d1", "w1_10_codes")
+        h = [keep.tile([P, S], F32, name="h%d" % t) for t in range(PACK)]
+        nc.vector.tensor_scalar_max(h[0][:, 0 : S // 2], h_banks[0][:], 0.0)
+        nc.scalar.activation(h[0][:, S // 2 : S], h_banks[1][:], ACT.Relu)
+        first_dealt = sbuf([P, PACK, P, PACK], BF16, "w_dealt_d1")
 
-        def deal_first(half):
-            nc.scalar.copy(
-                out=first_dealt[:].rearrange("p t (m e) j -> p m j e t", e=2)[:, P // 4 * half : P // 4 * (half + 1)],
-                in_=first_raw[:, half].rearrange("p j (m e t) -> p m j e t", e=2, t=PACK),
+        def deal_first(copy, half, m0, m1):
+            copy(
+                out=first_dealt[:].rearrange("p t (m e) j -> p m j e t", e=2)[:, P // 4 * half + m0 // 2 : P // 4 * half + m1 // 2],
+                in_=first_raw[:, half].rearrange("p j (m e t) -> p m j e t", e=2, t=PACK)[:, m0 // 2 : m1 // 2],
             )
 
-        deal_first(0)
+        deal_first(nc.vector.tensor_copy, 0, 0, FIRST_VECTOR)
+        deal_first(nc.scalar.copy, 0, FIRST_VECTOR, P // 2)
         for bank, (t, edges) in zip(h_banks[2:], pieces[2:]):
             nc.scalar.activation(h[t][:, edges], bank[:], ACT.Relu)
-        deal_first(1)
+        deal_first(nc.scalar.copy, 1, 0, P // 2)
 
         w_dealt = {"d1": first_dealt}
         w_mx = {}
@@ -214,8 +223,7 @@ def tile_picked_ymeshcnn_relu_po_kernel(tc, x_words, x_scales, w1, w2, w3, w4, w
             quantize(mx, slice(0, N), w_dealt[name][:].rearrange("p t m j -> p (t m j)"))
             w_mx[name] = [mx + (plane_cols(t),) for t in range(PACK)]
 
-        def quantize_two_planes(name, dealt):
-            mx = mx_tiles(2 * P, "w_" + name)
+        def quantize_two_planes(mx, dealt):
             for t in range(2):
                 quantize_plane(mx, dealt, t)
             return [mx + (plane_cols(t),) for t in range(2)]
@@ -240,9 +248,9 @@ def tile_picked_ymeshcnn_relu_po_kernel(tc, x_words, x_scales, w1, w2, w3, w4, w
                     is_transpose=True,
                 )
 
-        def round_turned(name, slot):
+        def round_turned(name, region, offset):
             for half in range(V // P):
-                turned[name, half] = late_tile([P, 2, P, 2], BF16, "turned_sb_%s%d" % (name, half), "d2", 2 * woven_bytes + turned_bytes * (2 * slot + half))
+                turned[name, half] = late_tile([P, 2, P, 2], BF16, "turned_sb_%s%d" % (name, half), region, offset + turned_bytes * half)
                 nc.scalar.activation(turned[name, half][:], turned_banks[name, half][:].rearrange("v (u e) p -> v u p e", e=2), ACT.Copy)
 
         def turn_back(name, slot):
@@ -256,8 +264,8 @@ def tile_picked_ymeshcnn_relu_po_kernel(tc, x_words, x_scales, w1, w2, w3, w4, w
             woven[name] = sbuf([P, V, PACK], BF16, "woven_" + name)
             nc.scalar.copy(out=woven[name][:].bitcast(F32), in_=words[:].rearrange("p u v -> p v u"))
 
-        def weave_abs(name, slot):
-            woven[name] = late_tile([P, V, PACK], BF16, "woven_" + name, "d2", woven_bytes * slot)
+        def weave_abs(name, region, offset):
+            woven[name] = late_tile([P, V, PACK], BF16, "woven_" + name, region, offset)
             nc.scalar.activation(as_woven(woven[name][:]), as_planes(planes[name]), ACT.Abs)
 
         def round_weight(name, dealt):
@@ -274,57 +282,72 @@ def tile_picked_ymeshcnn_relu_po_kernel(tc, x_words, x_scales, w1, w2, w3, w4, w
             for half in range(V // P):
                 turned_banks[name, half] = psum.tile([P, PACK, P], F32, name="turned_%s%d" % (name, half), tag="bank%d" % ((len(pieces) + 2 * i + half) % BANKS))
 
-        planes = {name: sbuf([P, PACK, V], F32, name) for name in ("hea", "heb", "d1")}
+        planes = {}
+
+        planes["hea"] = sbuf([P, PACK, V], F32, "hea")
+        planes["heb"] = sbuf([P, PACK, V], F32, "heb")
+        planes["d1"] = late_tile([P, PACK, V], F32, "d1", "first", 0)
         for t in range(PACK):
             pick(planes["hea"], "ea", t)
             pick(planes["heb"], "eb", t)
             pick_minus(planes["d1"], "ec", planes["hea"], t)
-            for name, term, start, stop in (
-                ("s1", "hea", t == 0, False),
-                ("s1", "hea", False, False),
-                ("s1", "d1", False, t == PACK - 1),
-                ("s2", "heb", t == 0, False),
-                ("s2", "heb", False, False),
-            ):
-                turn(name, term, t, start, stop)
-        planes["d2"] = late_tile([P, PACK, V], F32, "d2", "d1", 0)
+            turn("s1", "hea", t, t == 0, False)
+            turn("s1", "hea", t, False, False)
+            if t > 0:
+                turn("s2", "heb", t - 1, t == 1, False)
+                turn("s2", "heb", t - 1, False, False)
+            turn("s1", "d1", t, False, t == PACK - 1)
+        turn("s2", "heb", PACK - 1, False, False)
+        turn("s2", "heb", PACK - 1, False, False)
+        planes["d2"] = late_tile([P, PACK, V], F32, "d2", "second", 0)
         for t in range(PACK):
             pick_minus(planes["d2"], "ed", planes["heb"], t)
             turn("s2", "d2", t, False, t == PACK - 1)
 
-        round_weight("s1", sbuf(dealt_shape, BF16, "w_dealt_s1", "w1_13_codes"))
-        round_weight("d2", sbuf(dealt_shape, BF16, "w_dealt_d2", "w1_dealt0"))
-        round_turned("s1", 1)
-        words = turn_back("s1", 0)
-        weave_abs("d1", 0)
-        weave_abs("d2", 1)
-        round_turned("s2", 0)
-        weave_words("s1", words)
-        words = turn_back("s2", 1)
-        for name in ("d1", "s1", "d2"):
-            quantize_weight(name, mx_tiles(N, "w_" + name))
+        round_weight("s1", sbuf(dealt_shape, BF16, "w_dealt_s1"))
+        round_weight("d2", sbuf(dealt_shape, BF16, "w_dealt_d2"))
+        hown_raw.append(sbuf([P, PACK, N // 2], F32, "w_hown_b_raw", "w_six_raw"))
+        nc.sync.dma_start(out=hown_raw[1][:], in_=w2[:, N // 2 : N].rearrange("(p j) c -> p j c", j=PACK))
+        hown_dealt = sbuf(dealt_shape, BF16, "w_dealt_hown")
+        w_dealt["hown"] = hown_dealt
+
+        def deal_half(half):
+            nc.scalar.copy(
+                out=hown_dealt[:].rearrange("p t (m e) j -> p m j e t", e=2)[:, P // 4 * half : P // 4 * (half + 1)],
+                in_=hown_raw[half][:].rearrange("p j (m e t) -> p m j e t", e=2, t=PACK),
+            )
+
+        deal_half(0)
+        round_turned("s1", "d2", 64 + 3 * woven_bytes)
+        words_s1 = turn_back("s1", 0)
+        weave_abs("d1", "d2", 64)
+        weave_abs("d2", "d2", 64 - woven_bytes)
+        round_turned("s2", "d2", 64 + 3 * woven_bytes)
+        words_s2 = turn_back("s2", 1)
+        weave_words("s1", words_s1)
+        deal_half(1)
+        weave_words("s2", words_s2)
+
+        quantize_weight("d1", late_codes(N, "w_d1", "s1", 0))
+        quantize_weight("s1", mx_tiles(N, "w_s1"))
         product("d1", quantize_woven(woven["d1"], "d1"))
-        planes["hown"] = sbuf([P, PACK, V], F32, "hown", "d1")
+        quantize_weight("d2", late_codes(N, "w_d2", "d2", 64))
+        product("d2", quantize_woven(woven["d2"], "d2"))
+        planes["hown"] = late_tile([P, PACK, V], F32, "hown", "second", 0)
         for t in range(PACK):
             pick(planes["hown"], "own", t)
-        d2_mx = late_codes(V, "d2", "d2", 2 * woven_bytes)
-        quantize(d2_mx, slice(0, V), flat(woven["d2"]))
-        product("d2", d2_mx)
-        woven["hown"] = late_tile([P, V, PACK], BF16, "woven_hown", "d2", 2 * woven_bytes + turned_bytes)
-        nc.vector.tensor_copy(out=as_woven(woven["hown"][:])[:, HOWN_SCALAR_RUNS:], in_=as_planes(planes["hown"])[:, HOWN_SCALAR_RUNS:])
-        round_weight("hown", sbuf(dealt_shape, BF16, "w_dealt_hown", "w_s1_raw"))
-        nc.scalar.copy(out=as_woven(woven["hown"][:])[:, 0:HOWN_SCALAR_RUNS], in_=as_planes(planes["hown"])[:, 0:HOWN_SCALAR_RUNS])
-        weave_words("s2", words)
-        last_dealt = [late_tile([P, 2, P, PACK], BF16, "w_dealt_s2_%d" % i, "hown", woven_bytes * i) for i in range(2)]
-        deal_planes(nc.scalar.copy, last_dealt[1], w_raw["s2"], 2)
-
         product("s1", quantize_woven(woven["s1"], "s1"))
-        quantize_weight("hown", mx_tiles(N, "w_hown"))
-        hown_mx = quantize_woven(woven["hown"], "hown")
-        product("hown", hown_mx)
+        woven["hown"] = late_tile([P, V, PACK], BF16, "woven_hown", "d2", 64 + 3 * woven_bytes + turned_bytes)
+        nc.vector.tensor_copy(out=as_woven(woven["hown"][:])[:, HOWN_SCALAR_RUNS:], in_=as_planes(planes["hown"])[:, HOWN_SCALAR_RUNS:])
+        nc.scalar.copy(out=as_woven(woven["hown"][:])[:, 0:HOWN_SCALAR_RUNS], in_=as_planes(planes["hown"])[:, 0:HOWN_SCALAR_RUNS])
+        last_dealt = [sbuf([P, 2, P, PACK], BF16, "w_dealt_s2_0", "woven_s1"), late_tile([P, 2, P, PACK], BF16, "w_dealt_s2_1", "d2", 64 - woven_bytes)]
+        deal_planes(nc.scalar.copy, last_dealt[1], w_raw["s2"], 2)
         deal_planes(nc.vector.tensor_copy, last_dealt[0], w_raw["s2"], 0)
-        s2_mx = quantize_woven(woven["s2"], "s2")
-        w_mx["s2"] = quantize_two_planes("s2_0", last_dealt[0]) + quantize_two_planes("s2_1", last_dealt[1])
+        quantize_weight("hown", mx_tiles(N, "w_hown"))
+        product("hown", quantize_woven(woven["hown"], "hown"))
+        s2_mx = late_codes(V, "s2", "second", 0)
+        quantize(s2_mx, slice(0, V), flat(woven["s2"]))
+        w_mx["s2"] = quantize_two_planes(late_codes(2 * P, "w_s2_0", "second", 1024), last_dealt[0]) + quantize_two_planes(mx_tiles(2 * P, "w_s2_1"), last_dealt[1])
         product("s2", s2_mx)
 
         y = sbuf([P, PACK, V], F32, "y")

@@ -29,7 +29,8 @@ LATER_FILL = 36
 LATER_VECTOR = 76
 FIRST_VECTOR = 36
 WEAVE_VECTOR_RUNS = 38
-HOWN_SCALAR_RUNS = 48
+HOWN_SCALAR_RUNS = 32
+LAST_VECTOR = 88
 
 
 def tile_picked_ymeshcnn_relu_po_kernel(tc, x_words, x_scales, w1, w2, w3, w4, w5, w6, offs, own, ea, eb, ec, ed, out_0, out_1, out_2):
@@ -231,10 +232,10 @@ def tile_picked_ymeshcnn_relu_po_kernel(tc, x_words, x_scales, w1, w2, w3, w4, w
         def late_codes(width, name, region, offset):
             return late_tile([P, width], U32, name + "_codes", region, offset), sbuf([P, width], U8, name + "_scales")
 
-        def deal_planes(copy, dealt, raw, first):
+        def deal_planes(copy, dealt, raw, first, m0, m1):
             copy(
-                out=dealt[:].rearrange("p t (m e) j -> p m j e t", e=2),
-                in_=raw[:].rearrange("p j (m e t) -> p m j e t", e=2, t=PACK)[:, :, :, :, first : first + 2],
+                out=dealt[:].rearrange("p t (m e) j -> p m j e t", e=2)[:, m0 // 2 : m1 // 2],
+                in_=raw[:].rearrange("p j (m e t) -> p m j e t", e=2, t=PACK)[:, m0 // 2 : m1 // 2, :, :, first : first + 2],
             )
 
         def turn(name, term, t, start, stop):
@@ -303,6 +304,9 @@ def tile_picked_ymeshcnn_relu_po_kernel(tc, x_words, x_scales, w1, w2, w3, w4, w
         for t in range(PACK):
             pick_minus(planes["d2"], "ed", planes["heb"], t)
             turn("s2", "d2", t, False, t == PACK - 1)
+        planes["hown"] = late_tile([P, PACK, V], F32, "hown", "s1", 2048)
+        for t in range(PACK):
+            pick(planes["hown"], "own", t)
 
         round_weight("s1", sbuf(dealt_shape, BF16, "w_dealt_s1"))
         round_weight("d2", sbuf(dealt_shape, BF16, "w_dealt_d2"))
@@ -318,36 +322,35 @@ def tile_picked_ymeshcnn_relu_po_kernel(tc, x_words, x_scales, w1, w2, w3, w4, w
             )
 
         deal_half(0)
-        round_turned("s1", "d2", 64 + 3 * woven_bytes)
+        round_turned("s1", "d2", 64 + woven_bytes)
         words_s1 = turn_back("s1", 0)
         weave_abs("d1", "d2", 64)
-        weave_abs("d2", "d2", 64 - woven_bytes)
         round_turned("s2", "d2", 64 + 3 * woven_bytes)
         words_s2 = turn_back("s2", 1)
+        weave_abs("d2", "d2", 64 - woven_bytes)
         weave_words("s1", words_s1)
         deal_half(1)
-        weave_words("s2", words_s2)
 
         quantize_weight("d1", late_codes(N, "w_d1", "s1", 0))
-        quantize_weight("s1", mx_tiles(N, "w_s1"))
-        product("d1", quantize_woven(woven["d1"], "d1"))
-        quantize_weight("d2", late_codes(N, "w_d2", "d2", 64))
+        d1_mx = late_codes(V, "d1", "d2", 64 + 3 * woven_bytes)
+        quantize(d1_mx, slice(0, V), flat(woven["d1"]))
+        product("d1", d1_mx)
+        quantize_weight("d2", late_codes(N, "w_d2", "d2", 64 + 3 * woven_bytes + turned_bytes))
         product("d2", quantize_woven(woven["d2"], "d2"))
-        planes["hown"] = late_tile([P, PACK, V], F32, "hown", "second", 0)
-        for t in range(PACK):
-            pick(planes["hown"], "own", t)
+        quantize_weight("s1", late_codes(N, "w_s1", "second", -1024))
         product("s1", quantize_woven(woven["s1"], "s1"))
-        woven["hown"] = late_tile([P, V, PACK], BF16, "woven_hown", "d2", 64 + 3 * woven_bytes + turned_bytes)
+        woven["hown"] = late_tile([P, V, PACK], BF16, "woven_hown", "second", 1024)
         nc.vector.tensor_copy(out=as_woven(woven["hown"][:])[:, HOWN_SCALAR_RUNS:], in_=as_planes(planes["hown"])[:, HOWN_SCALAR_RUNS:])
         nc.scalar.copy(out=as_woven(woven["hown"][:])[:, 0:HOWN_SCALAR_RUNS], in_=as_planes(planes["hown"])[:, 0:HOWN_SCALAR_RUNS])
-        last_dealt = [sbuf([P, 2, P, PACK], BF16, "w_dealt_s2_0", "woven_s1"), late_tile([P, 2, P, PACK], BF16, "w_dealt_s2_1", "d2", 64 - woven_bytes)]
-        deal_planes(nc.scalar.copy, last_dealt[1], w_raw["s2"], 2)
-        deal_planes(nc.vector.tensor_copy, last_dealt[0], w_raw["s2"], 0)
+        weave_words("s2", words_s2)
         quantize_weight("hown", mx_tiles(N, "w_hown"))
         product("hown", quantize_woven(woven["hown"], "hown"))
-        s2_mx = late_codes(V, "s2", "second", 0)
-        quantize(s2_mx, slice(0, V), flat(woven["s2"]))
-        w_mx["s2"] = quantize_two_planes(late_codes(2 * P, "w_s2_0", "second", 1024), last_dealt[0]) + quantize_two_planes(mx_tiles(2 * P, "w_s2_1"), last_dealt[1])
+        last_dealt = [late_tile([P, 2, P, PACK], BF16, "w_dealt_s2_0", "d2", 64), late_tile([P, 2, P, PACK], BF16, "w_dealt_s2_1", "s1", 2048)]
+        deal_planes(nc.scalar.copy, last_dealt[0], w_raw["s2"], 0, 0, P)
+        deal_planes(nc.vector.tensor_copy, last_dealt[1], w_raw["s2"], 2, 0, LAST_VECTOR)
+        deal_planes(nc.scalar.copy, last_dealt[1], w_raw["s2"], 2, LAST_VECTOR, P)
+        s2_mx = quantize_woven(woven["s2"], "s2")
+        w_mx["s2"] = quantize_two_planes(mx_tiles(2 * P, "w_s2_0"), last_dealt[0]) + quantize_two_planes(mx_tiles(2 * P, "w_s2_1"), last_dealt[1])
         product("s2", s2_mx)
 
         y = sbuf([P, PACK, V], F32, "y")

@@ -26,9 +26,9 @@ RUN = 4
 PASS0_VECTOR = 84
 PLANE0_VECTOR = 72
 LATER_FILL = 36
-LATER_VECTOR = 76
-FIRST_VECTOR = 36
-WEAVE_VECTOR_RUNS = 38
+LATER_VECTOR = 96
+FIRST_VECTOR = 28
+WEAVE_VECTOR_RUNS = 46
 HOWN_SCALAR_RUNS = 32
 LAST_VECTOR = 88
 
@@ -96,8 +96,8 @@ def tile_picked_ymeshcnn_relu_po_kernel(tc, x_words, x_scales, w1, w2, w3, w4, w
 
         scales_in = sbuf([P, T], U8, "scales_in")
         nc.gpsimd.memset(scales_in[:].bitcast(I32), 0)
-        lists = {"offs": load_list(offs, "offs")}
         words_in = [load_words(0)]
+        lists = {"offs": load_list(offs, "offs")}
         for q in range(P // QUADRANT):
             nc.sync.dma_start(
                 out=scales_in[QUADRANT * q : QUADRANT * q + 2 * PACK, :].bitcast(I32),
@@ -167,13 +167,6 @@ def tile_picked_ymeshcnn_relu_po_kernel(tc, x_words, x_scales, w1, w2, w3, w4, w
         deal_later(nc.vector.tensor_copy, 0, LATER_FILL)
         deal_later(nc.vector.tensor_copy, LATER_FILL, LATER_VECTOR)
         deal_later(nc.scalar.copy, LATER_VECTOR, P)
-        for t in range(1, PACK):
-            mx = mx_tiles(P, "w1_1%d" % t)
-            quantize(mx, slice(0, P), later_planes[:, t - 1].rearrange("p m j -> p (m j)"))
-            first_product(1, t, mx, slice(0, P))
-        h = [keep.tile([P, S], F32, name="h%d" % t) for t in range(PACK)]
-        nc.vector.tensor_scalar_max(h[0][:, 0 : S // 2], h_banks[0][:], 0.0)
-        nc.scalar.activation(h[0][:, S // 2 : S], h_banks[1][:], ACT.Relu)
         first_dealt = sbuf([P, PACK, P, PACK], BF16, "w_dealt_d1")
 
         def deal_first(copy, half, m0, m1):
@@ -183,10 +176,21 @@ def tile_picked_ymeshcnn_relu_po_kernel(tc, x_words, x_scales, w1, w2, w3, w4, w
             )
 
         deal_first(nc.vector.tensor_copy, 0, 0, FIRST_VECTOR)
+        h = [keep.tile([P, S], F32, name="h%d" % t) for t in range(PACK)]
+        nc.vector.tensor_scalar_max(h[0][:, 0 : S // 2], h_banks[0][:], 0.0)
+        nc.scalar.activation(h[0][:, S // 2 : S], h_banks[1][:], ACT.Relu)
+        for t in range(1, PACK):
+            mx = mx_tiles(P, "w1_1%d" % t)
+            quantize(mx, slice(0, P), later_planes[:, t - 1].rearrange("p m j -> p (m j)"))
+            first_product(1, t, mx, slice(0, P))
         deal_first(nc.scalar.copy, 0, FIRST_VECTOR, P // 2)
         for bank, (t, edges) in zip(h_banks[2:], pieces[2:]):
             nc.scalar.activation(h[t][:, edges], bank[:], ACT.Relu)
-        deal_first(nc.scalar.copy, 1, 0, P // 2)
+        for first in (0, 2):
+            nc.scalar.copy(
+                out=first_dealt[:].rearrange("p t (m e) j -> p m j e t", e=2)[:, P // 4 : P // 2, :, :, first : first + 2],
+                in_=first_raw[:, 1].rearrange("p j (m e t) -> p m j e t", e=2, t=PACK)[:, :, :, :, first : first + 2],
+            )
 
         w_dealt = {"d1": first_dealt}
         w_mx = {}
@@ -271,7 +275,8 @@ def tile_picked_ymeshcnn_relu_po_kernel(tc, x_words, x_scales, w1, w2, w3, w4, w
 
         def round_weight(name, dealt):
             w_dealt[name] = dealt
-            deal(nc.scalar.copy, dealt, w_raw[name], 0, P)
+            for first in (0, 2):
+                deal_planes(nc.scalar.copy, dealt[:, first : first + 2], w_raw[name], first, 0, P)
 
         woven_bytes = 2 * V * PACK
         turned_bytes = 2 * H
@@ -316,10 +321,11 @@ def tile_picked_ymeshcnn_relu_po_kernel(tc, x_words, x_scales, w1, w2, w3, w4, w
         w_dealt["hown"] = hown_dealt
 
         def deal_half(half):
-            nc.scalar.copy(
-                out=hown_dealt[:].rearrange("p t (m e) j -> p m j e t", e=2)[:, P // 4 * half : P // 4 * (half + 1)],
-                in_=hown_raw[half][:].rearrange("p j (m e t) -> p m j e t", e=2, t=PACK),
-            )
+            for first in (0, 2):
+                nc.scalar.copy(
+                    out=hown_dealt[:].rearrange("p t (m e) j -> p m j e t", e=2)[:, P // 4 * half : P // 4 * (half + 1), :, :, first : first + 2],
+                    in_=hown_raw[half][:].rearrange("p j (m e t) -> p m j e t", e=2, t=PACK)[:, :, :, :, first : first + 2],
+                )
 
         deal_half(0)
         round_turned("s1", "d2", 64 + woven_bytes)
@@ -356,8 +362,8 @@ def tile_picked_ymeshcnn_relu_po_kernel(tc, x_words, x_scales, w1, w2, w3, w4, w
         y = sbuf([P, PACK, V], F32, "y")
         out_planes = out_0.rearrange("(p t) v -> p t v", t=PACK)
         for t in range(0, PACK, 2):
-            nc.scalar.copy(out=y[:, t, :], in_=y_banks[t][:])
-            nc.vector.tensor_copy(out=y[:, t + 1, :], in_=y_banks[t + 1][:])
+            nc.vector.tensor_copy(out=y[:, t, :], in_=y_banks[t][:])
+            nc.scalar.copy(out=y[:, t + 1, :], in_=y_banks[t + 1][:])
             nc.sync.dma_start(out=out_planes[:, t : t + 2, :], in_=y[:, t : t + 2, :])
         y_woven = sbuf([P, V, PACK], BF16, "woven_y")
         half = V // RUN // 2

@@ -24,13 +24,11 @@ BANKS = 8
 RUN = 4
 
 PASS0_VECTOR = 84
-PLANE0_VECTOR = 72
-LATER_FILL = 36
-LATER_VECTOR = 96
-FIRST_VECTOR = 28
+PAIR0_VECTOR = 84
+PAIR1_VECTOR = 96
 WEAVE_VECTOR_RUNS = 46
-HOWN_SCALAR_RUNS = 32
-LAST_VECTOR = 88
+HOWN_SCALAR_RUNS = 26
+LAST_VECTOR = 104
 
 
 def tile_picked_ymeshcnn_relu_po_kernel(tc, x_words, x_scales, w1, w2, w3, w4, w5, w6, offs, own, ea, eb, ec, ed, out_0, out_1, out_2):
@@ -67,10 +65,10 @@ def tile_picked_ymeshcnn_relu_po_kernel(tc, x_words, x_scales, w1, w2, w3, w4, w
             nc.sync.dma_start(out=raw[:], in_=rows.rearrange("(p j) c -> p j c", j=PACK))
             return raw
 
-        def deal(copy, dealt, raw, m0, m1):
+        def deal_planes(copy, dealt, raw, first, m0, m1):
             copy(
                 out=dealt[:].rearrange("p t (m e) j -> p m j e t", e=2)[:, m0 // 2 : m1 // 2],
-                in_=raw[:].rearrange("p j (m e t) -> p m j e t", e=2, t=PACK)[:, m0 // 2 : m1 // 2],
+                in_=raw[:].rearrange("p j (m e t) -> p m j e t", e=2, t=PACK)[:, m0 // 2 : m1 // 2, :, :, first : first + 2],
             )
 
         def mx_tiles(width, name, tag=None):
@@ -140,8 +138,9 @@ def tile_picked_ymeshcnn_relu_po_kernel(tc, x_words, x_scales, w1, w2, w3, w4, w
         nc.vector.tensor_copy(picked_words[0][:], words_in[0][:].bitcast(U32).indirect(lists["offs"][:]))
         nc.vector.tensor_copy(picked_scales[:], scales_in[:].indirect(lists["offs"][:]))
         w1_dealt0 = sbuf([P, PACK, P, PACK], BF16, "w1_dealt0")
-        deal(nc.vector.tensor_copy, w1_dealt0, w1_raw[0], 0, PASS0_VECTOR)
-        deal(nc.scalar.copy, w1_dealt0, w1_raw[0], PASS0_VECTOR, P)
+        for first in (0, 2):
+            deal_planes(nc.vector.tensor_copy, w1_dealt0[:, first : first + 2], w1_raw[0], first, 0, PASS0_VECTOR)
+            deal_planes(nc.scalar.copy, w1_dealt0[:, first : first + 2], w1_raw[0], first, PASS0_VECTOR, P)
         for u in range(2):
             mx = mx_tiles(2 * P, "w1_0%d" % u)
             quantize(mx, slice(0, 2 * P), w1_dealt0[:, 2 * u : 2 * u + 2].rearrange("p t m j -> p (t m j)"))
@@ -149,48 +148,38 @@ def tile_picked_ymeshcnn_relu_po_kernel(tc, x_words, x_scales, w1, w2, w3, w4, w
                 first_product(0, 2 * u + e, mx, plane_cols(e))
         picked_words.append(sbuf([P, S], U32, "picked_words1", "w1_dealt0"))
         nc.vector.tensor_copy(picked_words[1][:], words_in[1][:].bitcast(U32).indirect(lists["offs"][:]))
-        first_plane = sbuf([P, P, PACK], BF16, "w1_first_plane")
-        raw_columns = w1_raw[1][:].rearrange("p j (m t) -> p t m j", t=PACK)
-        nc.vector.tensor_copy(out=first_plane[:, 0:PLANE0_VECTOR], in_=raw_columns[:, 0, 0:PLANE0_VECTOR])
-        nc.scalar.copy(out=first_plane[:, PLANE0_VECTOR:P], in_=raw_columns[:, 0, PLANE0_VECTOR:P])
-        later_planes = sbuf([P, PACK - 1, P, PACK], BF16, "w1_later_planes")
+        pairs = [sbuf([P, 2, P, PACK], BF16, "w1_pair%d" % u) for u in range(2)]
 
-        def deal_later(copy, m0, m1):
-            copy(
-                out=later_planes[:].rearrange("p t (m e) j -> p m j e t", e=2)[:, m0 // 2 : m1 // 2],
-                in_=w1_raw[1][:].rearrange("p j (m e t) -> p m j e t", e=2, t=PACK)[:, m0 // 2 : m1 // 2, :, :, 1:PACK],
-            )
+        def second_pass(t):
+            mx = mx_tiles(P, "w1_1%d" % t)
+            quantize(mx, slice(0, P), pairs[t // 2][:, t % 2].rearrange("p m j -> p (m j)"))
+            first_product(1, t, mx, slice(0, P))
 
-        mx = mx_tiles(P, "w1_10")
-        quantize(mx, slice(0, P), flat(first_plane))
-        first_product(1, 0, mx, slice(0, P))
-        deal_later(nc.vector.tensor_copy, 0, LATER_FILL)
-        deal_later(nc.vector.tensor_copy, LATER_FILL, LATER_VECTOR)
-        deal_later(nc.scalar.copy, LATER_VECTOR, P)
+        deal_planes(nc.vector.tensor_copy, pairs[0], w1_raw[1], 0, 0, PAIR0_VECTOR)
+        deal_planes(nc.scalar.copy, pairs[0], w1_raw[1], 0, PAIR0_VECTOR, P)
+        second_pass(0)
+        second_pass(1)
+        deal_planes(nc.vector.tensor_copy, pairs[1], w1_raw[1], 2, 0, PAIR1_VECTOR)
+        deal_planes(nc.scalar.copy, pairs[1], w1_raw[1], 2, PAIR1_VECTOR, P)
         first_dealt = sbuf([P, PACK, P, PACK], BF16, "w_dealt_d1")
 
-        def deal_first(copy, half, m0, m1):
+        def deal_first(copy, half, first, m0, m1):
             copy(
-                out=first_dealt[:].rearrange("p t (m e) j -> p m j e t", e=2)[:, P // 4 * half + m0 // 2 : P // 4 * half + m1 // 2],
-                in_=first_raw[:, half].rearrange("p j (m e t) -> p m j e t", e=2, t=PACK)[:, m0 // 2 : m1 // 2],
+                out=first_dealt[:].rearrange("p t (m e) j -> p m j e t", e=2)[:, P // 4 * half + m0 // 2 : P // 4 * half + m1 // 2, :, :, first : first + 2],
+                in_=first_raw[:, half].rearrange("p j (m e t) -> p m j e t", e=2, t=PACK)[:, m0 // 2 : m1 // 2, :, :, first : first + 2],
             )
 
-        deal_first(nc.vector.tensor_copy, 0, 0, FIRST_VECTOR)
+        deal_first(nc.vector.tensor_copy, 0, 0, 0, P // 2)
         h = [keep.tile([P, S], F32, name="h%d" % t) for t in range(PACK)]
         nc.vector.tensor_scalar_max(h[0][:, 0 : S // 2], h_banks[0][:], 0.0)
         nc.scalar.activation(h[0][:, S // 2 : S], h_banks[1][:], ACT.Relu)
-        for t in range(1, PACK):
-            mx = mx_tiles(P, "w1_1%d" % t)
-            quantize(mx, slice(0, P), later_planes[:, t - 1].rearrange("p m j -> p (m j)"))
-            first_product(1, t, mx, slice(0, P))
-        deal_first(nc.scalar.copy, 0, FIRST_VECTOR, P // 2)
+        second_pass(2)
+        second_pass(3)
+        deal_first(nc.scalar.copy, 0, 2, 0, P // 2)
         for bank, (t, edges) in zip(h_banks[2:], pieces[2:]):
             nc.scalar.activation(h[t][:, edges], bank[:], ACT.Relu)
         for first in (0, 2):
-            nc.scalar.copy(
-                out=first_dealt[:].rearrange("p t (m e) j -> p m j e t", e=2)[:, P // 4 : P // 2, :, :, first : first + 2],
-                in_=first_raw[:, 1].rearrange("p j (m e t) -> p m j e t", e=2, t=PACK)[:, :, :, :, first : first + 2],
-            )
+            deal_first(nc.scalar.copy, 1, first, 0, P // 2)
 
         w_dealt = {"d1": first_dealt}
         w_mx = {}
@@ -235,12 +224,6 @@ def tile_picked_ymeshcnn_relu_po_kernel(tc, x_words, x_scales, w1, w2, w3, w4, w
 
         def late_codes(width, name, region, offset):
             return late_tile([P, width], U32, name + "_codes", region, offset), sbuf([P, width], U8, name + "_scales")
-
-        def deal_planes(copy, dealt, raw, first, m0, m1):
-            copy(
-                out=dealt[:].rearrange("p t (m e) j -> p m j e t", e=2)[:, m0 // 2 : m1 // 2],
-                in_=raw[:].rearrange("p j (m e t) -> p m j e t", e=2, t=PACK)[:, m0 // 2 : m1 // 2, :, :, first : first + 2],
-            )
 
         def turn(name, term, t, start, stop):
             for half in range(V // P):

@@ -1,7 +1,6 @@
 from contextlib import ExitStack
 
 import concourse.mybir as mybir
-from concourse.masks import make_identity
 
 K, T, S, H, N, V = 1024, 1024, 512, 512, 512, 256
 FLOPS = 2 * K * H * S + 5 * 2 * H * N * V
@@ -20,15 +19,12 @@ P = 128
 PACK = 4
 K_PASS = P * PACK
 QUADRANT = 32
-BANKS = 8
 RUN = 4
 
 PASS0_VECTOR = 84
 PAIR0_VECTOR = 84
 PAIR1_VECTOR = 96
 WEAVE_VECTOR_RUNS = 46
-HOWN_SCALAR_RUNS = 26
-LAST_VECTOR = 104
 
 
 def tile_picked_ymeshcnn_relu_po_kernel(tc, x_words, x_scales, w1, w2, w3, w4, w5, w6, offs, own, ea, eb, ec, ed, out_0, out_1, out_2):
@@ -37,15 +33,13 @@ def tile_picked_ymeshcnn_relu_po_kernel(tc, x_words, x_scales, w1, w2, w3, w4, w
         keep = ctx.enter_context(tc.tile_pool(name="keep", bufs=1))
         late = ctx.enter_context(tc.tile_pool(name="late", bufs=1))
         psum = ctx.enter_context(tc.psum_pool(name="psum", bufs=1))
+        woven_bytes = 2 * V * PACK
+        places = {"w_s2_raw": 0, "woven_s1": 0, "woven_e1": woven_bytes, "woven_s2": 2 * woven_bytes, "woven_e2": 3 * woven_bytes, "w_dealt_s2": 4 * woven_bytes, "woven_hown": 4 * woven_bytes}
 
         def sbuf(shape, dtype, name, tag=None):
+            if name in places:
+                return late.tile(shape, dtype, name=name, align_bytes=64, offset=places[name])
             return keep.tile(shape, dtype, name=name, tag=tag or name, align_bytes=64)
-
-        raw_bytes = 4 * PACK * N
-        regions = {"w_d1": 0, "w_s1": raw_bytes, "w_d2": 3 * raw_bytes, "w_first": 5 * raw_bytes, "w_second": 2 * raw_bytes - 64}
-
-        def late_tile(shape, dtype, name, region, offset):
-            return late.tile(shape, dtype, name=name, align_bytes=64, offset=regions["w_" + region] + offset)
 
         def load_list(ap, name):
             tile = keep.tile(list(ap.shape), U16, name=name)
@@ -58,21 +52,18 @@ def tile_picked_ymeshcnn_relu_po_kernel(tc, x_words, x_scales, w1, w2, w3, w4, w
             return tile
 
         def load_weight(rows, name):
-            if name in regions:
-                raw = late.tile([P, PACK, N], F32, name=name + "_raw", align_bytes=64, offset=regions[name])[:, :, 0 : rows.shape[1]]
-            else:
-                raw = sbuf([P, PACK, rows.shape[1]], F32, name + "_raw")
+            raw = sbuf([P, PACK, rows.shape[1]], F32, name + "_raw")
             nc.sync.dma_start(out=raw[:], in_=rows.rearrange("(p j) c -> p j c", j=PACK))
             return raw
 
-        def deal_planes(copy, dealt, raw, first, m0, m1):
+        def deal(copy, dealt, raw, first, m0, m1, at=0):
             copy(
-                out=dealt[:].rearrange("p t (m e) j -> p m j e t", e=2)[:, m0 // 2 : m1 // 2],
+                out=dealt.rearrange("p t (m e) j -> p m j e t", e=2)[:, (at + m0) // 2 : (at + m1) // 2],
                 in_=raw[:].rearrange("p j (m e t) -> p m j e t", e=2, t=PACK)[:, m0 // 2 : m1 // 2, :, :, first : first + 2],
             )
 
-        def mx_tiles(width, name, tag=None):
-            return sbuf([P, width], U32, name + "_codes", tag), sbuf([P, width], U8, name + "_scales")
+        def mx_tiles(width, name):
+            return sbuf([P, width], U32, name + "_codes"), sbuf([P, width], U8, name + "_scales")
 
         def quantize(mx, cols, values):
             nc.vector.quantize_mx(out=mx[0][:, cols].bitcast(FP8X4), scales=mx[1][:, cols], in_=values)
@@ -80,14 +71,11 @@ def tile_picked_ymeshcnn_relu_po_kernel(tc, x_words, x_scales, w1, w2, w3, w4, w
         def plane_cols(t):
             return slice(P * t, P * (t + 1))
 
-        def quantize_plane(mx, dealt, t):
-            quantize(mx, plane_cols(t), dealt[:, t].rearrange("p m j -> p (m j)"))
+        def as_woven(tile, run=RUN):
+            return tile[:].rearrange("p (c i) t -> p c t i", i=run)
 
-        def as_woven(ap):
-            return ap.rearrange("p (c i) t -> p c t i", i=RUN)
-
-        def as_planes(tile):
-            return tile[:].rearrange("p t (c i) -> p c t i", i=RUN)
+        def as_planes(tile, run=RUN):
+            return tile[:].rearrange("p t (c i) -> p c t i", i=run)
 
         def flat(tile):
             return tile[:].rearrange("p a b -> p (a b)")
@@ -104,18 +92,16 @@ def tile_picked_ymeshcnn_relu_po_kernel(tc, x_words, x_scales, w1, w2, w3, w4, w
         w1_raw = [load_weight(w1[0:K_PASS, :], "w1_pass0")]
         words_in.append(load_words(1))
         w1_raw.append(load_weight(w1[K_PASS:K, :], "w1_pass1"))
-        first_raw = late.tile([P, 2, PACK, N // 2], F32, name="w_d1_raw", align_bytes=64, offset=regions["w_d1"])
-        first_rows = w4.rearrange("(p j) c -> p j c", j=PACK)
-        nc.sync.dma_start(out=first_raw[:, 0], in_=first_rows[:, :, 0 : N // 2])
-        for name, ap in (("ea", ea), ("eb", eb), ("ec", ec)):
+        first_raw = [load_weight(w3[:, 0 : N // 2], "w_s1_0")]
+        for name, ap in (("ea", ea), ("ec", ec)):
             lists[name] = load_list(ap, name)
-        nc.sync.dma_start(out=first_raw[:, 1], in_=first_rows[:, :, N // 2 : N])
-        for name, ap in (("ed", ed), ("own", own)):
+        first_raw.append(load_weight(w3[:, N // 2 : N], "w_s1_1"))
+        for name, ap in (("eb", eb), ("ed", ed), ("own", own)):
             lists[name] = load_list(ap, name)
-        operands = ("d1", "d2", "s1", "hown", "s2")
-        w_raw = {"s1": load_weight(w3, "w_s1"), "d2": load_weight(w6, "w_six")}
-        hown_raw = [load_weight(w2[:, 0 : N // 2], "w_d2")]
-        w_raw["s2"] = load_weight(w5, "w_s2")
+        operands = ("s1", "d1", "s2", "d2", "hown")
+        w_raw = {}
+        for name, w in (("d1", w4), ("s2", w5), ("d2", w6), ("hown", w2)):
+            w_raw[name] = load_weight(w, "w_" + name)
 
         pieces = [(0, slice(0, S // 2)), (0, slice(S // 2, S))] + [(t, slice(0, S)) for t in range(1, PACK)]
         h_banks = [psum.tile([P, edges.stop - edges.start], F32, name="h_bank%d" % i, tag="bank%d" % i) for i, (t, edges) in enumerate(pieces)]
@@ -139,8 +125,8 @@ def tile_picked_ymeshcnn_relu_po_kernel(tc, x_words, x_scales, w1, w2, w3, w4, w
         nc.vector.tensor_copy(picked_scales[:], scales_in[:].indirect(lists["offs"][:]))
         w1_dealt0 = sbuf([P, PACK, P, PACK], BF16, "w1_dealt0")
         for first in (0, 2):
-            deal_planes(nc.vector.tensor_copy, w1_dealt0[:, first : first + 2], w1_raw[0], first, 0, PASS0_VECTOR)
-            deal_planes(nc.scalar.copy, w1_dealt0[:, first : first + 2], w1_raw[0], first, PASS0_VECTOR, P)
+            deal(nc.vector.tensor_copy, w1_dealt0[:, first : first + 2], w1_raw[0], first, 0, PASS0_VECTOR)
+            deal(nc.scalar.copy, w1_dealt0[:, first : first + 2], w1_raw[0], first, PASS0_VECTOR, P)
         for u in range(2):
             mx = mx_tiles(2 * P, "w1_0%d" % u)
             quantize(mx, slice(0, 2 * P), w1_dealt0[:, 2 * u : 2 * u + 2].rearrange("p t m j -> p (t m j)"))
@@ -155,204 +141,147 @@ def tile_picked_ymeshcnn_relu_po_kernel(tc, x_words, x_scales, w1, w2, w3, w4, w
             quantize(mx, slice(0, P), pairs[t // 2][:, t % 2].rearrange("p m j -> p (m j)"))
             first_product(1, t, mx, slice(0, P))
 
-        deal_planes(nc.vector.tensor_copy, pairs[0], w1_raw[1], 0, 0, PAIR0_VECTOR)
-        deal_planes(nc.scalar.copy, pairs[0], w1_raw[1], 0, PAIR0_VECTOR, P)
+        deal(nc.vector.tensor_copy, pairs[0][:], w1_raw[1], 0, 0, PAIR0_VECTOR)
+        deal(nc.scalar.copy, pairs[0][:], w1_raw[1], 0, PAIR0_VECTOR, P)
         second_pass(0)
         second_pass(1)
-        deal_planes(nc.vector.tensor_copy, pairs[1], w1_raw[1], 2, 0, PAIR1_VECTOR)
-        deal_planes(nc.scalar.copy, pairs[1], w1_raw[1], 2, PAIR1_VECTOR, P)
-        first_dealt = sbuf([P, PACK, P, PACK], BF16, "w_dealt_d1")
+        deal(nc.vector.tensor_copy, pairs[1][:], w1_raw[1], 2, 0, PAIR1_VECTOR)
+        deal(nc.scalar.copy, pairs[1][:], w1_raw[1], 2, PAIR1_VECTOR, P)
 
-        def deal_first(copy, half, first, m0, m1):
-            copy(
-                out=first_dealt[:].rearrange("p t (m e) j -> p m j e t", e=2)[:, P // 4 * half + m0 // 2 : P // 4 * half + m1 // 2, :, :, first : first + 2],
-                in_=first_raw[:, half].rearrange("p j (m e t) -> p m j e t", e=2, t=PACK)[:, m0 // 2 : m1 // 2, :, :, first : first + 2],
-            )
+        dealt_shape = [P, PACK, P, PACK]
+        w_dealt = {"s1": sbuf(dealt_shape, BF16, "w_dealt_s1")}
 
-        deal_first(nc.vector.tensor_copy, 0, 0, 0, P // 2)
+        def round_first(half, first):
+            deal(nc.vector.tensor_copy, w_dealt["s1"][:, first : first + 2], first_raw[half], first, 0, P // 2, P // 2 * half)
+
         h = [keep.tile([P, S], F32, name="h%d" % t) for t in range(PACK)]
+        round_first(0, 0)
         nc.vector.tensor_scalar_max(h[0][:, 0 : S // 2], h_banks[0][:], 0.0)
         nc.scalar.activation(h[0][:, S // 2 : S], h_banks[1][:], ACT.Relu)
         second_pass(2)
         second_pass(3)
-        deal_first(nc.scalar.copy, 0, 2, 0, P // 2)
-        for bank, (t, edges) in zip(h_banks[2:], pieces[2:]):
-            nc.scalar.activation(h[t][:, edges], bank[:], ACT.Relu)
-        for first in (0, 2):
-            deal_first(nc.scalar.copy, 1, first, 0, P // 2)
 
-        w_dealt = {"d1": first_dealt}
+        planes = {}
+        woven = {}
         w_mx = {}
+        mx_of = {}
         y_banks = {}
-        identity = sbuf([P, P], F32, "identity")
-        make_identity(nc, identity[:])
 
-        def pick(planes, list_name, t):
-            nc.vector.tensor_copy(planes[:, t, :], h[t][:].indirect(lists[list_name][:]))
+        def pick(name, list_name, t):
+            nc.scalar.activation(planes[name][:, t, :], h[t][:].indirect(lists[list_name][:]), ACT.Copy)
 
-        def pick_minus(planes, list_name, first, t):
-            nc.vector.tensor_tensor(planes[:, t, :], h[t][:].indirect(lists[list_name][:]), first[:, t, :], ALU.subtract)
+        def empty_h(t):
+            nc.vector.tensor_scalar_max(h[t][:], h_banks[1 + t][:], 0.0)
 
-        def quantize_woven(woven, name):
-            mx = mx_tiles(V, name)
-            quantize(mx, slice(0, V), flat(woven))
-            return mx
+        def round_weight(copy, name):
+            w_dealt[name] = sbuf(dealt_shape, BF16, "w_dealt_" + name)
+            for first in (0, 2):
+                deal(copy, w_dealt[name][:, first : first + 2], w_raw[name], first, 0, P)
 
-        def product(name, mx):
-            for t in range(PACK):
-                if name == operands[0]:
-                    y_banks[t] = psum.tile([P, V], F32, name="y_bank%d" % t, tag="bank%d" % (1 + t))
-                codes, scales, cols = w_mx[name][t]
-                nc.tensor.matmul_mx(
-                    out=y_banks[t][:],
-                    lhsT=codes[:, cols].bitcast(FP8X4),
-                    lhsT_scale=scales[:, cols],
-                    rhs=mx[0][:].bitcast(FP8X4),
-                    rhs_scale=mx[1][:],
-                    start=(name == operands[0]),
-                    stop=(name == operands[-1]),
-                )
-
-        def quantize_weight(name, mx):
+        def quantize_weight(name):
+            mx = mx_tiles(N, "w_" + name)
             quantize(mx, slice(0, N), w_dealt[name][:].rearrange("p t m j -> p (t m j)"))
             w_mx[name] = [mx + (plane_cols(t),) for t in range(PACK)]
 
-        def quantize_two_planes(mx, dealt):
-            for t in range(2):
-                quantize_plane(mx, dealt, t)
-            return [mx + (plane_cols(t),) for t in range(2)]
-
-        def late_codes(width, name, region, offset):
-            return late_tile([P, width], U32, name + "_codes", region, offset), sbuf([P, width], U8, name + "_scales")
-
-        def turn(name, term, t, start, stop):
-            for half in range(V // P):
-                nc.tensor.matmul(
-                    turned_banks[name, half][:, t, :],
-                    planes[term][:, t, P * half : P * (half + 1)],
-                    identity[:],
-                    start=start,
-                    stop=stop,
-                    is_transpose=True,
-                )
-
-        def round_turned(name, region, offset):
-            for half in range(V // P):
-                turned[name, half] = late_tile([P, 2, P, 2], BF16, "turned_sb_%s%d" % (name, half), region, offset + turned_bytes * half)
-                nc.scalar.activation(turned[name, half][:], turned_banks[name, half][:].rearrange("v (u e) p -> v u p e", e=2), ACT.Copy)
-
-        def turn_back(name, slot):
-            words = psum.tile([P, 2, V], F32, name="words_" + name, tag="bank%d" % (len(pieces) + slot))
-            for half in range(V // P):
-                for u in range(2):
-                    nc.tensor.transpose(words[:, u, P * half : P * (half + 1)], turned[name, half][:, u].rearrange("v p e -> v (p e)").bitcast(F32), identity[:])
-            return words
-
-        def weave_words(name, words):
+        def combine(name, x, y, op):
             woven[name] = sbuf([P, V, PACK], BF16, "woven_" + name)
-            nc.scalar.copy(out=woven[name][:].bitcast(F32), in_=words[:].rearrange("p u v -> p v u"))
+            nc.vector.tensor_tensor(as_woven(woven[name], 2), as_planes(planes[x], 2), as_planes(planes[y], 2), op)
 
-        def weave_abs(name, region, offset):
-            woven[name] = late_tile([P, V, PACK], BF16, "woven_" + name, region, offset)
-            nc.scalar.activation(as_woven(woven[name][:]), as_planes(planes[name]), ACT.Abs)
+        def absolute(name, signed):
+            woven[name] = sbuf([P, V, PACK], BF16, "woven_" + name)
+            nc.vector.scalar_tensor_tensor(flat(woven[name]), flat(woven[signed]), -1.0, flat(woven[signed]), ALU.mult, ALU.max)
 
-        def round_weight(name, dealt):
-            w_dealt[name] = dealt
-            for first in (0, 2):
-                deal_planes(nc.scalar.copy, dealt[:, first : first + 2], w_raw[name], first, 0, P)
+        def quantize_operand(name):
+            mx_of[name] = mx_tiles(V, name)
+            quantize(mx_of[name], slice(0, V), flat(woven[name]))
 
-        woven_bytes = 2 * V * PACK
-        turned_bytes = 2 * H
-        dealt_shape = [P, PACK, P, PACK]
-        woven = {}
-        turned = {}
-        turned_banks = {}
-        for i, name in enumerate(("s1", "s2")):
-            for half in range(V // P):
-                turned_banks[name, half] = psum.tile([P, PACK, P], F32, name="turned_%s%d" % (name, half), tag="bank%d" % ((len(pieces) + 2 * i + half) % BANKS))
+        def product(name, t):
+            if name == operands[0]:
+                y_banks[t] = psum.tile([P, V], F32, name="y_bank%d" % t, tag="bank%d" % ((5 + t) % 8))
+            codes, scales, cols = w_mx[name][t]
+            nc.tensor.matmul_mx(
+                out=y_banks[t][:],
+                lhsT=codes[:, cols].bitcast(FP8X4),
+                lhsT_scale=scales[:, cols],
+                rhs=mx_of[name][0][:].bitcast(FP8X4),
+                rhs_scale=mx_of[name][1][:],
+                start=(name == operands[0]),
+                stop=(name == operands[-1]),
+            )
 
-        planes = {}
+        def products(name):
+            for t in range(PACK):
+                product(name, t)
 
-        planes["hea"] = sbuf([P, PACK, V], F32, "hea")
-        planes["heb"] = sbuf([P, PACK, V], F32, "heb")
-        planes["d1"] = late_tile([P, PACK, V], F32, "d1", "first", 0)
+        for name in ("hea", "hec", "heb", "hed"):
+            planes[name] = sbuf([P, PACK, V], F32, name)
+        planes["hown"] = sbuf([P, PACK, V], BF16, "hown")
+
+        pick("hea", "ea", 0)
+        pick("hec", "ec", 0)
+        empty_h(1)
+        round_first(0, 2)
+        round_first(1, 0)
+        pick("hea", "ea", 1)
+        pick("hec", "ec", 1)
+        empty_h(2)
+        round_first(1, 2)
+        pick("hea", "ea", 2)
+        pick("hec", "ec", 2)
+        quantize_weight("s1")
+        nc.scalar.activation(h[3][:], h_banks[4][:], ACT.Relu)
+        pick("hea", "ea", 3)
+        pick("hec", "ec", 3)
         for t in range(PACK):
-            pick(planes["hea"], "ea", t)
-            pick(planes["heb"], "eb", t)
-            pick_minus(planes["d1"], "ec", planes["hea"], t)
-            turn("s1", "hea", t, t == 0, False)
-            turn("s1", "hea", t, False, False)
-            if t > 0:
-                turn("s2", "heb", t - 1, t == 1, False)
-                turn("s2", "heb", t - 1, False, False)
-            turn("s1", "d1", t, False, t == PACK - 1)
-        turn("s2", "heb", PACK - 1, False, False)
-        turn("s2", "heb", PACK - 1, False, False)
-        planes["d2"] = late_tile([P, PACK, V], F32, "d2", "second", 0)
+            pick("heb", "eb", t)
+            pick("hed", "ed", t)
         for t in range(PACK):
-            pick_minus(planes["d2"], "ed", planes["heb"], t)
-            turn("s2", "d2", t, False, t == PACK - 1)
-        planes["hown"] = late_tile([P, PACK, V], F32, "hown", "s1", 2048)
+            pick("hown", "own", t)
+
+        round_weight(nc.vector.tensor_copy, "d1")
+        quantize_weight("d1")
+        round_weight(nc.vector.tensor_copy, "s2")
+        quantize_weight("s2")
+        combine("s1", "hea", "hec", ALU.add)
+        combine("e1", "hea", "hec", ALU.subtract)
+        quantize_operand("s1")
+        products("s1")
+        absolute("d1", "e1")
+        round_weight(nc.vector.tensor_copy, "d2")
+        quantize_operand("d1")
+        products("d1")
+        quantize_weight("d2")
+        combine("s2", "heb", "hed", ALU.add)
+        combine("e2", "heb", "hed", ALU.subtract)
+        quantize_operand("s2")
+        products("s2")
+        absolute("d2", "e2")
+        woven["hown"] = sbuf([P, V, PACK], BF16, "woven_hown")
+        nc.vector.tensor_copy(out=as_woven(woven["hown"]), in_=as_planes(planes["hown"]))
+        quantize_operand("d2")
+        products("d2")
+        quantize_operand("hown")
+        last_dealt = [sbuf([P, 2, P, PACK], BF16, "w_dealt_last%d" % u) for u in range(2)]
+        for u in range(2):
+            deal(nc.scalar.copy, last_dealt[u][:], w_raw["hown"], 2 * u, 0, P)
+        w_mx["hown"] = {}
         for t in range(PACK):
-            pick(planes["hown"], "own", t)
-
-        round_weight("s1", sbuf(dealt_shape, BF16, "w_dealt_s1"))
-        round_weight("d2", sbuf(dealt_shape, BF16, "w_dealt_d2"))
-        hown_raw.append(sbuf([P, PACK, N // 2], F32, "w_hown_b_raw", "w_six_raw"))
-        nc.sync.dma_start(out=hown_raw[1][:], in_=w2[:, N // 2 : N].rearrange("(p j) c -> p j c", j=PACK))
-        hown_dealt = sbuf(dealt_shape, BF16, "w_dealt_hown")
-        w_dealt["hown"] = hown_dealt
-
-        def deal_half(half):
-            for first in (0, 2):
-                nc.scalar.copy(
-                    out=hown_dealt[:].rearrange("p t (m e) j -> p m j e t", e=2)[:, P // 4 * half : P // 4 * (half + 1), :, :, first : first + 2],
-                    in_=hown_raw[half][:].rearrange("p j (m e t) -> p m j e t", e=2, t=PACK)[:, :, :, :, first : first + 2],
-                )
-
-        deal_half(0)
-        round_turned("s1", "d2", 64 + woven_bytes)
-        words_s1 = turn_back("s1", 0)
-        weave_abs("d1", "d2", 64)
-        round_turned("s2", "d2", 64 + 3 * woven_bytes)
-        words_s2 = turn_back("s2", 1)
-        weave_abs("d2", "d2", 64 - woven_bytes)
-        weave_words("s1", words_s1)
-        deal_half(1)
-
-        quantize_weight("d1", late_codes(N, "w_d1", "s1", 0))
-        d1_mx = late_codes(V, "d1", "d2", 64 + 3 * woven_bytes)
-        quantize(d1_mx, slice(0, V), flat(woven["d1"]))
-        product("d1", d1_mx)
-        quantize_weight("d2", late_codes(N, "w_d2", "d2", 64 + 3 * woven_bytes + turned_bytes))
-        product("d2", quantize_woven(woven["d2"], "d2"))
-        quantize_weight("s1", late_codes(N, "w_s1", "second", -1024))
-        product("s1", quantize_woven(woven["s1"], "s1"))
-        woven["hown"] = late_tile([P, V, PACK], BF16, "woven_hown", "second", 1024)
-        nc.vector.tensor_copy(out=as_woven(woven["hown"][:])[:, HOWN_SCALAR_RUNS:], in_=as_planes(planes["hown"])[:, HOWN_SCALAR_RUNS:])
-        nc.scalar.copy(out=as_woven(woven["hown"][:])[:, 0:HOWN_SCALAR_RUNS], in_=as_planes(planes["hown"])[:, 0:HOWN_SCALAR_RUNS])
-        weave_words("s2", words_s2)
-        quantize_weight("hown", mx_tiles(N, "w_hown"))
-        product("hown", quantize_woven(woven["hown"], "hown"))
-        last_dealt = [late_tile([P, 2, P, PACK], BF16, "w_dealt_s2_0", "d2", 64), late_tile([P, 2, P, PACK], BF16, "w_dealt_s2_1", "s1", 2048)]
-        deal_planes(nc.scalar.copy, last_dealt[0], w_raw["s2"], 0, 0, P)
-        deal_planes(nc.vector.tensor_copy, last_dealt[1], w_raw["s2"], 2, 0, LAST_VECTOR)
-        deal_planes(nc.scalar.copy, last_dealt[1], w_raw["s2"], 2, LAST_VECTOR, P)
-        s2_mx = quantize_woven(woven["s2"], "s2")
-        w_mx["s2"] = quantize_two_planes(mx_tiles(2 * P, "w_s2_0"), last_dealt[0]) + quantize_two_planes(mx_tiles(2 * P, "w_s2_1"), last_dealt[1])
-        product("s2", s2_mx)
+            mx = mx_tiles(P, "w_last%d" % t)
+            quantize(mx, slice(0, P), last_dealt[t // 2][:, t % 2].rearrange("p m j -> p (m j)"))
+            w_mx["hown"][t] = mx + (slice(0, P),)
+            product("hown", t)
 
         y = sbuf([P, PACK, V], F32, "y")
         out_planes = out_0.rearrange("(p t) v -> p t v", t=PACK)
-        for t in range(0, PACK, 2):
+        for t in (0, 2):
             nc.vector.tensor_copy(out=y[:, t, :], in_=y_banks[t][:])
             nc.scalar.copy(out=y[:, t + 1, :], in_=y_banks[t + 1][:])
             nc.sync.dma_start(out=out_planes[:, t : t + 2, :], in_=y[:, t : t + 2, :])
         y_woven = sbuf([P, V, PACK], BF16, "woven_y")
         half = V // RUN // 2
-        nc.scalar.copy(out=as_woven(y_woven[:])[:, WEAVE_VECTOR_RUNS:], in_=as_planes(y)[:, WEAVE_VECTOR_RUNS:])
-        nc.vector.tensor_copy(out=as_woven(y_woven[:])[:, 0:half], in_=as_planes(y)[:, 0:half])
-        nc.vector.tensor_copy(out=as_woven(y_woven[:])[:, half:WEAVE_VECTOR_RUNS], in_=as_planes(y)[:, half:WEAVE_VECTOR_RUNS])
+        nc.scalar.copy(out=as_woven(y_woven)[:, WEAVE_VECTOR_RUNS:], in_=as_planes(y)[:, WEAVE_VECTOR_RUNS:])
+        nc.vector.tensor_copy(out=as_woven(y_woven)[:, 0:half], in_=as_planes(y)[:, 0:half])
+        nc.vector.tensor_copy(out=as_woven(y_woven)[:, half:WEAVE_VECTOR_RUNS], in_=as_planes(y)[:, half:WEAVE_VECTOR_RUNS])
         y_codes, y_scales = mx_tiles(V, "y")
         for cols in (slice(0, V // 2), slice(V // 2, V)):
             quantize((y_codes, y_scales), cols, y_woven[:, cols].rearrange("p v t -> p (v t)"))

@@ -1,6 +1,7 @@
 from contextlib import ExitStack
 
 import concourse.mybir as mybir
+from concourse.masks import make_identity
 
 K, T, S, H, N, V = 1024, 1024, 512, 512, 512, 256
 FLOPS = 2 * K * H * S + 5 * 2 * H * N * V
@@ -19,6 +20,7 @@ P = 128
 PACK = 4
 K_PASS = P * PACK
 QUADRANT = 32
+BANKS = 8
 RUN = 4
 
 PASS0_VECTOR = 84
@@ -34,12 +36,31 @@ def tile_picked_ymeshcnn_relu_po_kernel(tc, x_words, x_scales, w1, w2, w3, w4, w
         late = ctx.enter_context(tc.tile_pool(name="late", bufs=1))
         psum = ctx.enter_context(tc.psum_pool(name="psum", bufs=1))
         woven_bytes = 2 * V * PACK
-        places = {"w_s2_raw": 0, "woven_s1": 0, "woven_e1": woven_bytes, "woven_s2": 2 * woven_bytes, "woven_e2": 3 * woven_bytes, "w_dealt_s2": 4 * woven_bytes, "woven_hown": 4 * woven_bytes}
+        raw_bytes = 4 * PACK * N // 2
+        places = {
+            "hown": 0,
+            "woven_d1": 0,
+            "w_dealt_d1": raw_bytes,
+            "woven_d2": raw_bytes,
+            "w_d2_raw": 2 * raw_bytes,
+            "s1_codes": 2 * raw_bytes,
+            "s2_codes": 2 * raw_bytes + 4 * V,
+            "d1_codes": 3 * raw_bytes,
+            "d2_codes": 3 * raw_bytes + 4 * V,
+        }
 
         def sbuf(shape, dtype, name, tag=None):
             if name in places:
                 return late.tile(shape, dtype, name=name, align_bytes=64, offset=places[name])
             return keep.tile(shape, dtype, name=name, tag=tag or name, align_bytes=64)
+
+        plane_step = 1920
+        woven_words = V * PACK // 2
+        raw_words = PACK * N
+        own_at = PACK * plane_step
+        shared = sbuf([P, own_at + woven_words + raw_words], F32, "shared")
+        inside = {"w_hown_1": V - 16, "w_s1": plane_step, "w_s2": 2 * plane_step + V - 16, "w_d1": own_at + woven_words - 16}
+        woven_in = {"hown": own_at}
 
         def load_list(ap, name):
             tile = keep.tile(list(ap.shape), U16, name=name)
@@ -52,7 +73,10 @@ def tile_picked_ymeshcnn_relu_po_kernel(tc, x_words, x_scales, w1, w2, w3, w4, w
             return tile
 
         def load_weight(rows, name):
-            raw = sbuf([P, PACK, rows.shape[1]], F32, name + "_raw")
+            if name in inside:
+                raw = shared[:, inside[name] : inside[name] + PACK * rows.shape[1]].rearrange("p (j c) -> p j c", j=PACK)
+            else:
+                raw = sbuf([P, PACK, rows.shape[1]], F32, name + "_raw")
             nc.sync.dma_start(out=raw[:], in_=rows.rearrange("(p j) c -> p j c", j=PACK))
             return raw
 
@@ -92,15 +116,15 @@ def tile_picked_ymeshcnn_relu_po_kernel(tc, x_words, x_scales, w1, w2, w3, w4, w
         w1_raw = [load_weight(w1[0:K_PASS, :], "w1_pass0")]
         words_in.append(load_words(1))
         w1_raw.append(load_weight(w1[K_PASS:K, :], "w1_pass1"))
-        first_raw = [load_weight(w3[:, 0 : N // 2], "w_s1_0")]
-        for name, ap in (("ea", ea), ("ec", ec)):
+        first_raw = [load_weight(w2[:, 0 : N // 2], "w_hown_0")]
+        for name, ap in (("ea", ea), ("eb", eb), ("ec", ec)):
             lists[name] = load_list(ap, name)
-        first_raw.append(load_weight(w3[:, N // 2 : N], "w_s1_1"))
-        for name, ap in (("eb", eb), ("ed", ed), ("own", own)):
+        first_raw.append(load_weight(w2[:, N // 2 : N], "w_hown_1"))
+        for name, ap in (("ed", ed), ("own", own)):
             lists[name] = load_list(ap, name)
-        operands = ("s1", "d1", "s2", "d2", "hown")
+        operands = ("hown", "s1", "s2", "d1", "d2")
         w_raw = {}
-        for name, w in (("d1", w4), ("s2", w5), ("d2", w6), ("hown", w2)):
+        for name, w in (("s1", w3), ("s2", w5), ("d1", w4), ("d2", w6)):
             w_raw[name] = load_weight(w, "w_" + name)
 
         pieces = [(0, slice(0, S // 2)), (0, slice(S // 2, S))] + [(t, slice(0, S)) for t in range(1, PACK)]
@@ -149,12 +173,12 @@ def tile_picked_ymeshcnn_relu_po_kernel(tc, x_words, x_scales, w1, w2, w3, w4, w
         deal(nc.scalar.copy, pairs[1][:], w1_raw[1], 2, PAIR1_VECTOR, P)
 
         dealt_shape = [P, PACK, P, PACK]
-        w_dealt = {"s1": sbuf(dealt_shape, BF16, "w_dealt_s1")}
+        w_dealt = {"hown": sbuf(dealt_shape, BF16, "w_dealt_hown")}
 
         def round_first(half, first):
-            deal(nc.vector.tensor_copy, w_dealt["s1"][:, first : first + 2], first_raw[half], first, 0, P // 2, P // 2 * half)
+            deal(nc.vector.tensor_copy, w_dealt["hown"][:, first : first + 2], first_raw[half], first, 0, P // 2, P // 2 * half)
 
-        h = [keep.tile([P, S], F32, name="h%d" % t) for t in range(PACK)]
+        h = [sbuf([P, S], F32, "h%d" % t) for t in range(PACK)]
         round_first(0, 0)
         nc.vector.tensor_scalar_max(h[0][:, 0 : S // 2], h_banks[0][:], 0.0)
         nc.scalar.activation(h[0][:, S // 2 : S], h_banks[1][:], ACT.Relu)
@@ -166,30 +190,74 @@ def tile_picked_ymeshcnn_relu_po_kernel(tc, x_words, x_scales, w1, w2, w3, w4, w
         w_mx = {}
         mx_of = {}
         y_banks = {}
+        words = {}
+        turned_banks = {}
+        identity = sbuf([P, P], F32, "identity")
+        make_identity(nc, identity[:])
 
         def pick(name, list_name, t):
             nc.scalar.activation(planes[name][:, t, :], h[t][:].indirect(lists[list_name][:]), ACT.Copy)
 
-        def empty_h(t):
-            nc.vector.tensor_scalar_max(h[t][:], h_banks[1 + t][:], 0.0)
+        def turn(name, term, t, start, stop):
+            for half in range(V // P):
+                nc.tensor.matmul(
+                    turned_banks[name, half][:, t, :],
+                    planes[term][:, t, P * half : P * (half + 1)],
+                    identity[:],
+                    start=start,
+                    stop=stop,
+                    is_transpose=True,
+                )
 
-        def round_weight(copy, name):
-            w_dealt[name] = sbuf(dealt_shape, BF16, "w_dealt_" + name)
-            for first in (0, 2):
-                deal(copy, w_dealt[name][:, first : first + 2], w_raw[name], first, 0, P)
+        def pick_first(total, name, list_name, t):
+            pick(name, list_name, t)
+            turn(total, name, t, t == 0, False)
+            turn(total, name, t, False, False)
+
+        def pick_minus(total, name, list_name, first, t):
+            nc.vector.tensor_tensor(planes[name][:, t, :], h[t][:].indirect(lists[list_name][:]), planes[first][:, t, :], ALU.subtract)
+            turn(total, name, t, False, t == PACK - 1)
+
+        def empty_h(t):
+            nc.scalar.activation(h[t][:], h_banks[1 + t][:], ACT.Relu)
+
+        def round_part(name, m0, m1):
+            if name not in w_dealt:
+                w_dealt[name] = sbuf(dealt_shape, BF16, "w_dealt_" + name)
+            nc.vector.tensor_copy(
+                out=w_dealt[name][:].rearrange("p t (m e) j -> p m j e t", e=2)[:, m0 // 2 : m1 // 2],
+                in_=w_raw[name][:].rearrange("p j (m e t) -> p m j e t", e=2, t=PACK)[:, m0 // 2 : m1 // 2],
+            )
+
+        def round_half(name, half):
+            round_part(name, P // 2 * half, P // 2 * (half + 1))
 
         def quantize_weight(name):
             mx = mx_tiles(N, "w_" + name)
             quantize(mx, slice(0, N), w_dealt[name][:].rearrange("p t m j -> p (t m j)"))
             w_mx[name] = [mx + (plane_cols(t),) for t in range(PACK)]
 
-        def combine(name, x, y, op):
-            woven[name] = sbuf([P, V, PACK], BF16, "woven_" + name)
-            nc.vector.tensor_tensor(as_woven(woven[name], 2), as_planes(planes[x], 2), as_planes(planes[y], 2), op)
+        def weave_abs(name, signed):
+            woven[name] = woven_view(name)
+            nc.scalar.activation(as_woven(woven[name]), as_planes(planes[signed]), ACT.Abs)
 
-        def absolute(name, signed):
-            woven[name] = sbuf([P, V, PACK], BF16, "woven_" + name)
-            nc.vector.scalar_tensor_tensor(flat(woven[name]), flat(woven[signed]), -1.0, flat(woven[signed]), ALU.mult, ALU.max)
+        def turn_back(name, half, turned):
+            for u in range(2):
+                nc.tensor.transpose(words[name][:, u, P * half : P * (half + 1)], turned[:, u].rearrange("v p e -> v (p e)").bitcast(F32), identity[:])
+
+        def round_turned(name, half):
+            turned = sbuf([P, 2, P, 2], BF16, "turned_%s%d" % (name, half))
+            nc.scalar.activation(turned[:], turned_banks[name, half][:].rearrange("v (u e) p -> v u p e", e=2), ACT.Copy)
+            turn_back(name, half, turned)
+
+        def woven_view(name):
+            if name in woven_in:
+                return shared[:, woven_in[name] : woven_in[name] + woven_words].bitcast(BF16).rearrange("p (v t) -> p v t", t=PACK)
+            return sbuf([P, V, PACK], BF16, "woven_" + name)
+
+        def weave_words(name):
+            woven[name] = woven_view(name)
+            nc.scalar.copy(out=woven[name][:].bitcast(F32), in_=words[name][:].rearrange("p u v -> p v u"))
 
         def quantize_operand(name):
             mx_of[name] = mx_tiles(V, name)
@@ -197,7 +265,7 @@ def tile_picked_ymeshcnn_relu_po_kernel(tc, x_words, x_scales, w1, w2, w3, w4, w
 
         def product(name, t):
             if name == operands[0]:
-                y_banks[t] = psum.tile([P, V], F32, name="y_bank%d" % t, tag="bank%d" % ((5 + t) % 8))
+                y_banks[t] = psum.tile([P, V], F32, name="y_bank%d" % t, tag="bank%d" % (1 + t))
             codes, scales, cols = w_mx[name][t]
             nc.tensor.matmul_mx(
                 out=y_banks[t][:],
@@ -213,63 +281,79 @@ def tile_picked_ymeshcnn_relu_po_kernel(tc, x_words, x_scales, w1, w2, w3, w4, w
             for t in range(PACK):
                 product(name, t)
 
-        for name in ("hea", "hec", "heb", "hed"):
+        for name in ("hea", "heb"):
             planes[name] = sbuf([P, PACK, V], F32, name)
+        for i, name in enumerate(("e1", "e2")):
+            planes[name] = shared[:, 0 : PACK * plane_step].rearrange("p (t x) -> p t x", t=PACK)[:, :, V * i : V * (i + 1)]
         planes["hown"] = sbuf([P, PACK, V], BF16, "hown")
+        for i, name in enumerate(("s1", "s2")):
+            for half in range(V // P):
+                turned_banks[name, half] = psum.tile([P, PACK, P], F32, name="turned_%s%d" % (name, half), tag="bank%d" % ((len(pieces) + 2 * i + half) % BANKS))
 
-        pick("hea", "ea", 0)
-        pick("hec", "ec", 0)
-        empty_h(1)
-        round_first(0, 2)
-        round_first(1, 0)
-        pick("hea", "ea", 1)
-        pick("hec", "ec", 1)
-        empty_h(2)
-        round_first(1, 2)
-        pick("hea", "ea", 2)
-        pick("hec", "ec", 2)
-        quantize_weight("s1")
-        nc.scalar.activation(h[3][:], h_banks[4][:], ACT.Relu)
-        pick("hea", "ea", 3)
-        pick("hec", "ec", 3)
-        for t in range(PACK):
-            pick("heb", "eb", t)
-            pick("hed", "ed", t)
-        for t in range(PACK):
+        def pick_firsts(t):
+            if t > 0:
+                empty_h(t)
+            pick_first("s1", "hea", "ea", t)
+            pick_first("s2", "heb", "eb", t)
             pick("hown", "own", t)
 
-        round_weight(nc.vector.tensor_copy, "d1")
-        quantize_weight("d1")
-        round_weight(nc.vector.tensor_copy, "s2")
+        def minus1(t):
+            pick_minus("s1", "e1", "ec", "hea", t)
+
+        def minus2(t):
+            pick_minus("s2", "e2", "ed", "heb", t)
+
+        pick_firsts(0)
+        round_first(0, 2)
+        for quarter in range(2):
+            nc.vector.tensor_copy(
+                out=w_dealt["hown"][:].rearrange("p t (m e) j -> p m j e t", e=2)[:, P // 8 * (2 + quarter) : P // 8 * (3 + quarter)],
+                in_=first_raw[1][:].rearrange("p j (m e t) -> p m j e t", e=2, t=PACK)[:, P // 8 * quarter : P // 8 * (quarter + 1)],
+            )
+        minus1(0)
+        quantize_weight("hown")
+        minus2(0)
+        round_half("s1", 0)
+        round_half("s1", 1)
+        pick_firsts(1)
+        minus1(1)
+        minus2(1)
+        quantize_weight("s1")
+        round_half("s2", 0)
+        round_half("s2", 1)
+        pick_firsts(2)
+        minus1(2)
+        minus2(2)
+        pick_firsts(3)
+        minus1(3)
         quantize_weight("s2")
-        combine("s1", "hea", "hec", ALU.add)
-        combine("e1", "hea", "hec", ALU.subtract)
+        minus2(3)
+        for i, name in enumerate(("s1", "s2")):
+            words[name] = psum.tile([P, 2, V], F32, name="words_" + name, tag="bank%d" % (len(pieces) + i))
+            for half in range(V // P):
+                round_turned(name, half)
+        weave_words("s1")
+        weave_words("s2")
+        round_half("d1", 0)
+        round_half("d1", 1)
+        woven["hown"] = woven_view("hown")
+        nc.vector.tensor_copy(out=as_woven(woven["hown"]), in_=as_planes(planes["hown"]))
+        weave_abs("d1", "e1")
+        quantize_weight("d1")
+        weave_abs("d2", "e2")
+        quantize_operand("hown")
+        products("hown")
+        round_half("d2", 0)
+        round_half("d2", 1)
         quantize_operand("s1")
         products("s1")
-        absolute("d1", "e1")
-        round_weight(nc.vector.tensor_copy, "d2")
+        quantize_operand("s2")
+        quantize_weight("d2")
+        products("s2")
         quantize_operand("d1")
         products("d1")
-        quantize_weight("d2")
-        combine("s2", "heb", "hed", ALU.add)
-        combine("e2", "heb", "hed", ALU.subtract)
-        quantize_operand("s2")
-        products("s2")
-        absolute("d2", "e2")
-        woven["hown"] = sbuf([P, V, PACK], BF16, "woven_hown")
-        nc.vector.tensor_copy(out=as_woven(woven["hown"]), in_=as_planes(planes["hown"]))
         quantize_operand("d2")
         products("d2")
-        quantize_operand("hown")
-        last_dealt = [sbuf([P, 2, P, PACK], BF16, "w_dealt_last%d" % u) for u in range(2)]
-        for u in range(2):
-            deal(nc.scalar.copy, last_dealt[u][:], w_raw["hown"], 2 * u, 0, P)
-        w_mx["hown"] = {}
-        for t in range(PACK):
-            mx = mx_tiles(P, "w_last%d" % t)
-            quantize(mx, slice(0, P), last_dealt[t // 2][:, t % 2].rearrange("p m j -> p (m j)"))
-            w_mx["hown"][t] = mx + (slice(0, P),)
-            product("hown", t)
 
         y = sbuf([P, PACK, V], F32, "y")
         out_planes = out_0.rearrange("(p t) v -> p t v", t=PACK)

@@ -54,12 +54,12 @@ def tile_picked_ymeshcnn_relu_po_kernel(tc, x_words, x_scales, w1, w2, w3, w4, w
                 return late.tile(shape, dtype, name=name, align_bytes=64, offset=places[name])
             return keep.tile(shape, dtype, name=name, tag=tag or name, align_bytes=64)
 
-        plane_step = 1920
         woven_words = V * PACK // 2
         raw_words = PACK * N
-        own_at = PACK * plane_step
+        own_at = 6112
         shared = sbuf([P, own_at + woven_words + raw_words], F32, "shared")
-        inside = {"w_hown_1": V - 16, "w_s1": plane_step, "w_s2": 2 * plane_step + V - 16, "w_d1": own_at + woven_words - 16}
+        plane_at = {"e1": (1008, 2 * V), "e2": (752, 4 * V)}
+        inside = {"w_hown_1": 0, "w_s1": 1520, "w_s2": 4064, "w_d1": own_at + woven_words - 16}
         woven_in = {"hown": own_at}
 
         def load_list(ap, name):
@@ -283,8 +283,8 @@ def tile_picked_ymeshcnn_relu_po_kernel(tc, x_words, x_scales, w1, w2, w3, w4, w
 
         for name in ("hea", "heb"):
             planes[name] = sbuf([P, PACK, V], F32, name)
-        for i, name in enumerate(("e1", "e2")):
-            planes[name] = shared[:, 0 : PACK * plane_step].rearrange("p (t x) -> p t x", t=PACK)[:, :, V * i : V * (i + 1)]
+        for name, (at, step) in plane_at.items():
+            planes[name] = shared[:, at : at + PACK * step].rearrange("p (t x) -> p t x", t=PACK)[:, :, 0:V]
         planes["hown"] = sbuf([P, PACK, V], BF16, "hown")
         for i, name in enumerate(("s1", "s2")):
             for half in range(V // P):
@@ -295,7 +295,6 @@ def tile_picked_ymeshcnn_relu_po_kernel(tc, x_words, x_scales, w1, w2, w3, w4, w
                 empty_h(t)
             pick_first("s1", "hea", "ea", t)
             pick_first("s2", "heb", "eb", t)
-            pick("hown", "own", t)
 
         def minus1(t):
             pick_minus("s1", "e1", "ec", "hea", t)
@@ -305,7 +304,7 @@ def tile_picked_ymeshcnn_relu_po_kernel(tc, x_words, x_scales, w1, w2, w3, w4, w
 
         pick_firsts(0)
         round_first(0, 2)
-        for quarter in range(2):
+        for quarter in (1, 0):
             nc.vector.tensor_copy(
                 out=w_dealt["hown"][:].rearrange("p t (m e) j -> p m j e t", e=2)[:, P // 8 * (2 + quarter) : P // 8 * (3 + quarter)],
                 in_=first_raw[1][:].rearrange("p j (m e t) -> p m j e t", e=2, t=PACK)[:, P // 8 * quarter : P // 8 * (quarter + 1)],
@@ -316,18 +315,20 @@ def tile_picked_ymeshcnn_relu_po_kernel(tc, x_words, x_scales, w1, w2, w3, w4, w
         round_half("s1", 0)
         round_half("s1", 1)
         pick_firsts(1)
+        pick_firsts(2)
         minus1(1)
         minus2(1)
         quantize_weight("s1")
-        round_half("s2", 0)
-        round_half("s2", 1)
-        pick_firsts(2)
+        pick_firsts(3)
+        for t in range(PACK):
+            pick("hown", "own", t)
         minus1(2)
         minus2(2)
-        pick_firsts(3)
         minus1(3)
-        quantize_weight("s2")
+        round_half("s2", 0)
+        round_half("s2", 1)
         minus2(3)
+        quantize_weight("s2")
         for i, name in enumerate(("s1", "s2")):
             words[name] = psum.tile([P, 2, V], F32, name="words_" + name, tag="bank%d" % (len(pieces) + i))
             for half in range(V // P):

@@ -26,6 +26,7 @@ RUN = 4
 PASS0_VECTOR = 84
 PAIR0_VECTOR = 84
 PAIR1_VECTOR = 96
+SHARED_VECTOR = 64
 WEAVE_VECTOR_RUNS = 46
 
 
@@ -40,8 +41,7 @@ def tile_picked_ymeshcnn_relu_po_kernel(tc, x_words, x_scales, w1, w2, w3, w4, w
         places = {
             "hown": 0,
             "woven_d1": 0,
-            "w_dealt_d1": raw_bytes,
-            "woven_d2": raw_bytes,
+            "w_d1_codes": 2 * raw_bytes + 8 * V,
             "w_d2_raw": 2 * raw_bytes,
             "s1_codes": 2 * raw_bytes,
             "s2_codes": 2 * raw_bytes + 4 * V,
@@ -60,7 +60,7 @@ def tile_picked_ymeshcnn_relu_po_kernel(tc, x_words, x_scales, w1, w2, w3, w4, w
         shared = sbuf([P, own_at + woven_words + raw_words], F32, "shared")
         plane_at = {"e1": (1008, 2 * V), "e2": (752, 4 * V)}
         inside = {"w_hown_1": 0, "w_s1": 1520, "w_s2": 4064, "w_d1": own_at + woven_words - 16}
-        woven_in = {"hown": own_at}
+        woven_in = {"hown": own_at, "d2": own_at - woven_words // 2}
 
         def load_list(ap, name):
             tile = keep.tile(list(ap.shape), U16, name=name)
@@ -335,22 +335,27 @@ def tile_picked_ymeshcnn_relu_po_kernel(tc, x_words, x_scales, w1, w2, w3, w4, w
                 round_turned(name, half)
         weave_words("s1")
         weave_words("s2")
-        round_half("d1", 0)
-        round_half("d1", 1)
+        round_part("d1", 0, SHARED_VECTOR // 2)
+        round_part("d1", SHARED_VECTOR // 2, SHARED_VECTOR)
+        for first in (0, 2):
+            nc.scalar.copy(
+                out=w_dealt["d1"][:, first : first + 2].rearrange("p t (m e) j -> p m j e t", e=2)[:, SHARED_VECTOR // 2 :],
+                in_=w_raw["d1"][:].rearrange("p j (m e t) -> p m j e t", e=2, t=PACK)[:, SHARED_VECTOR // 2 :, :, :, first : first + 2],
+            )
         woven["hown"] = woven_view("hown")
         nc.vector.tensor_copy(out=as_woven(woven["hown"]), in_=as_planes(planes["hown"]))
         weave_abs("d1", "e1")
-        quantize_weight("d1")
-        weave_abs("d2", "e2")
         quantize_operand("hown")
         products("hown")
+        weave_abs("d2", "e2")
         round_half("d2", 0)
         round_half("d2", 1)
         quantize_operand("s1")
         products("s1")
         quantize_operand("s2")
-        quantize_weight("d2")
         products("s2")
+        quantize_weight("d1")
+        quantize_weight("d2")
         quantize_operand("d1")
         products("d1")
         quantize_operand("d2")

@@ -26,7 +26,7 @@ RUN = 4
 PASS0_VECTOR = 84
 PAIR0_VECTOR = 84
 PAIR1_VECTOR = 96
-SHARED_VECTOR = 64
+LAST_VECTOR = 96
 WEAVE_VECTOR_RUNS = 46
 
 
@@ -41,12 +41,12 @@ def tile_picked_ymeshcnn_relu_po_kernel(tc, x_words, x_scales, w1, w2, w3, w4, w
         places = {
             "hown": 0,
             "woven_d1": 0,
-            "w_d1_codes": 2 * raw_bytes + 8 * V,
-            "w_d2_raw": 2 * raw_bytes,
-            "s1_codes": 2 * raw_bytes,
-            "s2_codes": 2 * raw_bytes + 4 * V,
-            "d1_codes": 3 * raw_bytes,
-            "d2_codes": 3 * raw_bytes + 4 * V,
+            "w_dealt_d1": raw_bytes,
+            "s1_codes": raw_bytes,
+            "s2_codes": 2 * raw_bytes + 12 * V,
+            "w_d2_0_raw": 2 * raw_bytes,
+            "d1_codes": 2 * raw_bytes,
+            "woven_d2": 2 * raw_bytes + 4 * V,
         }
 
         def sbuf(shape, dtype, name, tag=None):
@@ -60,7 +60,7 @@ def tile_picked_ymeshcnn_relu_po_kernel(tc, x_words, x_scales, w1, w2, w3, w4, w
         shared = sbuf([P, own_at + woven_words + raw_words], F32, "shared")
         plane_at = {"e1": (1008, 2 * V), "e2": (752, 4 * V)}
         inside = {"w_hown_1": 0, "w_s1": 1520, "w_s2": 4064, "w_d1": own_at + woven_words - 16}
-        woven_in = {"hown": own_at, "d2": own_at - woven_words // 2}
+        woven_in = {"hown": own_at}
 
         def load_list(ap, name):
             tile = keep.tile(list(ap.shape), U16, name=name)
@@ -124,8 +124,10 @@ def tile_picked_ymeshcnn_relu_po_kernel(tc, x_words, x_scales, w1, w2, w3, w4, w
             lists[name] = load_list(ap, name)
         operands = ("hown", "s1", "s2", "d1", "d2")
         w_raw = {}
-        for name, w in (("s1", w3), ("s2", w5), ("d1", w4), ("d2", w6)):
+        for name, w in (("s1", w3), ("s2", w5), ("d1", w4)):
             w_raw[name] = load_weight(w, "w_" + name)
+        last_scalar = load_weight(w6[:, PACK * LAST_VECTOR : N], "w_d2_1")
+        last_raw = [load_weight(w6[:, 0 : PACK * LAST_VECTOR], "w_d2_0"), last_scalar]
 
         pieces = [(0, slice(0, S // 2)), (0, slice(S // 2, S))] + [(t, slice(0, S)) for t in range(1, PACK)]
         h_banks = [psum.tile([P, edges.stop - edges.start], F32, name="h_bank%d" % i, tag="bank%d" % i) for i, (t, edges) in enumerate(pieces)]
@@ -263,18 +265,18 @@ def tile_picked_ymeshcnn_relu_po_kernel(tc, x_words, x_scales, w1, w2, w3, w4, w
             mx_of[name] = mx_tiles(V, name)
             quantize(mx_of[name], slice(0, V), flat(woven[name]))
 
-        def product(name, t):
+        def product(name, t, edges=slice(0, V), stop=False):
             if name == operands[0]:
                 y_banks[t] = psum.tile([P, V], F32, name="y_bank%d" % t, tag="bank%d" % (1 + t))
             codes, scales, cols = w_mx[name][t]
             nc.tensor.matmul_mx(
-                out=y_banks[t][:],
+                out=y_banks[t][:, edges],
                 lhsT=codes[:, cols].bitcast(FP8X4),
                 lhsT_scale=scales[:, cols],
-                rhs=mx_of[name][0][:].bitcast(FP8X4),
-                rhs_scale=mx_of[name][1][:],
+                rhs=mx_of[name][0][:, edges].bitcast(FP8X4),
+                rhs_scale=mx_of[name][1][:, edges],
                 start=(name == operands[0]),
-                stop=(name == operands[-1]),
+                stop=stop,
             )
 
         def products(name):
@@ -335,31 +337,35 @@ def tile_picked_ymeshcnn_relu_po_kernel(tc, x_words, x_scales, w1, w2, w3, w4, w
                 round_turned(name, half)
         weave_words("s1")
         weave_words("s2")
-        round_part("d1", 0, SHARED_VECTOR // 2)
-        round_part("d1", SHARED_VECTOR // 2, SHARED_VECTOR)
-        for first in (0, 2):
-            nc.scalar.copy(
-                out=w_dealt["d1"][:, first : first + 2].rearrange("p t (m e) j -> p m j e t", e=2)[:, SHARED_VECTOR // 2 :],
-                in_=w_raw["d1"][:].rearrange("p j (m e t) -> p m j e t", e=2, t=PACK)[:, SHARED_VECTOR // 2 :, :, :, first : first + 2],
-            )
+        round_half("d1", 0)
+        round_half("d1", 1)
         woven["hown"] = woven_view("hown")
         nc.vector.tensor_copy(out=as_woven(woven["hown"]), in_=as_planes(planes["hown"]))
         weave_abs("d1", "e1")
-        quantize_operand("hown")
-        products("hown")
-        weave_abs("d2", "e2")
-        round_half("d2", 0)
-        round_half("d2", 1)
-        quantize_operand("s1")
-        products("s1")
-        quantize_operand("s2")
-        products("s2")
         quantize_weight("d1")
+        for name in ("hown", "s1"):
+            quantize_operand(name)
+            products(name)
+        w_dealt["d2"] = sbuf(dealt_shape, BF16, "w_dealt_d2")
+        for first in (0, 2):
+            deal(nc.scalar.copy, w_dealt["d2"][:, first : first + 2], last_raw[1], first, 0, P - LAST_VECTOR, LAST_VECTOR)
+        nc.vector.tensor_copy(
+            out=w_dealt["d2"][:].rearrange("p t (m e) j -> p m j e t", e=2)[:, 0 : LAST_VECTOR // 2],
+            in_=last_raw[0][:].rearrange("p j (m e t) -> p m j e t", e=2, t=PACK),
+        )
+        for name in ("s2", "d1"):
+            quantize_operand(name)
+            products(name)
         quantize_weight("d2")
-        quantize_operand("d1")
-        products("d1")
-        quantize_operand("d2")
-        products("d2")
+        woven["d2"] = woven_view("d2")
+        mx_of["d2"] = mx_tiles(V, "d2")
+        for half in range(2):
+            edges = slice(V // 2 * half, V // 2 * (half + 1))
+            runs = slice(V // RUN // 2 * half, V // RUN // 2 * (half + 1))
+            nc.scalar.activation(as_woven(woven["d2"])[:, runs], as_planes(planes["e2"])[:, runs], ACT.Abs)
+            quantize(mx_of["d2"], edges, woven["d2"][:, edges].rearrange("p v t -> p (v t)"))
+            for t in range(PACK):
+                product("d2", t, edges, half == 1)
 
         y = sbuf([P, PACK, V], F32, "y")
         out_planes = out_0.rearrange("(p t) v -> p t v", t=PACK)

@@ -27,7 +27,6 @@ PASS0_VECTOR = 84
 PAIR0_VECTOR = 84
 PAIR1_VECTOR = 96
 LAST_VECTOR = 96
-WEAVE_VECTOR_RUNS = 46
 
 
 def tile_picked_ymeshcnn_relu_po_kernel(tc, x_words, x_scales, w1, w2, w3, w4, w5, w6, offs, own, ea, eb, ec, ed, out_0, out_1, out_2):
@@ -177,11 +176,12 @@ def tile_picked_ymeshcnn_relu_po_kernel(tc, x_words, x_scales, w1, w2, w3, w4, w
         dealt_shape = [P, PACK, P, PACK]
         w_dealt = {"hown": sbuf(dealt_shape, BF16, "w_dealt_hown")}
 
-        def round_first(half, first):
-            deal(nc.vector.tensor_copy, w_dealt["hown"][:, first : first + 2], first_raw[half], first, 0, P // 2, P // 2 * half)
+        def round_first(copy, half, first):
+            deal(copy, w_dealt["hown"][:, first : first + 2], first_raw[half], first, 0, P // 2, P // 2 * half)
 
         h = [sbuf([P, S], F32, "h%d" % t) for t in range(PACK)]
-        round_first(0, 0)
+        round_first(nc.vector.tensor_copy, 0, 0)
+        round_first(nc.scalar.copy, 0, 2)
         nc.vector.tensor_scalar_max(h[0][:, 0 : S // 2], h_banks[0][:], 0.0)
         nc.scalar.activation(h[0][:, S // 2 : S], h_banks[1][:], ACT.Relu)
         second_pass(2)
@@ -265,23 +265,25 @@ def tile_picked_ymeshcnn_relu_po_kernel(tc, x_words, x_scales, w1, w2, w3, w4, w
             mx_of[name] = mx_tiles(V, name)
             quantize(mx_of[name], slice(0, V), flat(woven[name]))
 
-        def product(name, t, edges=slice(0, V), stop=False):
-            if name == operands[0]:
-                y_banks[t] = psum.tile([P, V], F32, name="y_bank%d" % t, tag="bank%d" % (1 + t))
-            codes, scales, cols = w_mx[name][t]
-            nc.tensor.matmul_mx(
-                out=y_banks[t][:, edges],
-                lhsT=codes[:, cols].bitcast(FP8X4),
-                lhsT_scale=scales[:, cols],
-                rhs=mx_of[name][0][:, edges].bitcast(FP8X4),
-                rhs_scale=mx_of[name][1][:, edges],
-                start=(name == operands[0]),
-                stop=stop,
-            )
+        def product(name, half):
+            edges = slice(P * half, P * (half + 1))
+            for t in range(PACK):
+                if name == operands[0] and t % 2 == 0:
+                    y_banks[half, t // 2] = psum.tile([P, 2, P], F32, name="y_bank%d%d" % (half, t // 2), tag="bank%d" % (1 + 2 * half + t // 2))
+                codes, scales, cols = w_mx[name][t]
+                nc.tensor.matmul_mx(
+                    out=y_banks[half, t // 2][:, t % 2, :],
+                    lhsT=codes[:, cols].bitcast(FP8X4),
+                    lhsT_scale=scales[:, cols],
+                    rhs=mx_of[name][0][:, edges].bitcast(FP8X4),
+                    rhs_scale=mx_of[name][1][:, edges],
+                    start=(name == operands[0] and t % 2 == 0),
+                    stop=(name == operands[-1] and t % 2 == 1),
+                )
 
         def products(name):
-            for t in range(PACK):
-                product(name, t)
+            for half in range(V // P):
+                product(name, half)
 
         for name in ("hea", "heb"):
             planes[name] = sbuf([P, PACK, V], F32, name)
@@ -305,14 +307,12 @@ def tile_picked_ymeshcnn_relu_po_kernel(tc, x_words, x_scales, w1, w2, w3, w4, w
             pick_minus("s2", "e2", "ed", "heb", t)
 
         pick_firsts(0)
-        round_first(0, 2)
-        for quarter in (1, 0):
-            nc.vector.tensor_copy(
-                out=w_dealt["hown"][:].rearrange("p t (m e) j -> p m j e t", e=2)[:, P // 8 * (2 + quarter) : P // 8 * (3 + quarter)],
-                in_=first_raw[1][:].rearrange("p j (m e t) -> p m j e t", e=2, t=PACK)[:, P // 8 * quarter : P // 8 * (quarter + 1)],
-            )
-        minus1(0)
+        nc.vector.tensor_copy(
+            out=w_dealt["hown"][:].rearrange("p t (m e) j -> p m j e t", e=2)[:, P // 4 :],
+            in_=first_raw[1][:].rearrange("p j (m e t) -> p m j e t", e=2, t=PACK),
+        )
         quantize_weight("hown")
+        minus1(0)
         minus2(0)
         round_half("s1", 0)
         round_half("s1", 1)
@@ -364,20 +364,21 @@ def tile_picked_ymeshcnn_relu_po_kernel(tc, x_words, x_scales, w1, w2, w3, w4, w
             runs = slice(V // RUN // 2 * half, V // RUN // 2 * (half + 1))
             nc.scalar.activation(as_woven(woven["d2"])[:, runs], as_planes(planes["e2"])[:, runs], ACT.Abs)
             quantize(mx_of["d2"], edges, woven["d2"][:, edges].rearrange("p v t -> p (v t)"))
-            for t in range(PACK):
-                product("d2", t, edges, half == 1)
+            product("d2", half)
 
         y = sbuf([P, PACK, V], F32, "y")
         out_planes = out_0.rearrange("(p t) v -> p t v", t=PACK)
-        for t in (0, 2):
-            nc.vector.tensor_copy(out=y[:, t, :], in_=y_banks[t][:])
-            nc.scalar.copy(out=y[:, t + 1, :], in_=y_banks[t + 1][:])
-            nc.sync.dma_start(out=out_planes[:, t : t + 2, :], in_=y[:, t : t + 2, :])
         y_woven = sbuf([P, V, PACK], BF16, "woven_y")
-        half = V // RUN // 2
-        nc.scalar.copy(out=as_woven(y_woven)[:, WEAVE_VECTOR_RUNS:], in_=as_planes(y)[:, WEAVE_VECTOR_RUNS:])
-        nc.vector.tensor_copy(out=as_woven(y_woven)[:, 0:half], in_=as_planes(y)[:, 0:half])
-        nc.vector.tensor_copy(out=as_woven(y_woven)[:, half:WEAVE_VECTOR_RUNS], in_=as_planes(y)[:, half:WEAVE_VECTOR_RUNS])
+        runs = V // RUN
+        for half in range(V // P):
+            edges = slice(P * half, P * (half + 1))
+            first_copy = nc.vector.tensor_copy if half == 1 else nc.scalar.copy
+            first_copy(out=y[:, 0:2, edges], in_=y_banks[half, 0][:])
+            nc.scalar.copy(out=y[:, 2:4, edges], in_=y_banks[half, 1][:])
+            nc.sync.dma_start(out=out_planes[:, :, edges], in_=y[:, :, edges])
+        for half in range(V // P):
+            part = slice(runs // 2 * half, runs // 2 * (half + 1))
+            nc.vector.tensor_copy(out=as_woven(y_woven)[:, part], in_=as_planes(y)[:, part])
         y_codes, y_scales = mx_tiles(V, "y")
         for cols in (slice(0, V // 2), slice(V // 2, V)):
             quantize((y_codes, y_scales), cols, y_woven[:, cols].rearrange("p v t -> p (v t)"))

@@ -26,7 +26,8 @@ RUN = 4
 PASS0_VECTOR = 84
 PAIR0_VECTOR = 84
 PAIR1_VECTOR = 96
-LAST_VECTOR = 96
+LAST_VECTOR = 88
+WEAVE_VECTOR_RUNS = 46
 
 
 def tile_picked_ymeshcnn_relu_po_kernel(tc, x_words, x_scales, w1, w2, w3, w4, w5, w6, offs, own, ea, eb, ec, ed, out_0, out_1, out_2):
@@ -265,25 +266,23 @@ def tile_picked_ymeshcnn_relu_po_kernel(tc, x_words, x_scales, w1, w2, w3, w4, w
             mx_of[name] = mx_tiles(V, name)
             quantize(mx_of[name], slice(0, V), flat(woven[name]))
 
-        def product(name, half):
-            edges = slice(P * half, P * (half + 1))
-            for t in range(PACK):
-                if name == operands[0] and t % 2 == 0:
-                    y_banks[half, t // 2] = psum.tile([P, 2, P], F32, name="y_bank%d%d" % (half, t // 2), tag="bank%d" % (1 + 2 * half + t // 2))
-                codes, scales, cols = w_mx[name][t]
-                nc.tensor.matmul_mx(
-                    out=y_banks[half, t // 2][:, t % 2, :],
-                    lhsT=codes[:, cols].bitcast(FP8X4),
-                    lhsT_scale=scales[:, cols],
-                    rhs=mx_of[name][0][:, edges].bitcast(FP8X4),
-                    rhs_scale=mx_of[name][1][:, edges],
-                    start=(name == operands[0] and t % 2 == 0),
-                    stop=(name == operands[-1] and t % 2 == 1),
-                )
+        def product(name, t, edges=slice(0, V), stop=False):
+            if name == operands[0]:
+                y_banks[t] = psum.tile([P, V], F32, name="y_bank%d" % t, tag="bank%d" % (1 + t))
+            codes, scales, cols = w_mx[name][t]
+            nc.tensor.matmul_mx(
+                out=y_banks[t][:, edges],
+                lhsT=codes[:, cols].bitcast(FP8X4),
+                lhsT_scale=scales[:, cols],
+                rhs=mx_of[name][0][:, edges].bitcast(FP8X4),
+                rhs_scale=mx_of[name][1][:, edges],
+                start=(name == operands[0]),
+                stop=stop,
+            )
 
         def products(name):
-            for half in range(V // P):
-                product(name, half)
+            for t in range(PACK):
+                product(name, t)
 
         for name in ("hea", "heb"):
             planes[name] = sbuf([P, PACK, V], F32, name)
@@ -364,21 +363,20 @@ def tile_picked_ymeshcnn_relu_po_kernel(tc, x_words, x_scales, w1, w2, w3, w4, w
             runs = slice(V // RUN // 2 * half, V // RUN // 2 * (half + 1))
             nc.scalar.activation(as_woven(woven["d2"])[:, runs], as_planes(planes["e2"])[:, runs], ACT.Abs)
             quantize(mx_of["d2"], edges, woven["d2"][:, edges].rearrange("p v t -> p (v t)"))
-            product("d2", half)
+            for t in range(PACK):
+                product("d2", t, edges, half == 1)
 
         y = sbuf([P, PACK, V], F32, "y")
         out_planes = out_0.rearrange("(p t) v -> p t v", t=PACK)
+        for t in (0, 2):
+            nc.vector.tensor_copy(out=y[:, t, :], in_=y_banks[t][:])
+            nc.scalar.copy(out=y[:, t + 1, :], in_=y_banks[t + 1][:])
+            nc.sync.dma_start(out=out_planes[:, t : t + 2, :], in_=y[:, t : t + 2, :])
         y_woven = sbuf([P, V, PACK], BF16, "woven_y")
-        runs = V // RUN
-        for half in range(V // P):
-            edges = slice(P * half, P * (half + 1))
-            first_copy = nc.vector.tensor_copy if half == 1 else nc.scalar.copy
-            first_copy(out=y[:, 0:2, edges], in_=y_banks[half, 0][:])
-            nc.scalar.copy(out=y[:, 2:4, edges], in_=y_banks[half, 1][:])
-            nc.sync.dma_start(out=out_planes[:, :, edges], in_=y[:, :, edges])
-        for half in range(V // P):
-            part = slice(runs // 2 * half, runs // 2 * (half + 1))
-            nc.vector.tensor_copy(out=as_woven(y_woven)[:, part], in_=as_planes(y)[:, part])
+        half = V // RUN // 2
+        nc.scalar.copy(out=as_woven(y_woven)[:, WEAVE_VECTOR_RUNS:], in_=as_planes(y)[:, WEAVE_VECTOR_RUNS:])
+        nc.vector.tensor_copy(out=as_woven(y_woven)[:, 0:half], in_=as_planes(y)[:, 0:half])
+        nc.vector.tensor_copy(out=as_woven(y_woven)[:, half:WEAVE_VECTOR_RUNS], in_=as_planes(y)[:, half:WEAVE_VECTOR_RUNS])
         y_codes, y_scales = mx_tiles(V, "y")
         for cols in (slice(0, V // 2), slice(V // 2, V)):
             quantize((y_codes, y_scales), cols, y_woven[:, cols].rearrange("p v t -> p (v t)"))

from contextlib import ExitStack

import concourse.mybir as mybir
from concourse.masks import make_identity

K, T, S, H, N, V = 1024, 1024, 512, 512, 512, 256
FLOPS = 2 * K * H * S + 5 * 2 * H * N * V

F32 = mybir.dt.float32
BF16 = mybir.dt.bfloat16
I32 = mybir.dt.int32
U32 = mybir.dt.uint32
U16 = mybir.dt.uint16
U8 = mybir.dt.uint8
FP8X4 = mybir.dt.float8_e4m3fn_x4
ACT = mybir.ActivationFunctionType
ALU = mybir.AluOpType

P = 128
PACK = 4
K_PASS = P * PACK
QUADRANT = 32
BANKS = 8
RUN = 4

PASS0_VECTOR = 84
PAIR0_VECTOR = 84
PAIR1_VECTOR = 96
LAST_VECTOR = 88
WEAVE_VECTOR_RUNS = 46


def tile_picked_ymeshcnn_relu_po_kernel(tc, x_words, x_scales, w1, w2, w3, w4, w5, w6, offs, own, ea, eb, ec, ed, out_0, out_1, out_2):
    nc = tc.nc
    with ExitStack() as ctx:
        keep = ctx.enter_context(tc.tile_pool(name="keep", bufs=1))
        late = ctx.enter_context(tc.tile_pool(name="late", bufs=1))
        psum = ctx.enter_context(tc.psum_pool(name="psum", bufs=1))
        woven_bytes = 2 * V * PACK
        raw_bytes = 4 * PACK * N // 2
        places = {
            "hown": 0,
            "woven_d1": 0,
            "w_dealt_d1": raw_bytes,
            "s1_codes": raw_bytes,
            "s2_codes": 2 * raw_bytes + 12 * V,
            "w_d2_0_raw": 2 * raw_bytes,
            "d1_codes": 2 * raw_bytes,
            "woven_d2": 2 * raw_bytes + 4 * V,
        }

        def sbuf(shape, dtype, name, tag=None):
            if name in places:
                return late.tile(shape, dtype, name=name, align_bytes=64, offset=places[name])
            return keep.tile(shape, dtype, name=name, tag=tag or name, align_bytes=64)

        woven_words = V * PACK // 2
        raw_words = PACK * N
        own_at = 6112
        shared = sbuf([P, own_at + woven_words + raw_words], F32, "shared")
        plane_at = {"e1": (1008, 2 * V), "e2": (752, 4 * V)}
        inside = {"w_hown_1": 0, "w_s1": 1520, "w_s2": 4064, "w_d1": own_at + woven_words - 16}
        woven_in = {"hown": own_at}

        def load_list(ap, name):
            tile = keep.tile(list(ap.shape), U16, name=name)
            nc.sync.dma_start(tile[:], ap)
            return tile

        def load_words(o):
            tile = sbuf([P, T], I32, "x_words%d" % o)
            nc.sync.dma_start(out=tile[:], in_=x_words[o].rearrange("p n t -> p (n t)").bitcast(I32))
            return tile

        def load_weight(rows, name):
            if name in inside:
                raw = shared[:, inside[name] : inside[name] + PACK * rows.shape[1]].rearrange("p (j c) -> p j c", j=PACK)
            else:
                raw = sbuf([P, PACK, rows.shape[1]], F32, name + "_raw")
            nc.sync.dma_start(out=raw[:], in_=rows.rearrange("(p j) c -> p j c", j=PACK))
            return raw

        def deal(copy, dealt, raw, first, m0, m1, at=0):
            copy(
                out=dealt.rearrange("p t (m e) j -> p m j e t", e=2)[:, (at + m0) // 2 : (at + m1) // 2],
                in_=raw[:].rearrange("p j (m e t) -> p m j e t", e=2, t=PACK)[:, m0 // 2 : m1 // 2, :, :, first : first + 2],
            )

        def mx_tiles(width, name):
            return sbuf([P, width], U32, name + "_codes"), sbuf([P, width], U8, name + "_scales")

        def quantize(mx, cols, values):
            nc.vector.quantize_mx(out=mx[0][:, cols].bitcast(FP8X4), scales=mx[1][:, cols], in_=values)

        def plane_cols(t):
            return slice(P * t, P * (t + 1))

        def as_woven(tile, run=RUN):
            return tile[:].rearrange("p (c i) t -> p c t i", i=run)

        def as_planes(tile, run=RUN):
            return tile[:].rearrange("p t (c i) -> p c t i", i=run)

        def flat(tile):
            return tile[:].rearrange("p a b -> p (a b)")

        scales_in = sbuf([P, T], U8, "scales_in")
        nc.gpsimd.memset(scales_in[:].bitcast(I32), 0)
        words_in = [load_words(0)]
        lists = {"offs": load_list(offs, "offs")}
        for q in range(P // QUADRANT):
            nc.sync.dma_start(
                out=scales_in[QUADRANT * q : QUADRANT * q + 2 * PACK, :].bitcast(I32),
                in_=x_scales[:, PACK * q : PACK * (q + 1), :].bitcast(I32),
            )
        w1_raw = [load_weight(w1[0:K_PASS, :], "w1_pass0")]
        words_in.append(load_words(1))
        w1_raw.append(load_weight(w1[K_PASS:K, :], "w1_pass1"))
        first_raw = [load_weight(w2[:, 0 : N // 2], "w_hown_0")]
        for name, ap in (("ea", ea), ("eb", eb), ("ec", ec)):
            lists[name] = load_list(ap, name)
        first_raw.append(load_weight(w2[:, N // 2 : N], "w_hown_1"))
        for name, ap in (("ed", ed), ("own", own)):
            lists[name] = load_list(ap, name)
        operands = ("hown", "s1", "s2", "d1", "d2")
        w_raw = {}
        for name, w in (("s1", w3), ("s2", w5), ("d1", w4)):
            w_raw[name] = load_weight(w, "w_" + name)
        last_scalar = load_weight(w6[:, PACK * LAST_VECTOR : N], "w_d2_1")
        last_raw = [load_weight(w6[:, 0 : PACK * LAST_VECTOR], "w_d2_0"), last_scalar]

        pieces = [(0, slice(0, S // 2)), (0, slice(S // 2, S))] + [(t, slice(0, S)) for t in range(1, PACK)]
        h_banks = [psum.tile([P, edges.stop - edges.start], F32, name="h_bank%d" % i, tag="bank%d" % i) for i, (t, edges) in enumerate(pieces)]
        picked_words = [sbuf([P, S], U32, "picked_words0")]
        picked_scales = sbuf([P, S], U8, "picked_scales")

        def first_product(o, t, mx, cols):
            for bank, (plane, edges) in zip(h_banks, pieces):
                if plane == t:
                    nc.tensor.matmul_mx(
                        out=bank[:],
                        lhsT=mx[0][:, cols].bitcast(FP8X4),
                        lhsT_scale=mx[1][:, cols],
                        rhs=picked_words[o][:, edges].bitcast(FP8X4),
                        rhs_scale=picked_scales[PACK * o : P, edges],
                        start=(o == 0),
                        stop=(o == K // K_PASS - 1),
                    )

        nc.vector.tensor_copy(picked_words[0][:], words_in[0][:].bitcast(U32).indirect(lists["offs"][:]))
        nc.vector.tensor_copy(picked_scales[:], scales_in[:].indirect(lists["offs"][:]))
        w1_dealt0 = sbuf([P, PACK, P, PACK], BF16, "w1_dealt0")
        for first in (0, 2):
            deal(nc.vector.tensor_copy, w1_dealt0[:, first : first + 2], w1_raw[0], first, 0, PASS0_VECTOR)
            deal(nc.scalar.copy, w1_dealt0[:, first : first + 2], w1_raw[0], first, PASS0_VECTOR, P)
        for u in range(2):
            mx = mx_tiles(2 * P, "w1_0%d" % u)
            quantize(mx, slice(0, 2 * P), w1_dealt0[:, 2 * u : 2 * u + 2].rearrange("p t m j -> p (t m j)"))
            for e in range(2):
                first_product(0, 2 * u + e, mx, plane_cols(e))
        picked_words.append(sbuf([P, S], U32, "picked_words1", "w1_dealt0"))
        nc.vector.tensor_copy(picked_words[1][:], words_in[1][:].bitcast(U32).indirect(lists["offs"][:]))
        pairs = [sbuf([P, 2, P, PACK], BF16, "w1_pair%d" % u) for u in range(2)]

        def second_pass(t):
            mx = mx_tiles(P, "w1_1%d" % t)
            quantize(mx, slice(0, P), pairs[t // 2][:, t % 2].rearrange("p m j -> p (m j)"))
            first_product(1, t, mx, slice(0, P))

        deal(nc.vector.tensor_copy, pairs[0][:], w1_raw[1], 0, 0, PAIR0_VECTOR)
        deal(nc.scalar.copy, pairs[0][:], w1_raw[1], 0, PAIR0_VECTOR, P)
        second_pass(0)
        second_pass(1)
        deal(nc.vector.tensor_copy, pairs[1][:], w1_raw[1], 2, 0, PAIR1_VECTOR)
        deal(nc.scalar.copy, pairs[1][:], w1_raw[1], 2, PAIR1_VECTOR, P)

        dealt_shape = [P, PACK, P, PACK]
        w_dealt = {"hown": sbuf(dealt_shape, BF16, "w_dealt_hown")}

        def round_first(copy, half, first):
            deal(copy, w_dealt["hown"][:, first : first + 2], first_raw[half], first, 0, P // 2, P // 2 * half)

        h = [sbuf([P, S], F32, "h%d" % t) for t in range(PACK)]
        round_first(nc.vector.tensor_copy, 0, 0)
        round_first(nc.scalar.copy, 0, 2)
        nc.vector.tensor_scalar_max(h[0][:, 0 : S // 2], h_banks[0][:], 0.0)
        nc.scalar.activation(h[0][:, S // 2 : S], h_banks[1][:], ACT.Relu)
        second_pass(2)
        second_pass(3)

        planes = {}
        woven = {}
        w_mx = {}
        mx_of = {}
        y_banks = {}
        words = {}
        turned_banks = {}
        identity = sbuf([P, P], F32, "identity")
        make_identity(nc, identity[:])

        def pick(name, list_name, t):
            nc.scalar.activation(planes[name][:, t, :], h[t][:].indirect(lists[list_name][:]), ACT.Copy)

        def turn(name, term, t, start, stop):
            for half in range(V // P):
                nc.tensor.matmul(
                    turned_banks[name, half][:, t, :],
                    planes[term][:, t, P * half : P * (half + 1)],
                    identity[:],
                    start=start,
                    stop=stop,
                    is_transpose=True,
                )

        def pick_first(total, name, list_name, t):
            pick(name, list_name, t)
            turn(total, name, t, t == 0, False)
            turn(total, name, t, False, False)

        def pick_minus(total, name, list_name, first, t):
            nc.vector.tensor_tensor(planes[name][:, t, :], h[t][:].indirect(lists[list_name][:]), planes[first][:, t, :], ALU.subtract)
            turn(total, name, t, False, t == PACK - 1)

        def empty_h(t):
            nc.scalar.activation(h[t][:], h_banks[1 + t][:], ACT.Relu)

        def round_part(name, m0, m1):
            if name not in w_dealt:
                w_dealt[name] = sbuf(dealt_shape, BF16, "w_dealt_" + name)
            nc.vector.tensor_copy(
                out=w_dealt[name][:].rearrange("p t (m e) j -> p m j e t", e=2)[:, m0 // 2 : m1 // 2],
                in_=w_raw[name][:].rearrange("p j (m e t) -> p m j e t", e=2, t=PACK)[:, m0 // 2 : m1 // 2],
            )

        def round_half(name, half):
            round_part(name, P // 2 * half, P // 2 * (half + 1))

        def quantize_weight(name):
            mx = mx_tiles(N, "w_" + name)
            quantize(mx, slice(0, N), w_dealt[name][:].rearrange("p t m j -> p (t m j)"))
            w_mx[name] = [mx + (plane_cols(t),) for t in range(PACK)]

        def weave_abs(name, signed):
            woven[name] = woven_view(name)
            nc.scalar.activation(as_woven(woven[name]), as_planes(planes[signed]), ACT.Abs)

        def turn_back(name, half, turned):
            for u in range(2):
                nc.tensor.transpose(words[name][:, u, P * half : P * (half + 1)], turned[:, u].rearrange("v p e -> v (p e)").bitcast(F32), identity[:])

        def round_turned(name, half):
            turned = sbuf([P, 2, P, 2], BF16, "turned_%s%d" % (name, half))
            nc.scalar.activation(turned[:], turned_banks[name, half][:].rearrange("v (u e) p -> v u p e", e=2), ACT.Copy)
            turn_back(name, half, turned)

        def woven_view(name):
            if name in woven_in:
                return shared[:, woven_in[name] : woven_in[name] + woven_words].bitcast(BF16).rearrange("p (v t) -> p v t", t=PACK)
            return sbuf([P, V, PACK], BF16, "woven_" + name)

        def weave_words(name):
            woven[name] = woven_view(name)
            nc.scalar.copy(out=woven[name][:].bitcast(F32), in_=words[name][:].rearrange("p u v -> p v u"))

        def quantize_operand(name):
            mx_of[name] = mx_tiles(V, name)
            quantize(mx_of[name], slice(0, V), flat(woven[name]))

        def product(name, t, edges=slice(0, V), stop=False):
            if name == operands[0]:
                y_banks[t] = psum.tile([P, V], F32, name="y_bank%d" % t, tag="bank%d" % (1 + t))
            codes, scales, cols = w_mx[name][t]
            nc.tensor.matmul_mx(
                out=y_banks[t][:, edges],
                lhsT=codes[:, cols].bitcast(FP8X4),
                lhsT_scale=scales[:, cols],
                rhs=mx_of[name][0][:, edges].bitcast(FP8X4),
                rhs_scale=mx_of[name][1][:, edges],
                start=(name == operands[0]),
                stop=stop,
            )

        def products(name):
            for t in range(PACK):
                product(name, t)

        for name in ("hea", "heb"):
            planes[name] = sbuf([P, PACK, V], F32, name)
        for name, (at, step) in plane_at.items():
            planes[name] = shared[:, at : at + PACK * step].rearrange("p (t x) -> p t x", t=PACK)[:, :, 0:V]
        planes["hown"] = sbuf([P, PACK, V], BF16, "hown")
        for i, name in enumerate(("s1", "s2")):
            for half in range(V // P):
                turned_banks[name, half] = psum.tile([P, PACK, P], F32, name="turned_%s%d" % (name, half), tag="bank%d" % ((len(pieces) + 2 * i + half) % BANKS))

        def pick_firsts(t):
            if t > 0:
                empty_h(t)
            pick_first("s1", "hea", "ea", t)
            pick_first("s2", "heb", "eb", t)

        def minus1(t):
            pick_minus("s1", "e1", "ec", "hea", t)

        def minus2(t):
            pick_minus("s2", "e2", "ed", "heb", t)

        pick_firsts(0)
        nc.vector.tensor_copy(
            out=w_dealt["hown"][:].rearrange("p t (m e) j -> p m j e t", e=2)[:, P // 4 :],
            in_=first_raw[1][:].rearrange("p j (m e t) -> p m j e t", e=2, t=PACK),
        )
        quantize_weight("hown")
        minus1(0)
        minus2(0)
        round_half("s1", 0)
        round_half("s1", 1)
        pick_firsts(1)
        pick_firsts(2)
        minus1(1)
        minus2(1)
        quantize_weight("s1")
        pick_firsts(3)
        for t in range(PACK):
            pick("hown", "own", t)
        minus1(2)
        minus2(2)
        minus1(3)
        round_half("s2", 0)
        round_half("s2", 1)
        minus2(3)
        quantize_weight("s2")
        for i, name in enumerate(("s1", "s2")):
            words[name] = psum.tile([P, 2, V], F32, name="words_" + name, tag="bank%d" % (len(pieces) + i))
            for half in range(V // P):
                round_turned(name, half)
        weave_words("s1")
        weave_words("s2")
        round_half("d1", 0)
        round_half("d1", 1)
        woven["hown"] = woven_view("hown")
        nc.vector.tensor_copy(out=as_woven(woven["hown"]), in_=as_planes(planes["hown"]))
        weave_abs("d1", "e1")
        quantize_weight("d1")
        for name in ("hown", "s1"):
            quantize_operand(name)
            products(name)
        w_dealt["d2"] = sbuf(dealt_shape, BF16, "w_dealt_d2")
        for first in (0, 2):
            deal(nc.scalar.copy, w_dealt["d2"][:, first : first + 2], last_raw[1], first, 0, P - LAST_VECTOR, LAST_VECTOR)
        nc.vector.tensor_copy(
            out=w_dealt["d2"][:].rearrange("p t (m e) j -> p m j e t", e=2)[:, 0 : LAST_VECTOR // 2],
            in_=last_raw[0][:].rearrange("p j (m e t) -> p m j e t", e=2, t=PACK),
        )
        for name in ("s2", "d1"):
            quantize_operand(name)
            products(name)
        quantize_weight("d2")
        woven["d2"] = woven_view("d2")
        mx_of["d2"] = mx_tiles(V, "d2")
        for half in range(2):
            edges = slice(V // 2 * half, V // 2 * (half + 1))
            runs = slice(V // RUN // 2 * half, V // RUN // 2 * (half + 1))
            nc.scalar.activation(as_woven(woven["d2"])[:, runs], as_planes(planes["e2"])[:, runs], ACT.Abs)
            quantize(mx_of["d2"], edges, woven["d2"][:, edges].rearrange("p v t -> p (v t)"))
            for t in range(PACK):
                product("d2", t, edges, half == 1)

        y = sbuf([P, PACK, V], F32, "y")
        out_planes = out_0.rearrange("(p t) v -> p t v", t=PACK)
        for t in (0, 2):
            nc.vector.tensor_copy(out=y[:, t, :], in_=y_banks[t][:])
            nc.scalar.copy(out=y[:, t + 1, :], in_=y_banks[t + 1][:])
            nc.sync.dma_start(out=out_planes[:, t : t + 2, :], in_=y[:, t : t + 2, :])
        y_woven = sbuf([P, V, PACK], BF16, "woven_y")
        half = V // RUN // 2
        nc.scalar.copy(out=as_woven(y_woven)[:, WEAVE_VECTOR_RUNS:], in_=as_planes(y)[:, WEAVE_VECTOR_RUNS:])
        nc.vector.tensor_copy(out=as_woven(y_woven)[:, 0:half], in_=as_planes(y)[:, 0:half])
        nc.vector.tensor_copy(out=as_woven(y_woven)[:, half:WEAVE_VECTOR_RUNS], in_=as_planes(y)[:, half:WEAVE_VECTOR_RUNS])
        y_codes, y_scales = mx_tiles(V, "y")
        for cols in (slice(0, V // 2), slice(V // 2, V)):
            quantize((y_codes, y_scales), cols, y_woven[:, cols].rearrange("p v t -> p (v t)"))
        nc.sync.dma_start(out=out_1[0].rearrange("p v t -> p (v t)").bitcast(I32), in_=y_codes[:].bitcast(I32))
        for q in range(P // QUADRANT):
            queue = nc.scalar if q % 2 else nc.sync
            queue.dma_start(
                out=out_2[0, PACK * q : PACK * (q + 1), :].bitcast(I32),
                in_=y_scales[QUADRANT * q : QUADRANT * q + PACK, :].bitcast(I32),
            )
